import numpy as np, ml_dtypes
CORES = [9,25,41,57]
N = 4
import mx_ref
BF = ml_dtypes.bfloat16
def cut(t, i, w=512):
    return t[:, w * i:w * i + w]
def tile(rs):
    return np.stack(rs, axis=2).reshape(128, -1).astype(BF)
def pick(q, e):
    c = np.concatenate([q[0].reshape(128, -1, 4), np.zeros((128, 1, 4), np.uint8)], axis=1); s = np.concatenate([q[1], np.ones((16, 1), np.uint8)], axis=1)
    return (np.ascontiguousarray(c[:, e].reshape(128, -1)), np.ascontiguousarray(s[:, e]))
def join(*qs):
    return (np.concatenate([q[0] for q in qs], axis=1), np.concatenate([q[1] for q in qs], axis=1))
def put(q, e, v):
    c, s = q[0].reshape(128, -1, 4).copy(), q[1].copy(); c[:, e] = v[0].reshape(128, -1, 4); s[:, e] = v[1]
    return (c.reshape(128, -1), s)
def pk(c, s):
    return (np.ascontiguousarray(c), mx_ref.live(s))
def emit(q):
    return q[0], q[1]
def f(rng, *shape):
    return mx_ref.flush((rng.standard_normal(shape, dtype=np.float32) * np.exp2(rng.integers(-2, 3, shape[:-1] + (1,)))).astype(BF))
def wide(rng, *shape, cols=0):
    v = rng.standard_normal(shape, dtype=np.float32) * np.exp2(rng.integers(-12, 13, shape)).astype(np.float32)
    if cols: v *= np.repeat(np.exp2(rng.integers(-cols, cols + 1, shape[:-2] + (1, shape[-1] // 4))) * (rng.random(shape[:-2] + (1, shape[-1] // 4)) > 0.0625), 4, axis=-1).astype(np.float32)
    return mx_ref.flush(v.astype(BF))
P, S, R = 256, 40, 3
E = P + 2 * S * R
def randoms(rng):
    s = np.where(rng.random((N, P)) < rng.random((N, 1)), -1, 1)
    x = np.abs(f(rng, N, 128, 4 * P).astype(np.float32)) * np.repeat(s, 4, axis=1)[:, None, :].astype(np.float32)
    a = f(rng, N, 128, 512).astype(np.float32) + np.float32(0.05) * rng.standard_normal((N, 1, 1)).astype(np.float32)
    return {"x": mx_ref.flush(x.astype(BF)), "a": mx_ref.flush(a.astype(BF)), "w": f(rng, N, 128, 2048)}
def planted(rng, n, sign):
    up = np.stack([rng.permutation(128) < n[r] for r in range(N)])
    a = (1 + rng.random((N, 128, 512))) * np.exp2(rng.integers(-2, 3, (N, 128, 1))) * np.repeat(np.where(up, 1.0, -1.0), 4, axis=1)[:, None, :]
    x = np.abs(f(rng, N, 128, 4 * P).astype(np.float32)) * np.float32(sign)
    return {"x": x.astype(BF), "a": a.astype(np.float32).astype(BF), "w": f(rng, N, 128, 2048)}
def setup_inputs(rng):
    return randoms(rng)
def setup_inputs_shrink(rng):
    k = N // 2 - int(rng.integers(0, 2))
    n = rng.integers(0, 2, N)
    n[k] = rng.integers(112, 128)
    d = planted(rng, n, 1)
    d["x"][k, :, :4 * S * R] = 0
    d["x"][k, :, 4 * (P - S * R):] = 0
    return d
def setup_inputs_grow(rng):
    k, big = N // 2 - int(rng.integers(0, 2)), int(rng.integers(113, 129))
    less = big if N > 4 else 3 * big // 4
    n = np.full(N, less - 1)
    if k < N // 2: n[:k] = big - 1
    else: n[k + 1:] = big - 1
    n[k] = rng.integers(0, 4)
    return planted(rng, n, 1)
def setup_inputs_spread(rng):
    return {**randoms(rng), "x": wide(rng, N, 128, 4 * P, cols=6)}
def setup_inputs_part(rng):
    k, m = (N - 1) * int(rng.integers(0, 2)), 4 * int(rng.integers(0, 4)) + 2
    d = planted(rng, np.where(np.arange(N) == k, 1, 0), 1)
    on = np.zeros(P, bool)
    on[16 + rng.permutation(P - 32)[:m]] = True
    d["x"][k][:, np.repeat(~on, 4)] = 0
    return d
def setup_inputs_turn(rng):
    k = N // 2 - int(rng.integers(0, 2))
    n = np.full(N, int(rng.integers(112, 128)))
    n[k] = rng.integers(0, 4)
    return planted(rng, n, -1)
def check_inputs(d):
    b = []
    for k in ("x", "a", "w"):
        v = np.abs(d[k].astype(np.float32))
        if not (np.isfinite(v).all() and ((v == 0) | (v >= 2.0 ** -30) & (v <= 2.0 ** 30)).all()): b.append("a value of " + k)
    return b
def held(row, bo, r, m=4):
    e = np.arange(bo[r], bo[r + 1])
    return pick(row, np.concatenate([e, np.full(-e.size % m, -1)]))
def moved(bo, cost):
    before, new = np.concatenate([[0], np.cumsum(cost)]), bo.copy()
    for b in range(1, N):
        g = int(np.argmax(N * before >= b * before[-1]))
        new[b] = bo[b] + min(S, max(-S, g - int(bo[b])))
    return new
def reference(x, a, w):
    qa = [mx_ref.quantize(np.ascontiguousarray(a[r])) for r in range(N)]
    qw = [[mx_ref.quantize(np.ascontiguousarray(cut(w[r], b))) for b in range(4)] for r in range(N)]
    bo, out = P * np.arange(N + 1), []
    row = join(*[mx_ref.quantize(np.ascontiguousarray(x[r])) for r in range(N)])
    for t in range(R):
        cost = []
        for r in range(N):
            z = mx_ref.matmul(qa[r], held(row, bo, r))[:, :bo[r + 1] - bo[r]]
            cost.append(1 + np.sum(z > 0, axis=0).astype(np.int64))
        bo = moved(bo, np.concatenate(cost))
        new = []
        for r in range(N):
            h = held(row, bo, r)
            v = tile([np.maximum(mx_ref.matmul(qw[r][b], h), np.float32(0)) * np.float32(0.0625) for b in range(4)])
            new.append(pick(mx_ref.quantize(np.ascontiguousarray(v)), np.arange(bo[r + 1] - bo[r])))
        row = join(*new)
        out.append(bo)
    y, oc, osc = np.zeros((N, 128, E), np.float32), np.zeros((N, 128, 4 * E), np.uint8), np.zeros((N, 16, E), np.uint8)
    for r in range(N):
        n = int(bo[r + 1] - bo[r])
        y[r, :, :n] = mx_ref.matmul(qa[r], held(row, bo, r))[:, :n]
        oc[r], osc[r] = emit(held(row, bo, r, E))
    return {"y": y, "oc": oc, "osc": osc, "bd": np.stack([np.stack(out).astype(np.float32) for r in range(N)])}

@@ -1,0 +1,489 @@
+import numpy as np
+from concourse.bass import DstId, RemoteDMATransfer
+from concourse.mybir import dt, AluOpType as Op, AxisListType, ActivationFunctionType as Act
+
+F32, BF, I32, U16, F8, U8 = "float32", "bfloat16", "int32", "uint16", "float8_e4m3fn_x4", "uint8"
+SCRATCH = {"ps": ("psum", [128, 4096], F32)}
+for _names, _d in (("xt:1024 at:512 wt:2048 h1:1536 m2:2048 m3:1664 hh2:512 zt:512 junk:1408", BF),
+                   ("eps:4 kb:4 c130:256 nh:32 nha:32 nhb:32 MM:288 XX:96 lo:96 hi:4 BBB:96 row:16 rjunk:1536 B0:15 Bh:16 Ball:16 "
+                    "pf:31 j0:31 J:31 J2:31 J2m:31 JL:8 JR:8 Jm:16 J8:8 gi:4 wq:4 z16:16 WT:48 MW:48 LW:48 MK1:16 MK2:16 "
+                    "LM:48 PS:48 TW:16 t1:16 t2:16 kk:4 terms:192 sum3:64 sum1:32 yt:512 YC:544 L0:16 L1:16 L2:16 "
+                    "Zq0:128 Zq1:128 Zq2:128 Zh0:128 Zh1:160 Zh2:256 Ih0:132 Ih1:164 Ih2:244", F32),
+                   ("pi:31 pm:31", I32), ("la:16 lb:8 lf:32", U16)):
+    for _s in _names.split():
+        SCRATCH[_s.split(":")[0]] = ("sbuf", [128, int(_s.split(":")[1])], _d)
+for _n, _w in (("qa", 128), ("qw", 512), ("C0", 256), ("W1", 640), ("M1", 256), ("C2", 512), ("C3", 544), ("H2", 128),
+               ("N0", 352), ("N2", 352), ("F", 496)):
+    SCRATCH[_n] = ("sbuf", [128, _w], F8)
+    SCRATCH[_n + "s"] = ("sbuf", [128, _w], U8)
+SEMAPHORES = ["sv", "sa", "sp", "gc", "dx0", "dx1", "da", "dw", "dout", "ls"] + \
+    ["%s%d" % (n, t) for n in ("nc", "ns", "lm") for t in range(3)]
+HALF = (64, 80, 120)
+MOVE = (40, 80, 120)
+
+
+def rank_program(g, core, T, topo):
+    r = T.rank_of(core)
+    if r is None:
+        return
+    n = len(T.cores)
+    left, right = (r - 1 if r else None), (r + 1 if r < n - 1 else None)
+    vec, act, ten = g.vector, g.scalar, g.tensor
+    queue = {"v": vec, "a": act, "p": ten, "g": g, "s": g.sync}
+    cnt, seen = {}, {q: {} for q in queue}
+
+    def W(q, *toks):
+        need = {}
+        for s, c in toks:
+            need[s] = max(need.get(s, 0), c)
+        for s, c in need.items():
+            if seen[q].get(s, 0) < c:
+                queue[q].wait_ge(T.sem[s], c)
+                seen[q][s] = c
+
+    def inc(sem, ins, k=1):
+        ins.then_inc(T.sem[sem], k)
+        cnt[sem] = cnt.get(sem, 0) + k
+        return (sem, cnt[sem])
+
+    V = lambda ins: inc("sv", ins)
+    A = lambda ins: inc("sa", ins)
+    P = lambda ins: inc("sp", ins)
+    G = lambda ins: inc("gc", ins)
+    bank = lambda k, a, b: T.ps[:, 512 * k + a:512 * k + b]
+
+    def nbs(q):
+        return [p for p in (q - 1, q + 1) if 0 <= p < n]
+
+    def engs(q, p):
+        e = topo.engines(T.cores[q], T.cores[p])
+        k = len(e) // len(nbs(q))
+        i = nbs(q).index(p)
+        return e[k * i:k * i + k]
+
+    def did(p):
+        rid, pnc, _ = topo.addr(T.cores[p])
+        return DstId(rid=rid, pnc=pnc)
+
+    def send_ends(t, name, src, dst, w, to_left, to_right):
+        tr = []
+        for p in nbs(r):
+            a, c = to_left if p < r else to_right
+            if name == "nc":
+                s, d = T[src][:, a:a + w].bitcast(dt.uint8), T[dst][:, c:c + w].bitcast(dt.uint8)
+            else:
+                s, d = T[src + "s"][:, a:a + w], T[dst + "s"][:, c:c + w]
+            e = engs(r, p)
+            tr.append(RemoteDMATransfer(dst_ids=[did(p)], dma_engine_mask=sum(1 << i for i in e),
+                                        remote_sem=T.sem["%s%d" % (name, t)], src=s, dst=d))
+            cnt["ls"] = cnt.get("ls", 0) + len(e)
+        g.remote_dma_fused(tr, local_sem=T.sem.ls)
+
+    others = [p for p in range(n) if p != r]
+
+    def send_costs(t):
+        s = T["L%d" % t][:, 4 * r:4 * r + 4]
+        e = topo.engines(T.cores[r], T.cores[others[0]])
+        g.remote_dma_fused([RemoteDMATransfer(dst_ids=[did(p) for p in others], dma_engine_mask=sum(1 << i for i in e),
+                                              remote_sem=T.sem["lm%d" % t], srcs=[s], dsts=[s for p in others])],
+                           local_sem=T.sem.ls)
+        cnt["ls"] = cnt.get("ls", 0) + len(e)
+
+    n_in = sum(len(engs(p, r)) for p in nbs(r))
+    l_in = sum(len(topo.engines(T.cores[p], T.cores[r])) for p in others)
+
+    kx0 = inc("dx0", g.sync.dma_start(T.xt[:, 0:512], T.x[:, 0:512]), 16)
+    kx1 = inc("dx1", act.dma_start(T.xt[:, 512:1024], T.x[:, 512:1024]), 16)
+    ka = inc("da", g.sync.dma_start(T.at[:], T.a[:]), 16)
+    inc("dw", act.dma_start(T.wt[:, 1024:2048], T.w[:, 1024:2048]), 16)
+    kw = inc("dw", g.sync.dma_start(T.wt[:, 0:1024], T.w[:, 0:1024]), 16)
+
+    def zeros(name, *cols):
+        return [V(vec.quantize_mx(T[name][:, a:a + 128], T[name + "s"][:, a:a + 128], T.zt[:])) for a in cols]
+    pads = ([48] if left is None else []) + [224 if right is not None else 176]
+    vnh = V(vec.memset(T.nh[0:32, :], 80.0))
+    vz = V(vec.memset(T.zt[:], 0.0))
+    for t in range(3):
+        V(vec.memset(T["L%d" % t][:, 4 * r:4 * r + 4], 0.0))
+    veps = V(vec.memset(T.eps[:, 0:1], -(2.0 ** -120)))
+    for b in range(1, n):
+        k, c = 16 * (b - 1), 4 * (b - 1) + 2
+        V(vec.memset(T.WT[:, k:k + c], 1 - b / 4.0))
+        V(vec.memset(T.WT[:, k + c:k + 16], -b / 4.0))
+    W("v", vz)
+    vpad0 = zeros("N0", *pads)
+    G(g.iota(T.pi[:], [[0, 31]], 0, 1))
+    G(g.iota(T.j0[:], [[16, 31]], 0, 0, allow_small_or_imprecise_dtypes=True))
+    G(g.iota(T.B0[:], [[0, 3], [256, 5]], 0, 0, allow_small_or_imprecise_dtypes=True))
+    for k, b0 in enumerate((-160, -240, 16)):
+        G(g.iota(T.gi[:, k:k + 1], [[0, 1]], b0, 2, allow_small_or_imprecise_dtypes=True))
+    W("g", vnh)
+    gk = G(g.affine_select(T.nha[0:32, :], T.nh[0:32, :], [[0, 32]], Op.is_ge, 0.0, -1, 1))
+    W("g", gk)
+    gset = G(g.affine_select(T.nhb[0:32, :], T.nha[0:32, :], [[0, 32]], Op.is_ge, 0.0, n - 1, -1))
+
+    W("v", kx0)
+    V(vec.quantize_mx(T.C0[:, 0:128], T.C0s[:, 0:128], T.xt[:, 0:512]))
+    W("v", kx1)
+    vx = V(vec.quantize_mx(T.C0[:, 128:256], T.C0s[:, 128:256], T.xt[:, 512:1024]))
+    W("v", ka)
+    va = V(vec.quantize_mx(T.qa[:], T.qas[:], T.at[:]))
+    W("g", vx)
+    send_ends(0, "nc", "C0", "N0", 48, (0, 176), (208, 128))
+    send_ends(0, "ns", "C0", "N0", 48, (0, 176), (208, 128))
+
+    def cost_mm(k, name, a):
+        return P(ten.matmul_mx(bank(k, 0, 128), T[name][:, a:a + 128], T[name + "s"][:, a:a + 128], T.qa[:], T.qas[:], True, True))
+
+    junk = []
+
+    def count(t, piece, k, tok, a=0, b=128):
+        W("a", tok)
+        j = 128 * len(junk)
+        junk.append(j)
+        c = 4 * r + piece
+        return A(act.activation(T.junk[a:b, j:j + 128], T.ps[a:b, 512 * k:512 * k + 128], Act.Sign, bias=T.eps[a:b, 0:1],
+                                accum_out=T["L%d" % t][a:b, c:c + 1]))
+
+    W("p", va)
+    p0, p1 = cost_mm(4, "C0", 0), cost_mm(5, "C0", 128)
+    W("a", veps)
+    count(0, 0, 4, p0)
+    count(0, 1, 5, p1, 0, 64)
+    a1 = count(0, 2, 5, p1, 64, 128)
+    W("g", a1)
+    send_costs(0)
+
+    V(vec.memset(T.h1[:, 0:160], 0.0))
+    V(vec.memset(T.h1[:, 1504:1536], 0.0))
+    vmm = V(vec.memset(T.MM[:], 0.0))
+    V(vec.memset(T.XX[0:32, :], 0.0))
+    W("v", kw)
+    vw = V(vec.quantize_mx(T.qw[:], T.qws[:], T.wt[:]))
+
+    def w_mm(k, b, name, a, m):
+        return P(ten.matmul_mx(bank(k, 0, m), T.qw[:, 128 * b:128 * b + 128], T.qws[:, 128 * b:128 * b + 128],
+                               T[name][:, a:a + m], T[name + "s"][:, a:a + m], True, True))
+
+    def relu(q, out, src):
+        if q == "a":
+            return A(act.activation(out, src, Act.Relu, scale=0.0625))
+        return V(vec.tensor_scalar(out, src, 0.0, 0.0625, Op.max, Op.mult))
+
+    def relus(q, bs, pm, k0, h, *runs):
+        out = []
+        for b in bs:
+            W(q, pm[b])
+            for a, c, m in runs:
+                out.append(relu(q, h[:, 4 * c + b:4 * (c + m):4], bank(k0 + b, a, a + m)))
+        return out
+
+    W("p", vx, vw)
+    pm = [w_mm(b, b, "C0", 0, 256) for b in range(4)]
+    V(vec.memset(T.z16[:], 0.0))
+    for b in range(1, n):
+        V(vec.memset(T.wq[:, b - 1:b], b / 4.0))
+    V(vec.memset(T.c130[0:32, :], 130.0))
+    rl = relus("a", (0, 2), pm, 0, T.h1, (0, 80, 256)) + relus("v", (1, 3), pm, 0, T.h1, (0, 80, 256))
+    W("v", *rl)
+    vq1 = V(vec.quantize_mx(T.W1[:, 128:256], T.W1s[:, 128:256], T.h1[:, 512:1024]))
+    for t in range(3):
+        V(vec.memset(T.kb[0:32, t:t + 1], 130.0 * HALF[t] - 0.125))
+    W("p", *vpad0, a1, ("nc0", n_in), ("ns0", n_in))
+    ph0 = [w_mm(4 + b, b, "N0", 128, 128) for b in range(4)]
+    W("p", vq1, *rl)
+    pc1 = cost_mm(0, "W1", 128)
+
+    BO = lambda t, a, b: T.BBB[:, 32 * t + a:32 * t + b]
+
+    def b_mask(t, *toks):
+        W("v", ("lm%d" % t, l_in), *toks)
+        return V(vec.tensor_tensor(T.LM[:, 16 * t:16 * t + 16], T["L%d" % t][:], T["MK%d" % t][:], Op.mult))
+
+    def b_ps(t, *toks):
+        W("v", *toks)
+        src = T.LM[:, 16 * t:16 * t + 16] if t else T.L0[:]
+        return V(vec.tensor_tensor_scan(T.PS[:, 16 * t:16 * t + 16], src, T.z16[:], 0.0, Op.add, Op.add))
+
+    def b_x(t):
+        m, mo = 16 * t, 96 * t
+        v = V(vec.tensor_tensor(T.MM[:, mo + 33:mo + 36], T.LM[:, m + 2:m + 11:4], T.LM[:, m + 4:m + 13:4], Op.add))
+        if t == 1:
+            return V(vec.tensor_copy(T.MM[0:32, mo + 65:mo + 68], T.L1[0:32, 5:14:4]))
+        return V(vec.tensor_tensor(T.MM[:, mo + 65:mo + 68], T.LM[:, m + 3:m + 12:4], T.LM[:, m + 5:m + 14:4], Op.add))
+
+    def b_share(t, v):
+        W("v", v)
+        return V(vec.tensor_scalar(T.TW[:, 4 * t:4 * t + 3], T.wq[:, 0:3], T.PS[:, 16 * t + 15:16 * t + 16], None, Op.mult))
+
+    def b_sub(t, v):
+        W("v", v)
+        return V(vec.tensor_tensor(T.MM[:, 96 * t + 1:96 * t + 4], T.PS[:, 16 * t + 1:16 * t + 10:4], T.TW[:, 4 * t:4 * t + 3],
+                                   Op.subtract))
+
+    def b_tq(t, vq):
+        mo = 96 * t
+        W("v", vq)
+        for k in range(4):
+            v = V(vec.transpose(T["Zq%d" % t][0:32, 32 * k:32 * k + 32], T.MM[32 * k:32 * k + 32, mo:mo + 32]))
+        return v
+
+    def b_qsum(t, v):
+        W("a", v)
+        return A(act.activation(T.rjunk[0:5, 512 * t:512 * t + 128], T["Zq%d" % t][0:5, :], Act.Copy,
+                                accum_out=T["Ih%d" % t][0:5, 0:1]))
+
+    def b_tx(t, vxx, half):
+        mo, Zh = 96 * t + 32, T["Zh%d" % t]
+        W("v", vxx)
+        if half == 0:
+            for k in range(4):
+                z = k if t else (k + 2) % 4
+                v = V(vec.transpose(Zh[0:32, 32 * z:32 * z + 32], T.MM[32 * k:32 * k + 32, mo:mo + 32]))
+        else:
+            for k in range((0, 1, 4)[t]):
+                v = V(vec.transpose(Zh[0:32, 128 + 32 * k:160 + 32 * k], T.MM[32 * k:32 * k + 32, mo + 32:mo + 64]))
+        return v
+
+    def b_scan(t, v, aq):
+        h = 2 * HALF[t]
+        Ih = T["Ih%d" % t]
+        W("v", v, aq)
+        return V(vec.tensor_tensor_scan(Ih[0:5, 1:1 + h], T["Zh%d" % t][0:5, 0:h], T.c130[0:5, 0:h], Ih[0:5, 0:1], Op.add, Op.add))
+
+    def b_sign(t, v):
+        a, w = HALF[t] - MOVE[t], 2 * MOVE[t]
+        W("a", v)
+        return A(act.activation(T.rjunk[0:5, 512 * t + 128:512 * t + 128 + w], T["Ih%d" % t][0:5, a:a + w], Act.Sign,
+                                bias=T.kb[0:5, t:t + 1], scale=-1.0, accum_out=T.row[0:5, t:t + 1]))
+
+    def b_clamp(t, av):
+        W("v", av)
+        v = V(vec.tensor_scalar(T.XX[0:5, 32 * t:32 * t + 32], T.lo[0:5, 32 * t:32 * t + 32], T.row[0:5, t:t + 1],
+                                T.hi[0:5, t:t + 1], Op.max, Op.min))
+        W("v", v)
+        for k in range(4):
+            v = V(vec.transpose(T.BBB[32 * k:32 * k + 32, 32 * t:32 * t + 32], T.XX[0:32, 32 * t:32 * t + 32]))
+        return v
+
+    def b_range(t):
+        V(vec.tensor_tensor(T.lo[0:5, 32 * t + 32:32 * t + 64], T.XX[0:5, 32 * t:32 * t + 32], T.nhb[0:5, :], Op.subtract))
+        V(vec.tensor_tensor(T.hi[0:5, t + 1:t + 2], T.XX[0:5, 32 * t:32 * t + 1], T.nhb[0:5, 0:1], Op.add))
+
+    def masks(t, cols):
+        MK = T["MK%d" % t]
+        for p, gc, is_left in cols:
+            if is_left:
+                v = V(vec.tensor_scalar(MK[:, p:16:4], BO(t - 1, 0, 4), T.gi[:, gc:gc + 1], None, Op.is_le))
+            else:
+                v = V(vec.tensor_scalar(MK[:, p:16:4], BO(t - 1, 1, 5), T.gi[:, gc:gc + 1], None, Op.is_gt))
+        return v
+
+    lm0 = ("lm0", l_in)
+    W("a", lm0, vmm, a1)
+    A(act.activation(T.MM[64:128, 33:36], T.L0[64:128, 2:11:4], Act.Copy))
+    ax = A(act.activation(T.MM[0:64, 33:36], T.L0[0:64, 4:13:4], Act.Copy))
+    halo = ((8, 40, 40), (48, 336, 40))
+    hr = relus("a", (0, 2), ph0, 4, T.h1, *halo)
+    vps = b_ps(0, lm0, a1)
+    hr += relus("v", (1,), ph0, 4, T.h1, *halo)
+    vsh = b_share(0, vps)
+    hr += relus("v", (3,), ph0, 4, T.h1, *halo)
+    W("v", *hr, *rl)
+    vp0 = V(vec.quantize_mx(T.W1[:, 0:128], T.W1s[:, 0:128], T.h1[:, 0:512]))
+    vp2 = V(vec.quantize_mx(T.W1[:, 256:384], T.W1s[:, 256:384], T.h1[:, 1024:1536]))
+    vq = b_sub(0, vsh)
+    vt2 = b_tx(0, ax, 0)
+    vt = b_tq(0, vq)
+    W("p", vp0)
+    pc0 = cost_mm(1, "W1", 0)
+    W("p", vp2)
+    pc2 = cost_mm(2, "W1", 256)
+    ac1 = count(1, 1, 0, pc1)
+    ac0 = count(1, 0, 1, pc0)
+    ac2 = count(1, 2, 2, pc2)
+    aq = b_qsum(0, vt)
+    W("g", vp2)
+    send_ends(1, "nc", "W1", "W1", 120, (40, 512), (256, 384))
+    send_ends(1, "ns", "W1", "W1", 120, (40, 512), (256, 384))
+    W("g", ac0, ac1, ac2)
+    send_costs(1)
+    W("v", gset)
+    vj = V(vec.tensor_scalar(T.pm[:], T.pi[:], 15, None, Op.bitwise_and))
+    V(vec.tensor_scalar(T.lo[0:32, 0:32], T.nhb[0:32, :], -1.0, None, Op.mult))
+    V(vec.tensor_copy(T.hi[0:32, 0:1], T.nhb[0:32, 0:1]))
+    W("v", vj)
+    vj = V(vec.tensor_copy(T.pf[:], T.pm[:]))
+    V(vec.memset(T.MK1[:], 1.0))
+    vs = b_scan(0, vt2, aq)
+    av = b_sign(0, vs)
+    W("v", vj)
+    vj = V(vec.tensor_tensor(T.J[:], T.j0[:], T.pf[:], Op.add))
+    V(vec.memset(T.m2[:, 0:160], 0.0))
+    W("v", vj)
+    V(vec.tensor_scalar(T.JL[:], T.J[:, 0:8], 2.0, -160.0, Op.mult, Op.add))
+    V(vec.tensor_scalar(T.JR[:], T.J[:, 0:8], 2.0, -96.0, Op.mult, Op.add))
+    V(vec.tensor_copy(T.Jm[:, 0:8], T.J[:, 0:8]))
+    vj = V(vec.tensor_scalar(T.Jm[:, 8:16], T.J[:, 0:8], 288.0, None, Op.add))
+    W("p", *rl, ac0, ac1, ac2)
+    pm = [w_mm(b, b, "W1", 128, 160) for b in range(4)]
+    vB = b_clamp(0, av)
+    W("v", vB, vj)
+    V(vec.tensor_scalar(T.t1[:, 0:8], T.JL[:], BO(0, r, r + 1), 384.0, Op.is_lt, Op.mult))
+    vl = V(vec.tensor_scalar(T.t1[:, 8:16], T.JR[:], BO(0, r + 1, r + 2), 216.0, Op.is_ge, Op.mult))
+    mk1 = masks(1, ((0, 0, True), (2, 0, False)))
+    W("v", vl)
+    vl = V(vec.tensor_tensor(T.t2[:], T.t1[:], T.Jm[:], Op.add))
+    b_range(0)
+    W("v", vl)
+    vl = V(vec.tensor_copy(T.la[:], T.t2[:]))
+    rm = relus("a", (0, 2), pm, 0, T.m2, (0, 168, 160)) + relus("v", (1, 3), pm, 0, T.m2, (0, 168, 160))
+    vpad1 = zeros("W1", *(([384] if left is None else []) + ([512] if right is None else [])))
+    V(vec.memset(T.m2[:, 1824:2048], 0.0))
+    V(vec.tensor_scalar(T.J8[:, 0:4], T.J[:, 0:4], 2.0, 240.0, Op.mult, Op.add))
+    vj = V(vec.tensor_scalar(T.J8[:, 4:8], T.J[:, 0:4], 2.0, 624.0, Op.mult, Op.add))
+
+    vpk, apk = [], []
+    W("v", vl, vp2, vq1, *vpad1, ("nc1", n_in))
+    W("a", vl, vp2, vq1, *vpad1, ("ns1", n_in))
+    for k in (0, 1):
+        s = slice(128 * k, 128 * k + 128)
+        l = T.la[:, 8 * k:8 * k + 8]
+        vpk.append(V(vec.tensor_copy(T.M1[:, s].bitcast(dt.uint32), T.W1[:, 0:640].bitcast(dt.uint32).indirect(l))))
+        apk.append(A(act.activation(T.M1s[:, s], T.W1s[:, 0:640].indirect(l), Act.Copy)))
+    W("p", vpk[0], apk[0], *hr)
+    pL = [w_mm(4 + b, b, "M1", 0, 128) for b in range(4)]
+    W("p", vpk[1], apk[1], *rm)
+    pR = [w_mm(b, b, "M1", 128, 128) for b in range(4)]
+    vpad2 = zeros("N2", *pads)
+    vm = b_mask(1, mk1, ac0, ac1, ac2)
+    rL = relus("a", (0, 2), pL, 4, T.m2, (0, 40, 128)) + relus("v", (1,), pL, 4, T.m2, (0, 40, 128))
+    vps = b_ps(1, vm)
+    vxx = b_x(1)
+    rL += relus("v", (3,), pL, 4, T.m2, (0, 40, 128))
+    vsh = b_share(1, vps)
+    W("v", *rL, *rm)
+    vc0 = V(vec.quantize_mx(T.C2[:, 0:256], T.C2s[:, 0:256], T.m2[:, 0:1024]))
+    vq = b_sub(1, vsh)
+    rR = relus("v", (1,), pR, 0, T.m2, (0, 328, 128))
+    vt = b_tq(1, vq)
+    rR += relus("a", (0, 2), pR, 0, T.m2, (0, 328, 128)) + relus("v", (3,), pR, 0, T.m2, (0, 328, 128))
+    aq = b_qsum(1, vt)
+    W("v", *rR)
+    vc1 = V(vec.quantize_mx(T.C2[:, 256:512], T.C2s[:, 256:512], T.m2[:, 1024:2048]))
+    b_tx(1, vxx, 0)
+    vt2 = b_tx(1, vxx, 1)
+    vs = b_scan(1, vt2, aq)
+    W("p", vc0, *rL)
+    pc = [cost_mm(4, "C2", 0), cost_mm(5, "C2", 128)]
+    W("p", vc1)
+    pc += [cost_mm(6, "C2", 256), cost_mm(7, "C2", 384)]
+    ac = [count(2, k, 4 + k, pc[k]) for k in range(4)]
+    av = b_sign(1, vs)
+    W("g", *ac)
+    send_costs(2)
+    W("p", *rR)
+    pm = [w_mm(b, b, "C2", 40, 416) for b in range(4)]
+    ro = relus("a", (0,), pm, 0, T.m3, (0, 0, 416))
+    V(vec.tensor_scalar(T.J2[:], T.J[:], 2.0, None, Op.mult))
+    V(vec.tensor_scalar(T.J2m[:], T.J[:], 2.0, -512.0, Op.mult, Op.add))
+    vhz = V(vec.memset(T.hh2[:, 320:512], 0.0))
+    vB = b_clamp(1, av)
+    W("v", vB, vj)
+    V(vec.tensor_scalar(T.lb[:, 0:4], T.J8[:, 0:4], BO(1, r, r + 1), 0.5, Op.add, Op.mult))
+    vl = V(vec.tensor_scalar(T.lb[:, 4:8], T.J8[:, 4:8], BO(1, r + 1, r + 2), 0.5, Op.add, Op.mult))
+    mk2 = masks(2, ((0, 1, True), (1, 2, True), (2, 1, False), (3, 2, False)))
+    W("v", vl)
+    vh = V(vec.tensor_copy(T.H2[:].bitcast(dt.uint32), T.C2[:, 0:512].bitcast(dt.uint32).indirect(T.lb[:, 0:8])))
+    W("v", mk2)
+    for b in range(n - 1):
+        vw = V(vec.tensor_tensor(T.MW[:, 16 * b:16 * b + 16], T.MK2[:], T.WT[:, 16 * b:16 * b + 16], Op.mult))
+    W("a", vl, vc1)
+    ah = A(act.activation(T.H2s[:], T.C2s[:, 0:512].indirect(T.lb[:, 0:8]), Act.Copy))
+    W("g", vh)
+    send_ends(2, "nc", "H2", "N2", 48, (0, 176), (80, 128))
+    W("g", ah)
+    send_ends(2, "ns", "H2", "N2", 48, (0, 176), (80, 128))
+    ro += relus("a", (1, 2, 3), pm, 0, T.m3, (0, 0, 416))
+
+    W("v", ("lm2", l_in), vw, *ac)
+    for b in range(n - 1):
+        vw = V(vec.tensor_tensor(T.LW[:, 16 * b:16 * b + 16], T.L2[:], T.MW[:, 16 * b:16 * b + 16], Op.mult))
+    vm = b_mask(2)
+    W("v", vw)
+    for b in range(n - 1):
+        vq = V(vec.tensor_reduce(T.MM[:, 193 + b:194 + b], T.LW[:, 16 * b:16 * b + 16], AxisListType.X, Op.add))
+    W("v", vm)
+    vxx = b_x(2)
+    vt = b_tq(2, vq)
+    b_tx(2, vxx, 0)
+    vt2 = b_tx(2, vxx, 1)
+    b_range(1)
+    aq = b_qsum(2, vt)
+    vs = b_scan(2, vt2, aq)
+    av = b_sign(2, vs)
+    V(vec.tensor_scalar(T.kk[:, 0:1], BO(1, r, r + 1), -0.5, 376.0, Op.mult, Op.add))
+    vk = V(vec.tensor_scalar(T.kk[:, 1:2], BO(1, r + 1, r + 2), -0.5, 120.0, Op.mult, Op.add))
+    W("p", *vpad2, *ac, ("nc2", n_in), ("ns2", n_in))
+    ph = [w_mm(4 + b, b, "N2", 128, 128) for b in range(4)]
+    W("v", *ro)
+    vc3 = V(vec.quantize_mx(T.C3[:, 0:416], T.C3s[:, 0:416], T.m3[:]))
+    h2 = relus("a", (0, 2), ph, 4, T.hh2, (8, 0, 80))
+    vB = b_clamp(2, av)
+    h2 += relus("v", (1, 3), ph, 4, T.hh2, (8, 0, 80))
+    W("a", vB)
+    for t in range(3):
+        ab = A(act.activation(T.Bh[:, 5 * t:5 * t + 5], BO(t, 0, 5), Act.Copy, scale=0.5))
+    W("v", vB, vk)
+    U2, V2, U = T.terms[:, 0:31], T.terms[:, 31:62], T.terms[:, 62:93]
+    V(vec.tensor_scalar(U2, T.J2[:], BO(2, r, r + 1), None, Op.add))
+    V(vec.tensor_scalar(V2, T.J2m[:], BO(2, r, r + 1), None, Op.add))
+    vu = V(vec.tensor_scalar(U, T.J2[:], BO(2, r, r + 1), 0.5, Op.add, Op.mult))
+    W("v", vhz, *h2)
+    vch = V(vec.quantize_mx(T.C3[:, 416:544], T.C3s[:, 416:544], T.hh2[:]))
+    W("v", vu)
+    V(vec.tensor_scalar(T.terms[:, 93:124], U2, BO(1, r, r + 1), T.kk[:, 0:1], Op.is_lt, Op.mult))
+    V(vec.tensor_scalar(T.terms[:, 124:155], V2, BO(1, r + 1, r + 2), T.kk[:, 1:2], Op.is_ge, Op.mult))
+    vu = V(vec.tensor_scalar(T.terms[:, 155:186], V2, BO(2, r + 1, r + 2), 2000.0, Op.is_ge, Op.mult))
+    W("v", vu)
+    vu = V(vec.tensor_tensor(T.sum3[:, 0:62], T.terms[:, 62:124], T.terms[:, 124:186], Op.add))
+    W("v", vu)
+    vu = V(vec.tensor_tensor(T.sum1[:, 0:31], T.sum3[:, 0:31], T.sum3[:, 31:62], Op.add))
+    W("v", vu)
+    vl = V(vec.tensor_scalar(T.lf[:, 0:31], T.sum1[:, 0:31], 80.0, 500.0, Op.add, Op.min))
+    W("v", ab)
+    vN = V(vec.tensor_tensor(T.Ball[:, 0:15], T.Bh[:, 0:15], T.B0[:], Op.add))
+    W("p", vc3, *ro)
+    py = P(ten.matmul_mx(bank(0, 0, 416), T.qa[:], T.qas[:], T.C3[:, 0:416], T.C3s[:, 0:416], True, True))
+    W("p", vch)
+    pz = P(ten.matmul_mx(bank(1, 0, 128), T.qa[:], T.qas[:], T.C3[:, 416:544], T.C3s[:, 416:544], True, True))
+    W("a", py)
+    A(act.activation(T.YC[:, 0:416], bank(0, 0, 416), Act.Copy))
+    W("a", pz)
+    yc = A(act.activation(T.YC[:, 416:544], bank(1, 0, 128), Act.Copy))
+
+    W("v", vl, vch, vc3)
+    W("a", vl, vch, vc3)
+    halves = ((0, 256), (256, 496))
+    vf, af = [], []
+    for a, b in halves:
+        l = T.lf[:, a // 16:b // 16]
+        vf.append(V(vec.tensor_copy(T.F[:, a:b].bitcast(dt.uint32), T.C3[:, 0:544].bitcast(dt.uint32).indirect(l))))
+        af.append(A(act.activation(T.Fs[:, a:b], T.C3s[:, 0:544].indirect(l), Act.Copy)))
+    W("v", yc)
+    W("a", yc)
+    vy = V(vec.tensor_copy(T.yt[:, 0:256], T.YC[:, 0:544].indirect(T.lf[:, 0:16])))
+    ay = A(act.activation(T.yt[:, 256:496], T.YC[:, 0:544].indirect(T.lf[:, 16:31]), Act.Copy))
+    W("s", vN)
+    inc("dout", g.sync.dma_start(T.bd[:], T.Ball[0:1, 0:15]), 16)
+    for k, (a, b) in enumerate(halves):
+        W("s", vf[k])
+        inc("dout", g.sync.dma_start(T.oc[:, 4 * a:4 * b], T.F[:, a:b].bitcast(dt.uint8)), 16)
+    W("s", af[1])
+    for i in range(4):
+        inc("dout", g.sync.dma_start(T.osc[4 * i:4 * i + 4, :], T.Fs[32 * i:32 * i + 4, :]), 16)
+    W("s", vy)
+    inc("dout", g.sync.dma_start(T.y[:, 0:256], T.yt[:, 0:256]), 16)
+    W("a", ay)
+    inc("dout", act.dma_start(T.y[:, 256:496], T.yt[:, 256:496]), 16)
+    W("g", *[(s, c) for s, c in cnt.items()])

@@ -5,21 +5,22 @@ from concourse.mybir import dt, AluOpType as Op, AxisListType, ActivationFunctio
 F32, BF, I32, U16, F8, U8 = "float32", "bfloat16", "int32", "uint16", "float8_e4m3fn_x4", "uint8"
 SCRATCH = {"ps": ("psum", [128, 4096], F32)}
 for _names, _d in (("xt:1024 at:512 wt:2048 h1:1536 m2:2048 m3:1664 hh2:512 zt:512 junk:1408", BF),
-                   ("eps:4 kb:4 c130:256 nh:32 nha:32 nhb:32 MM:288 XX:96 lo:96 hi:4 BBB:96 row:16 rjunk:1536 B0:15 Bh:16 Ball:16 "
-                    "pf:31 j0:31 J:31 J2:31 J2m:31 JL:8 JR:8 Jm:16 J8:8 gi:4 wq:4 z16:16 WT:48 MW:48 LW:48 MK1:16 MK2:16 "
+                   ("eps:4 kb:4 c130:384 nh:32 nha:32 nhb:32 MM:288 XX:96 lo:96 hi:4 BBB:96 row:16 rjunk:1536 B0:4 Bh:32 Ball:32 "
+                    "pf:31 j0:31 J:31 J2:31 J2m:31 J2n:62 JL:8 JR:8 Jm:16 J8:8 gi:4 wq:4 z16:16 MK1:16 MK2:16 "
                     "LM:48 PS:48 TW:16 t1:16 t2:16 kk:4 terms:192 sum3:64 sum1:32 yt:512 YC:544 L0:16 L1:16 L2:16 "
-                    "Zq0:128 Zq1:128 Zq2:128 Zh0:128 Zh1:160 Zh2:256 Ih0:132 Ih1:164 Ih2:244", F32),
+                    "Zh0:256 Zh1:288 Zh2:384 Ih0:256 Ih1:288 Ih2:384", F32),
                    ("pi:31 pm:31", I32), ("la:16 lb:8 lf:32", U16)):
     for _s in _names.split():
         SCRATCH[_s.split(":")[0]] = ("sbuf", [128, int(_s.split(":")[1])], _d)
-for _n, _w in (("qa", 128), ("qw", 512), ("C0", 256), ("W1", 640), ("M1", 256), ("C2", 512), ("C3", 544), ("H2", 128),
-               ("N0", 352), ("N2", 352), ("F", 496)):
+for _n, _w in (("qa", 128), ("qw", 512), ("C0", 256), ("W1", 640), ("M1", 256), ("C2", 512), ("C3", 544),
+               ("H2", 128), ("N0", 352), ("N2", 352), ("F", 496)):
     SCRATCH[_n] = ("sbuf", [128, _w], F8)
     SCRATCH[_n + "s"] = ("sbuf", [128, _w], U8)
 SEMAPHORES = ["sv", "sa", "sp", "gc", "dx0", "dx1", "da", "dw", "dout", "ls"] + \
     ["%s%d" % (n, t) for n in ("nc", "ns", "lm") for t in range(3)]
 HALF = (64, 80, 120)
 MOVE = (40, 80, 120)
+SC = 2048.0
 
 
 def rank_program(g, core, T, topo):
@@ -100,21 +101,20 @@ def rank_program(g, core, T, topo):
 
     def zeros(name, *cols):
         return [V(vec.quantize_mx(T[name][:, a:a + 128], T[name + "s"][:, a:a + 128], T.zt[:])) for a in cols]
+    pads0 = ([48] if right is None else []) + [224 if left is not None else 176]
     pads = ([48] if left is None else []) + [224 if right is not None else 176]
+    kb = lambda t: V(vec.memset(T.kb[0:32, t:t + 1], 130.0 * HALF[t] - 0.125))
     vnh = V(vec.memset(T.nh[0:32, :], 80.0))
     vz = V(vec.memset(T.zt[:], 0.0))
     for t in range(3):
         V(vec.memset(T["L%d" % t][:, 4 * r:4 * r + 4], 0.0))
     veps = V(vec.memset(T.eps[:, 0:1], -(2.0 ** -120)))
-    for b in range(1, n):
-        k, c = 16 * (b - 1), 4 * (b - 1) + 2
-        V(vec.memset(T.WT[:, k:k + c], 1 - b / 4.0))
-        V(vec.memset(T.WT[:, k + c:k + 16], -b / 4.0))
     W("v", vz)
-    vpad0 = zeros("N0", *pads)
+    vpad0 = zeros("N0", *pads0)
+    vpc = zeros("C2", 0, 384)
     G(g.iota(T.pi[:], [[0, 31]], 0, 1))
-    G(g.iota(T.j0[:], [[16, 31]], 0, 0, allow_small_or_imprecise_dtypes=True))
-    G(g.iota(T.B0[:], [[0, 3], [256, 5]], 0, 0, allow_small_or_imprecise_dtypes=True))
+    gj = G(g.iota(T.j0[:], [[16, 31]], 0, 0, allow_small_or_imprecise_dtypes=True))
+    G(g.iota(T.B0[:, 0:1], [[0, 1]], 0, 256, allow_small_or_imprecise_dtypes=True))
     for k, b0 in enumerate((-160, -240, 16)):
         G(g.iota(T.gi[:, k:k + 1], [[0, 1]], b0, 2, allow_small_or_imprecise_dtypes=True))
     W("g", vnh)
@@ -126,11 +126,13 @@ def rank_program(g, core, T, topo):
     V(vec.quantize_mx(T.C0[:, 0:128], T.C0s[:, 0:128], T.xt[:, 0:512]))
     W("v", kx1)
     vx = V(vec.quantize_mx(T.C0[:, 128:256], T.C0s[:, 128:256], T.xt[:, 512:1024]))
+    W("v", gj)
+    vj = V(vec.tensor_scalar(T.pm[:], T.pi[:], 15, None, Op.bitwise_and))
     W("v", ka)
     va = V(vec.quantize_mx(T.qa[:], T.qas[:], T.at[:]))
     W("g", vx)
-    send_ends(0, "nc", "C0", "N0", 48, (0, 176), (208, 128))
-    send_ends(0, "ns", "C0", "N0", 48, (0, 176), (208, 128))
+    send_ends(0, "nc", "C0", "N0", 48, (0, 128), (208, 176))
+    send_ends(0, "ns", "C0", "N0", 48, (0, 128), (208, 176))
 
     def cost_mm(k, name, a):
         return P(ten.matmul_mx(bank(k, 0, 128), T[name][:, a:a + 128], T[name + "s"][:, a:a + 128], T.qa[:], T.qas[:], True, True))
@@ -145,7 +147,7 @@ def rank_program(g, core, T, topo):
         return A(act.activation(T.junk[a:b, j:j + 128], T.ps[a:b, 512 * k:512 * k + 128], Act.Sign, bias=T.eps[a:b, 0:1],
                                 accum_out=T["L%d" % t][a:b, c:c + 1]))
 
-    W("p", va)
+    W("p", va, vx)
     p0, p1 = cost_mm(4, "C0", 0), cost_mm(5, "C0", 128)
     W("a", veps)
     count(0, 0, 4, p0)
@@ -154,10 +156,11 @@ def rank_program(g, core, T, topo):
     W("g", a1)
     send_costs(0)
 
-    V(vec.memset(T.h1[:, 0:160], 0.0))
-    V(vec.memset(T.h1[:, 1504:1536], 0.0))
+    W("v", vj)
+    vj = V(vec.tensor_copy(T.pf[:], T.pm[:]))
     vmm = V(vec.memset(T.MM[:], 0.0))
-    V(vec.memset(T.XX[0:32, :], 0.0))
+    W("v", vj)
+    vj = V(vec.tensor_tensor(T.J[:], T.j0[:], T.pf[:], Op.add))
     W("v", kw)
     vw = V(vec.quantize_mx(T.qw[:], T.qws[:], T.wt[:]))
 
@@ -183,16 +186,16 @@ def rank_program(g, core, T, topo):
     V(vec.memset(T.z16[:], 0.0))
     for b in range(1, n):
         V(vec.memset(T.wq[:, b - 1:b], b / 4.0))
-    V(vec.memset(T.c130[0:32, :], 130.0))
-    rl = relus("a", (0, 2), pm, 0, T.h1, (0, 80, 256)) + relus("v", (1, 3), pm, 0, T.h1, (0, 80, 256))
+    V(vec.memset(T.XX[0:32, :], 0.0))
+    own = ((0, 176, 208), (176, 0, 80))
+    rl = relus("a", (0, 2), pm, 0, T.h1, *own) + relus("v", (1, 3), pm, 0, T.h1, *own)
+    V(vec.memset(T.c130[0:32, 0:128], 0.0))
     W("v", *rl)
-    vq1 = V(vec.quantize_mx(T.W1[:, 128:256], T.W1s[:, 128:256], T.h1[:, 512:1024]))
-    for t in range(3):
-        V(vec.memset(T.kb[0:32, t:t + 1], 130.0 * HALF[t] - 0.125))
+    vq1 = V(vec.quantize_mx(T.W1[:, 224:384], T.W1s[:, 224:384], T.h1[:, 896:1536]))
     W("p", *vpad0, a1, ("nc0", n_in), ("ns0", n_in))
     ph0 = [w_mm(4 + b, b, "N0", 128, 128) for b in range(4)]
     W("p", vq1, *rl)
-    pc1 = cost_mm(0, "W1", 128)
+    pc1 = cost_mm(0, "W1", 224)
 
     BO = lambda t, a, b: T.BBB[:, 32 * t + a:32 * t + b]
 
@@ -225,42 +228,39 @@ def rank_program(g, core, T, topo):
         mo = 96 * t
         W("v", vq)
         for k in range(4):
-            v = V(vec.transpose(T["Zq%d" % t][0:32, 32 * k:32 * k + 32], T.MM[32 * k:32 * k + 32, mo:mo + 32]))
+            v = V(vec.transpose(T["Zh%d" % t][0:32, 32 * k:32 * k + 32], T.MM[32 * k:32 * k + 32, mo:mo + 32]))
         return v
-
-    def b_qsum(t, v):
-        W("a", v)
-        return A(act.activation(T.rjunk[0:5, 512 * t:512 * t + 128], T["Zq%d" % t][0:5, :], Act.Copy,
-                                accum_out=T["Ih%d" % t][0:5, 0:1]))
 
     def b_tx(t, vxx, half):
         mo, Zh = 96 * t + 32, T["Zh%d" % t]
         W("v", vxx)
         if half == 0:
             for k in range(4):
-                z = k if t else (k + 2) % 4
+                z = 4 + (k if t else (k + 2) % 4)
                 v = V(vec.transpose(Zh[0:32, 32 * z:32 * z + 32], T.MM[32 * k:32 * k + 32, mo:mo + 32]))
         else:
             for k in range((0, 1, 4)[t]):
-                v = V(vec.transpose(Zh[0:32, 128 + 32 * k:160 + 32 * k], T.MM[32 * k:32 * k + 32, mo + 32:mo + 64]))
+                v = V(vec.transpose(Zh[0:32, 256 + 32 * k:288 + 32 * k], T.MM[32 * k:32 * k + 32, mo + 32:mo + 64]))
         return v
 
-    def b_scan(t, v, aq):
-        h = 2 * HALF[t]
-        Ih = T["Ih%d" % t]
-        W("v", v, aq)
-        return V(vec.tensor_tensor_scan(Ih[0:5, 1:1 + h], T["Zh%d" % t][0:5, 0:h], T.c130[0:5, 0:h], Ih[0:5, 0:1], Op.add, Op.add))
+    def b_scan(t, v):
+        h = 128 + HALF[t] + MOVE[t]
+        W("v", v)
+        return V(vec.tensor_tensor_scan(T["Ih%d" % t][0:5, 0:h], T["Zh%d" % t][0:5, 0:h], T.c130[0:5, 0:h], 0.0, Op.add, Op.add))
 
     def b_sign(t, v):
-        a, w = HALF[t] - MOVE[t], 2 * MOVE[t]
+        a, w = 127 + HALF[t] - MOVE[t], 2 * MOVE[t]
         W("a", v)
         return A(act.activation(T.rjunk[0:5, 512 * t + 128:512 * t + 128 + w], T["Ih%d" % t][0:5, a:a + w], Act.Sign,
                                 bias=T.kb[0:5, t:t + 1], scale=-1.0, accum_out=T.row[0:5, t:t + 1]))
 
-    def b_clamp(t, av):
+    xx = {}
+
+    def b_clamp(t, av, fill):
         W("v", av)
-        v = V(vec.tensor_scalar(T.XX[0:5, 32 * t:32 * t + 32], T.lo[0:5, 32 * t:32 * t + 32], T.row[0:5, t:t + 1],
-                                T.hi[0:5, t:t + 1], Op.max, Op.min))
+        v = xx[t] = V(vec.tensor_scalar(T.XX[0:5, 32 * t:32 * t + 32], T.lo[0:5, 32 * t:32 * t + 32], T.row[0:5, t:t + 1],
+                                        T.hi[0:5, t:t + 1], Op.max, Op.min))
+        fill()
         W("v", v)
         for k in range(4):
             v = V(vec.transpose(T.BBB[32 * k:32 * k + 32, 32 * t:32 * t + 32], T.XX[0:32, 32 * t:32 * t + 32]))
@@ -268,7 +268,7 @@ def rank_program(g, core, T, topo):
 
     def b_range(t):
         V(vec.tensor_tensor(T.lo[0:5, 32 * t + 32:32 * t + 64], T.XX[0:5, 32 * t:32 * t + 32], T.nhb[0:5, :], Op.subtract))
-        V(vec.tensor_tensor(T.hi[0:5, t + 1:t + 2], T.XX[0:5, 32 * t:32 * t + 1], T.nhb[0:5, 0:1], Op.add))
+        return V(vec.tensor_tensor(T.hi[0:5, t + 1:t + 2], T.XX[0:5, 32 * t:32 * t + 1], T.nhb[0:5, 0:1], Op.add))
 
     def masks(t, cols):
         MK = T["MK%d" % t]
@@ -280,68 +280,56 @@ def rank_program(g, core, T, topo):
         return v
 
     lm0 = ("lm0", l_in)
-    W("a", lm0, vmm, a1)
-    A(act.activation(T.MM[64:128, 33:36], T.L0[64:128, 2:11:4], Act.Copy))
-    ax = A(act.activation(T.MM[0:64, 33:36], T.L0[0:64, 4:13:4], Act.Copy))
-    halo = ((8, 40, 40), (48, 336, 40))
-    hr = relus("a", (0, 2), ph0, 4, T.h1, *halo)
-    vps = b_ps(0, lm0, a1)
-    hr += relus("v", (1,), ph0, 4, T.h1, *halo)
-    vsh = b_share(0, vps)
-    hr += relus("v", (3,), ph0, 4, T.h1, *halo)
+    halo = ((0, 80, 96),)
+    hr = relus("a", (0, 2), ph0, 4, T.h1, *halo) + relus("v", (1, 3), ph0, 4, T.h1, *halo)
+    kb(0)
     W("v", *hr, *rl)
-    vp0 = V(vec.quantize_mx(T.W1[:, 0:128], T.W1s[:, 0:128], T.h1[:, 0:512]))
-    vp2 = V(vec.quantize_mx(T.W1[:, 256:384], T.W1s[:, 256:384], T.h1[:, 1024:1536]))
-    vq = b_sub(0, vsh)
-    vt2 = b_tx(0, ax, 0)
-    vt = b_tq(0, vq)
-    W("p", vp0)
-    pc0 = cost_mm(1, "W1", 0)
+    vp2 = V(vec.quantize_mx(T.W1[:, 0:224], T.W1s[:, 0:224], T.h1[:, 0:896]))
+    W("g", vp2)
+    send_ends(1, "nc", "W1", "W1", 120, (136, 512), (0, 384))
+    send_ends(1, "ns", "W1", "W1", 120, (136, 512), (0, 384))
     W("p", vp2)
-    pc2 = cost_mm(2, "W1", 256)
+    pc0 = cost_mm(1, "W1", 96)
+    pc2 = cost_mm(2, "W1", 0)
     ac1 = count(1, 1, 0, pc1)
     ac0 = count(1, 0, 1, pc0)
     ac2 = count(1, 2, 2, pc2)
-    aq = b_qsum(0, vt)
-    W("g", vp2)
-    send_ends(1, "nc", "W1", "W1", 120, (40, 512), (256, 384))
-    send_ends(1, "ns", "W1", "W1", 120, (40, 512), (256, 384))
     W("g", ac0, ac1, ac2)
     send_costs(1)
-    W("v", gset)
-    vj = V(vec.tensor_scalar(T.pm[:], T.pi[:], 15, None, Op.bitwise_and))
+    vps = b_ps(0, lm0, a1, vmm)
+    V(vec.tensor_copy(T.MM[64:128, 33:36], T.L0[64:128, 2:11:4]))
+    vsh = b_share(0, vps)
+    ax = V(vec.tensor_copy(T.MM[0:64, 33:36], T.L0[0:64, 4:13:4]))
+    vq = b_sub(0, vsh)
+    V(vec.memset(T.c130[0:32, 128:232], 130.0))
+    b_tx(0, ax, 0)
+    vt = b_tq(0, vq)
+    W("v", gset, vj)
     V(vec.tensor_scalar(T.lo[0:32, 0:32], T.nhb[0:32, :], -1.0, None, Op.mult))
-    V(vec.tensor_copy(T.hi[0:32, 0:1], T.nhb[0:32, 0:1]))
-    W("v", vj)
-    vj = V(vec.tensor_copy(T.pf[:], T.pm[:]))
-    V(vec.memset(T.MK1[:], 1.0))
-    vs = b_scan(0, vt2, aq)
+    vs = b_scan(0, vt)
     av = b_sign(0, vs)
-    W("v", vj)
-    vj = V(vec.tensor_tensor(T.J[:], T.j0[:], T.pf[:], Op.add))
-    V(vec.memset(T.m2[:, 0:160], 0.0))
-    W("v", vj)
+    vhi = V(vec.tensor_copy(T.hi[0:32, 0:1], T.nhb[0:32, 0:1]))
     V(vec.tensor_scalar(T.JL[:], T.J[:, 0:8], 2.0, -160.0, Op.mult, Op.add))
     V(vec.tensor_scalar(T.JR[:], T.J[:, 0:8], 2.0, -96.0, Op.mult, Op.add))
-    V(vec.tensor_copy(T.Jm[:, 0:8], T.J[:, 0:8]))
-    vj = V(vec.tensor_scalar(T.Jm[:, 8:16], T.J[:, 0:8], 288.0, None, Op.add))
+    V(vec.tensor_scalar(T.Jm[:, 0:8], T.J[:, 0:8], 96.0, None, Op.add))
+    vj = V(vec.tensor_scalar(T.Jm[:, 8:16], T.J[:, 0:8], 32.0, None, Op.add))
     W("p", *rl, ac0, ac1, ac2)
-    pm = [w_mm(b, b, "W1", 128, 160) for b in range(4)]
-    vB = b_clamp(0, av)
+    pm = [w_mm(b, b, "W1", 224, 160) for b in range(4)]
+    rm = relus("a", (0, 1, 2, 3), pm, 0, T.m2, (0, 168, 160))
+    W("v", vhi)
+    vB = b_clamp(0, av, lambda: V(vec.memset(T.MK1[:], 1.0)))
+    kb(1)
     W("v", vB, vj)
-    V(vec.tensor_scalar(T.t1[:, 0:8], T.JL[:], BO(0, r, r + 1), 384.0, Op.is_lt, Op.mult))
-    vl = V(vec.tensor_scalar(T.t1[:, 8:16], T.JR[:], BO(0, r + 1, r + 2), 216.0, Op.is_ge, Op.mult))
-    mk1 = masks(1, ((0, 0, True), (2, 0, False)))
+    V(vec.tensor_scalar(T.t1[:, 0:8], T.JL[:], BO(0, r, r + 1), 288.0, Op.is_lt, Op.mult))
+    vl = V(vec.tensor_scalar(T.t1[:, 8:16], T.JR[:], BO(0, r + 1, r + 2), 472.0, Op.is_ge, Op.mult))
+    masks(1, ((0, 0, True),))
     W("v", vl)
     vl = V(vec.tensor_tensor(T.t2[:], T.t1[:], T.Jm[:], Op.add))
-    b_range(0)
+    mk1 = masks(1, ((2, 0, False),))
     W("v", vl)
     vl = V(vec.tensor_copy(T.la[:], T.t2[:]))
-    rm = relus("a", (0, 2), pm, 0, T.m2, (0, 168, 160)) + relus("v", (1, 3), pm, 0, T.m2, (0, 168, 160))
     vpad1 = zeros("W1", *(([384] if left is None else []) + ([512] if right is None else [])))
-    V(vec.memset(T.m2[:, 1824:2048], 0.0))
-    V(vec.tensor_scalar(T.J8[:, 0:4], T.J[:, 0:4], 2.0, 240.0, Op.mult, Op.add))
-    vj = V(vec.tensor_scalar(T.J8[:, 4:8], T.J[:, 0:4], 2.0, 624.0, Op.mult, Op.add))
+    b_range(0)
 
     vpk, apk = [], []
     W("v", vl, vp2, vq1, *vpad1, ("nc1", n_in))
@@ -355,49 +343,52 @@ def rank_program(g, core, T, topo):
     pL = [w_mm(4 + b, b, "M1", 0, 128) for b in range(4)]
     W("p", vpk[1], apk[1], *rm)
     pR = [w_mm(b, b, "M1", 128, 128) for b in range(4)]
-    vpad2 = zeros("N2", *pads)
+    W("v", *rm, *vpc)
+    V(vec.quantize_mx(T.C2[:, 168:328], T.C2s[:, 168:328], T.m2[:, 672:1312]))
+    V(vec.memset(T.c130[0:32, 232:368], 130.0))
+    rL = relus("a", (0, 2), pL, 4, T.m2, (0, 40, 128)) + relus("v", (1, 3), pL, 4, T.m2, (0, 40, 128))
+    rR = relus("a", (0, 1, 2, 3), pR, 0, T.m2, (0, 328, 128))
     vm = b_mask(1, mk1, ac0, ac1, ac2)
-    rL = relus("a", (0, 2), pL, 4, T.m2, (0, 40, 128)) + relus("v", (1,), pL, 4, T.m2, (0, 40, 128))
+    W("v", *rL)
+    vc0 = V(vec.quantize_mx(T.C2[:, 40:168], T.C2s[:, 40:168], T.m2[:, 160:672]))
     vps = b_ps(1, vm)
     vxx = b_x(1)
-    rL += relus("v", (3,), pL, 4, T.m2, (0, 40, 128))
     vsh = b_share(1, vps)
-    W("v", *rL, *rm)
-    vc0 = V(vec.quantize_mx(T.C2[:, 0:256], T.C2s[:, 0:256], T.m2[:, 0:1024]))
-    vq = b_sub(1, vsh)
-    rR = relus("v", (1,), pR, 0, T.m2, (0, 328, 128))
-    vt = b_tq(1, vq)
-    rR += relus("a", (0, 2), pR, 0, T.m2, (0, 328, 128)) + relus("v", (3,), pR, 0, T.m2, (0, 328, 128))
-    aq = b_qsum(1, vt)
-    W("v", *rR)
-    vc1 = V(vec.quantize_mx(T.C2[:, 256:512], T.C2s[:, 256:512], T.m2[:, 1024:2048]))
     b_tx(1, vxx, 0)
-    vt2 = b_tx(1, vxx, 1)
-    vs = b_scan(1, vt2, aq)
+    vq = b_sub(1, vsh)
+    W("v", *rR)
+    vc1 = V(vec.quantize_mx(T.C2[:, 328:456], T.C2s[:, 328:456], T.m2[:, 1312:1824]))
+    b_tx(1, vxx, 1)
+    vt = b_tq(1, vq)
     W("p", vc0, *rL)
     pc = [cost_mm(4, "C2", 0), cost_mm(5, "C2", 128)]
     W("p", vc1)
     pc += [cost_mm(6, "C2", 256), cost_mm(7, "C2", 384)]
     ac = [count(2, k, 4 + k, pc[k]) for k in range(4)]
-    av = b_sign(1, vs)
     W("g", *ac)
     send_costs(2)
+    kb(2)
+    vs = b_scan(1, vt)
+    av = b_sign(1, vs)
     W("p", *rR)
     pm = [w_mm(b, b, "C2", 40, 416) for b in range(4)]
     ro = relus("a", (0,), pm, 0, T.m3, (0, 0, 416))
-    V(vec.tensor_scalar(T.J2[:], T.J[:], 2.0, None, Op.mult))
+    V(vec.tensor_scalar(T.J8[:, 0:4], T.J[:, 0:4], 2.0, 240.0, Op.mult, Op.add))
+    vj = V(vec.tensor_scalar(T.J8[:, 4:8], T.J[:, 0:4], 2.0, 624.0, Op.mult, Op.add))
+    vpad2 = zeros("N2", *pads)
     V(vec.tensor_scalar(T.J2m[:], T.J[:], 2.0, -512.0, Op.mult, Op.add))
+    vB = b_clamp(1, av, lambda: V(vec.tensor_scalar(T.J2[:], T.J[:], 2.0, 160.0, Op.mult, Op.add)))
     vhz = V(vec.memset(T.hh2[:, 320:512], 0.0))
-    vB = b_clamp(1, av)
     W("v", vB, vj)
     V(vec.tensor_scalar(T.lb[:, 0:4], T.J8[:, 0:4], BO(1, r, r + 1), 0.5, Op.add, Op.mult))
     vl = V(vec.tensor_scalar(T.lb[:, 4:8], T.J8[:, 4:8], BO(1, r + 1, r + 2), 0.5, Op.add, Op.mult))
-    mk2 = masks(2, ((0, 1, True), (1, 2, True), (2, 1, False), (3, 2, False)))
+    masks(2, ((0, 1, True),))
     W("v", vl)
     vh = V(vec.tensor_copy(T.H2[:].bitcast(dt.uint32), T.C2[:, 0:512].bitcast(dt.uint32).indirect(T.lb[:, 0:8])))
+    mk2 = masks(2, ((1, 2, True), (2, 1, False), (3, 2, False)))
+    V(vec.tensor_scalar(T.kk[:, 0:1], BO(1, r, r + 1), -0.5 / SC, 376.0 / SC, Op.mult, Op.add))
     W("v", mk2)
-    for b in range(n - 1):
-        vw = V(vec.tensor_tensor(T.MW[:, 16 * b:16 * b + 16], T.MK2[:], T.WT[:, 16 * b:16 * b + 16], Op.mult))
+    vm = b_mask(2, *ac)
     W("a", vl, vc1)
     ah = A(act.activation(T.H2s[:], T.C2s[:, 0:512].indirect(T.lb[:, 0:8]), Act.Copy))
     W("g", vh)
@@ -406,84 +397,70 @@ def rank_program(g, core, T, topo):
     send_ends(2, "ns", "H2", "N2", 48, (0, 176), (80, 128))
     ro += relus("a", (1, 2, 3), pm, 0, T.m3, (0, 0, 416))
 
-    W("v", ("lm2", l_in), vw, *ac)
-    for b in range(n - 1):
-        vw = V(vec.tensor_tensor(T.LW[:, 16 * b:16 * b + 16], T.L2[:], T.MW[:, 16 * b:16 * b + 16], Op.mult))
-    vm = b_mask(2)
-    W("v", vw)
-    for b in range(n - 1):
-        vq = V(vec.tensor_reduce(T.MM[:, 193 + b:194 + b], T.LW[:, 16 * b:16 * b + 16], AxisListType.X, Op.add))
-    W("v", vm)
+    V(vec.tensor_scalar(T.kk[:, 1:2], BO(1, r + 1, r + 2), -0.5 / SC, 120.0 / SC, Op.mult, Op.add))
+    vps = b_ps(2, vm)
     vxx = b_x(2)
-    vt = b_tq(2, vq)
+    vsh = b_share(2, vps)
     b_tx(2, vxx, 0)
-    vt2 = b_tx(2, vxx, 1)
+    vq = b_sub(2, vsh)
+    b_tx(2, vxx, 1)
+    vt = b_tq(2, vq)
     b_range(1)
-    aq = b_qsum(2, vt)
-    vs = b_scan(2, vt2, aq)
+    vs = b_scan(2, vt)
     av = b_sign(2, vs)
-    V(vec.tensor_scalar(T.kk[:, 0:1], BO(1, r, r + 1), -0.5, 376.0, Op.mult, Op.add))
-    vk = V(vec.tensor_scalar(T.kk[:, 1:2], BO(1, r + 1, r + 2), -0.5, 120.0, Op.mult, Op.add))
-    W("p", *vpad2, *ac, ("nc2", n_in), ("ns2", n_in))
-    ph = [w_mm(4 + b, b, "N2", 128, 128) for b in range(4)]
     W("v", *ro)
     vc3 = V(vec.quantize_mx(T.C3[:, 0:416], T.C3s[:, 0:416], T.m3[:]))
-    h2 = relus("a", (0, 2), ph, 4, T.hh2, (8, 0, 80))
-    vB = b_clamp(2, av)
-    h2 += relus("v", (1, 3), ph, 4, T.hh2, (8, 0, 80))
-    W("a", vB)
-    for t in range(3):
-        ab = A(act.activation(T.Bh[:, 5 * t:5 * t + 5], BO(t, 0, 5), Act.Copy, scale=0.5))
-    W("v", vB, vk)
-    U2, V2, U = T.terms[:, 0:31], T.terms[:, 31:62], T.terms[:, 62:93]
-    V(vec.tensor_scalar(U2, T.J2[:], BO(2, r, r + 1), None, Op.add))
-    V(vec.tensor_scalar(V2, T.J2m[:], BO(2, r, r + 1), None, Op.add))
-    vu = V(vec.tensor_scalar(U, T.J2[:], BO(2, r, r + 1), 0.5, Op.add, Op.mult))
+    V(vec.tensor_scalar(T.J2n[:, 0:31], T.J[:], -2.0, BO(1, r, r + 1), Op.mult, Op.add))
+    W("p", *vpad2, *ac, ("nc2", n_in), ("ns2", n_in))
+    ph = [w_mm(4 + b, b, "N2", 128, 128) for b in range(4)]
+    W("p", vc3, *ro)
+    py = P(ten.matmul_mx(bank(0, 0, 416), T.qa[:], T.qas[:], T.C3[:, 0:416], T.C3s[:, 0:416], True, True))
+    vB = b_clamp(2, av, lambda: V(vec.tensor_scalar(T.J2n[:, 31:62], T.J2m[:], -1.0, BO(1, r + 1, r + 2), Op.mult, Op.add)))
+    vbz = V(vec.memset(T.Bh[0:32, :], 0.0))
+    h2 = relus("a", (0, 1, 2, 3), ph, 4, T.hh2, (8, 0, 80))
+    W("a", py)
+    A(act.activation(T.YC[:, 0:416], bank(0, 0, 416), Act.Copy))
+    W("v", vB)
+    d2 = BO(2, r, r + 1)
+    V(vec.tensor_scalar(T.terms[:, 0:31], T.J2[:], d2, 0.5 / SC, Op.add, Op.mult))
+    V(vec.tensor_scalar(T.terms[:, 31:62], T.J2n[:, 0:31], d2, T.kk[:, 0:1], Op.is_gt, Op.mult))
+    V(vec.tensor_scalar(T.terms[:, 62:93], T.J2n[:, 31:62], d2, T.kk[:, 1:2], Op.is_le, Op.mult))
+    vu = V(vec.tensor_scalar(T.terms[:, 93:124], T.J2m[:], d2, BO(2, r + 1, r + 2), Op.add, Op.is_ge))
+    W("v", vbz)
+    vb = V(vec.tensor_scalar(T.Bh[0:5, 0:3], T.XX[0:5, 0:96:32], 0.5, T.B0[0:5, 0:1], Op.mult, Op.add))
+    W("v", vu)
+    vu = V(vec.tensor_tensor(T.sum3[:, 0:62], T.terms[:, 0:62], T.terms[:, 62:124], Op.add))
     W("v", vhz, *h2)
     vch = V(vec.quantize_mx(T.C3[:, 416:544], T.C3s[:, 416:544], T.hh2[:]))
     W("v", vu)
-    V(vec.tensor_scalar(T.terms[:, 93:124], U2, BO(1, r, r + 1), T.kk[:, 0:1], Op.is_lt, Op.mult))
-    V(vec.tensor_scalar(T.terms[:, 124:155], V2, BO(1, r + 1, r + 2), T.kk[:, 1:2], Op.is_ge, Op.mult))
-    vu = V(vec.tensor_scalar(T.terms[:, 155:186], V2, BO(2, r + 1, r + 2), 2000.0, Op.is_ge, Op.mult))
-    W("v", vu)
-    vu = V(vec.tensor_tensor(T.sum3[:, 0:62], T.terms[:, 62:124], T.terms[:, 124:186], Op.add))
-    W("v", vu)
     vu = V(vec.tensor_tensor(T.sum1[:, 0:31], T.sum3[:, 0:31], T.sum3[:, 31:62], Op.add))
+    vN = V(vec.transpose(T.Ball[0:32, :], T.Bh[0:32, :]))
     W("v", vu)
-    vl = V(vec.tensor_scalar(T.lf[:, 0:31], T.sum1[:, 0:31], 80.0, 500.0, Op.add, Op.min))
-    W("v", ab)
-    vN = V(vec.tensor_tensor(T.Ball[:, 0:15], T.Bh[:, 0:15], T.B0[:], Op.add))
-    W("p", vc3, *ro)
-    py = P(ten.matmul_mx(bank(0, 0, 416), T.qa[:], T.qas[:], T.C3[:, 0:416], T.C3s[:, 0:416], True, True))
+    vl = V(vec.tensor_scalar(T.lf[:, 0:31], T.sum1[:, 0:31], SC, 500.0, Op.mult, Op.min))
     W("p", vch)
     pz = P(ten.matmul_mx(bank(1, 0, 128), T.qa[:], T.qas[:], T.C3[:, 416:544], T.C3s[:, 416:544], True, True))
-    W("a", py)
-    A(act.activation(T.YC[:, 0:416], bank(0, 0, 416), Act.Copy))
     W("a", pz)
     yc = A(act.activation(T.YC[:, 416:544], bank(1, 0, 128), Act.Copy))
 
     W("v", vl, vch, vc3)
-    W("a", vl, vch, vc3)
+    W("a", vl, vch, vc3, yc)
     halves = ((0, 256), (256, 496))
     vf, af = [], []
     for a, b in halves:
         l = T.lf[:, a // 16:b // 16]
         vf.append(V(vec.tensor_copy(T.F[:, a:b].bitcast(dt.uint32), T.C3[:, 0:544].bitcast(dt.uint32).indirect(l))))
-        af.append(A(act.activation(T.Fs[:, a:b], T.C3s[:, 0:544].indirect(l), Act.Copy)))
-    W("v", yc)
-    W("a", yc)
-    vy = V(vec.tensor_copy(T.yt[:, 0:256], T.YC[:, 0:544].indirect(T.lf[:, 0:16])))
-    ay = A(act.activation(T.yt[:, 256:496], T.YC[:, 0:544].indirect(T.lf[:, 16:31]), Act.Copy))
+        af.append(A(act.activation(T.yt[:, a:b], T.YC[:, 0:544].indirect(l), Act.Copy)))
+    vs0 = V(vec.tensor_copy(T.Fs[:, 0:352], T.C3s[:, 0:544].indirect(T.lf[:, 0:22])))
+    as1 = A(act.activation(T.Fs[:, 352:496], T.C3s[:, 0:544].indirect(T.lf[:, 22:31]), Act.Copy))
     W("s", vN)
-    inc("dout", g.sync.dma_start(T.bd[:], T.Ball[0:1, 0:15]), 16)
+    inc("dout", g.sync.dma_start(T.bd[:], T.Ball[0:3, 0:5]), 16)
     for k, (a, b) in enumerate(halves):
         W("s", vf[k])
         inc("dout", g.sync.dma_start(T.oc[:, 4 * a:4 * b], T.F[:, a:b].bitcast(dt.uint8)), 16)
-    W("s", af[1])
+        W("s", af[k])
+        inc("dout", g.sync.dma_start(T.y[:, a:b], T.yt[:, a:b]), 16)
+    W("s", vs0, as1)
+    W("a", vs0, as1)
     for i in range(4):
-        inc("dout", g.sync.dma_start(T.osc[4 * i:4 * i + 4, :], T.Fs[32 * i:32 * i + 4, :]), 16)
-    W("s", vy)
-    inc("dout", g.sync.dma_start(T.y[:, 0:256], T.yt[:, 0:256]), 16)
-    W("a", ay)
-    inc("dout", act.dma_start(T.y[:, 256:496], T.yt[:, 256:496]), 16)
+        inc("dout", (act if i % 2 else g.sync).dma_start(T.osc[4 * i:4 * i + 4, :], T.Fs[32 * i:32 * i + 4, :]), 16)
     W("g", *[(s, c) for s, c in cnt.items()])

@@ -1,26 +1,38 @@
-import numpy as np
 from concourse.bass import DstId, RemoteDMATransfer
-from concourse.mybir import dt, AluOpType as Op, AxisListType, ActivationFunctionType as Act
+from concourse.mybir import dt, AluOpType as Op, ActivationFunctionType as Act
 
 F32, BF, I32, U16, F8, U8 = "float32", "bfloat16", "int32", "uint16", "float8_e4m3fn_x4", "uint8"
 SCRATCH = {"ps": ("psum", [128, 4096], F32)}
-for _names, _d in (("xt:1024 at:512 wt:2048 h1:1536 m2:2048 m3:1664 hh2:512 zt:512 junk:1408", BF),
-                   ("eps:4 kb:4 c130:384 nh:32 nha:32 nhb:32 MM:288 XX:96 lo:96 hi:4 BBB:96 row:16 rjunk:1536 B0:4 Bh:32 Ball:32 "
-                    "pf:31 j0:31 J:31 J2:31 J2m:31 J2n:62 JL:8 JR:8 Jm:16 J8:8 gi:4 wq:4 z16:16 MK1:16 MK2:16 "
-                    "LM:48 PS:48 TW:16 t1:16 t2:16 kk:4 terms:192 sum3:64 sum1:32 yt:512 YC:544 L0:16 L1:16 L2:16 "
-                    "Zh0:256 Zh1:288 Zh2:384 Ih0:256 Ih1:288 Ih2:384", F32),
-                   ("pi:31 pm:31", I32), ("la:16 lb:8 lf:32", U16)):
+for _names, _d in (("xt:1024 at:512 wt:2048 h1:1664 m2:1728 m3:1728 hh2:512 junk:1408", BF),
+                   ("eps:4 kb:4 RA:192 nh:32 nha:32 nhb:32 MM:160 XX:128 lo:32 hi:4 BBB:96 row:16 rjunk:480 B0:4 Bh:32 Ball:32 "
+                    "pf:4 K:76 KK:76 gi:8 wq:4 cp:4 cc:4 MK1:16 MK2:16 LA:172 L1:16 L2:16 PS:48 TW:12 th:100 TM:188 HM:188 SM:188 "
+                    "yt:496 Zh0:160 Zh1:192 Zh2:192 Ih:192", F32),
+                   ("pi:4 pm:4", I32), ("la:16 lb:8 lf:32", U16)):
     for _s in _names.split():
         SCRATCH[_s.split(":")[0]] = ("sbuf", [128, int(_s.split(":")[1])], _d)
-for _n, _w in (("qa", 128), ("qw", 512), ("C0", 256), ("W1", 640), ("M1", 256), ("C2", 512), ("C3", 544),
-               ("H2", 128), ("N0", 352), ("N2", 352), ("F", 496)):
+for _n, _w in (("qa", 128), ("qw", 512), ("C0", 464), ("W1", 672), ("M1", 256), ("C2", 440), ("C3", 560),
+               ("H2", 176), ("F", 496)):
     SCRATCH[_n] = ("sbuf", [128, _w], F8)
     SCRATCH[_n + "s"] = ("sbuf", [128, _w], U8)
-SEMAPHORES = ["sv", "sa", "sp", "gc", "dx0", "dx1", "da", "dw", "dout", "ls"] + \
+SEMAPHORES = ["sv", "sa", "sp", "sg", "dx0", "dx1", "dx2", "da", "dw0", "dw1", "dout", "ls"] + \
     ["%s%d" % (n, t) for n in ("nc", "ns", "lm") for t in range(3)]
-HALF = (64, 80, 120)
-MOVE = (40, 80, 120)
-SC = 2048.0
+HALF = (64, 80, 80)
+MOVE = (40, 80, 80)
+BIG = 2048.0
+CUTS = ((0, 256), (256, 496))
+ORDER = {
+    "s0": "lxa lxr lw0 sbd soc0 soc1 sos0 sos2 sy0",
+    "g0": "ipi sel0 sel1 iwq igi sc0a ss0a sl0 iN iM0 iM1 iM2 iM3 iB0 icp0 icp1 sc1a ss1a sl1 sl2 sc2a ss2a",
+    "p0": "mM mE o1 o0 o3 o2 h1 h2 h0 h3 d0 d1 k11 d2 k12 k10 d3 k22 L3 L2 L1 L0 R2 R0 R3 R1 k21 k23 k20 f0 f3 f1 f2 n3 n1 n0 n2 y0 y1",
+    "a0": "lxb la lw1 c01 c00 ro1a ro0a ro3b ro0b ro3a ro1b rh2 rh3 rd0 c11 rd1 c12 rd3 sign0 c10 pMs0 c22 pMs1 ro7b ro7a rR2 rR0 rR1 c21 c23 c20 bh0 sign1 rf3 rf1 pHs th1 rf2 kb2 hi2 sign2 th4 bh2 tbase rn1 rn3 bh1 pFs0 pFs1 sos3 sos1 sy1",
+    "v0": "znh zkb1 zh1 zeps zL0 zhh zHM zHM2 qE pand zLa zXX pcopy zL1 qR qD qa zkb0 zgj qw1 zMM qw0 zHM1 zLb qw3 zMK qw2 ro2a zBh zRWb lo0 zgi q1a ro2b rh1 rh0 KK q1b tz03 ps0 tz02 tz01 sh0 sub0 tz00 tl00 tl01 rd2 scan0 q2m clamp0 clamp0b tb00 tb01 lM1 lM0 lM2 pM0 mk22 pM1 th35 mk12 mk21 ro6a ro6b ro4b ro5b ro5a mk10 ro4a rR3 mask1 q2L x1 q2R ps1 tz11 tz12 sh1 tz13 tz14 sub1 tz10 tl10 tl11 zHM0 scan1 rf0 clamp1 xd xdb c23c tb11 tb10 lH0 lH1 mk23 mk20 pH mask2 x2 ps2 tz24 tz20 sh2 tz21 tz22 sub2 lo2 tz23 tl21 tl20 c14c scan2 q3w clamp2 clamp2b tb20 tb21 t1 t3 t4 t2 tend rn0 rn2 sum q3h lF tbd pF0 pF1 yc0 yc1",
+    "s1": "lxa lxr lw0 soc0 soc1 sos0 sbd sy0 sos2",
+    "g1": "ipi sel0 sel1 iwq igi sc0a ss0a sl0 iN iM0 iM1 iM2 iM3 iB0 icp0 icp1 sc1a ss1a sl1 sl2 sc2a ss2a",
+    "p1": "mM mE o1 o0 o2 o3 h3 h0 h2 h1 d3 k11 d2 d0 d1 k12 k10 k22 L2 L3 L0 L1 R3 R1 R0 R2 k21 k23 k20 f0 f2 f3 f1 n1 n3 n2 n0 y0 y1",
+    "a1": "lxb la lw1 c01 ro0a c00 ro0b ro3a ro3b rh3 rh2 rd3 c11 rd0 rd1 c10 sign0 c12 kb2 pMs0 c22 pMs1 ro7a ro7b rR3 rR1 rR0 c21 c23 c20 sign1 rf0 rf2 pHs rf1 rf3 sign2 th4 bh0 tbase rn3 rn1 bh1 bh2 pFs0 pFs1 sos3 sos1 sy1",
+    "v1": "znh zkb1 zh1 zhh zHM pand zXX zLb zHM1 qE zLa zL1 qD zeps lo0 zgi zL0 qR pcopy zMK qa qw1 qw0 zHM2 zRWb zMM zBh qw2 qw3 ro2a ro1a zgj ro2b q1a ro1b rh0 rh1 q1b ps0 tz01 tz00 sh0 rd2 sub0 tz02 tz03 tl01 tl00 zkb0 scan0 KK q2m clamp0b clamp0 tb01 tb00 lM1 lM0 mk21 pM0 th35 mk12 lM2 mk10 pM1 ro6b ro6a ro4a mk22 ro5b ro5a ro4b mask1 q2L x1 ps1 tz14 rR2 sh1 q2R tz10 sub1 tz13 tz11 tl11 tz12 tl10 c23c scan1 zHM0 clamp1 xd xdb tb11 tb10 lH0 lH1 mk23 mk20 pH hi2 mask2 th1 lo2 x2 ps2 tz24 sh2 tz20 tz22 sub2 tz23 tz21 tl20 tl21 scan2 c14c q3w clamp2b clamp2 tb20 tb21 t4 t2 t3 t1 tend rn2 rn0 sum q3h lF tbd pF0 pF1 yc0 yc1",
+}
+OPS = {}
 
 
 def rank_program(g, core, T, topo):
@@ -28,30 +40,21 @@ def rank_program(g, core, T, topo):
     if r is None:
         return
     n = len(T.cores)
-    left, right = (r - 1 if r else None), (r + 1 if r < n - 1 else None)
+    left, right = r > 0, r < n - 1
     vec, act, ten = g.vector, g.scalar, g.tensor
     queue = {"v": vec, "a": act, "p": ten, "g": g, "s": g.sync}
-    cnt, seen = {}, {q: {} for q in queue}
+    order = {q: ORDER[q + str(int(left and right))].split() for q in queue}
+    where = {name: q for q in order for name in order[q]}
+    ops, arrive, sent, turns = {}, {}, [0], []
 
-    def W(q, *toks):
-        need = {}
-        for s, c in toks:
-            need[s] = max(need.get(s, 0), c)
-        for s, c in need.items():
-            if seen[q].get(s, 0) < c:
-                queue[q].wait_ge(T.sem[s], c)
-                seen[q][s] = c
+    def op(name, fn, deps="", sem=None):
+        ops[name] = (fn, deps.split(), sem)
 
-    def inc(sem, ins, k=1):
-        ins.then_inc(T.sem[sem], k)
-        cnt[sem] = cnt.get(sem, 0) + k
-        return (sem, cnt[sem])
-
-    V = lambda ins: inc("sv", ins)
-    A = lambda ins: inc("sa", ins)
-    P = lambda ins: inc("sp", ins)
-    G = lambda ins: inc("gc", ins)
+    def rng(s, k=4):
+        return " " + " ".join(s % i for i in range(k)) + " "
     bank = lambda k, a, b: T.ps[:, 512 * k + a:512 * k + b]
+
+    inner = lambda ps: sorted(ps, key=lambda p: abs(2 * p - n + 1))
 
     def nbs(q):
         return [p for p in (q - 1, q + 1) if 0 <= p < n]
@@ -66,401 +69,329 @@ def rank_program(g, core, T, topo):
         rid, pnc, _ = topo.addr(T.cores[p])
         return DstId(rid=rid, pnc=pnc)
 
-    def send_ends(t, name, src, dst, w, to_left, to_right):
+    def send_ends(t, kind, name, w, to):
         tr = []
         for p in nbs(r):
-            a, c = to_left if p < r else to_right
-            if name == "nc":
-                s, d = T[src][:, a:a + w].bitcast(dt.uint8), T[dst][:, c:c + w].bitcast(dt.uint8)
+            a, c = to[int(p > r)]
+            if kind == "c":
+                s, d = T[name][:, a:a + w].bitcast(dt.uint8), T[name][:, c:c + w].bitcast(dt.uint8)
             else:
-                s, d = T[src + "s"][:, a:a + w], T[dst + "s"][:, c:c + w]
+                s, d = T[name + "s"][:, a:a + w], T[name + "s"][:, c:c + w]
             e = engs(r, p)
             tr.append(RemoteDMATransfer(dst_ids=[did(p)], dma_engine_mask=sum(1 << i for i in e),
-                                        remote_sem=T.sem["%s%d" % (name, t)], src=s, dst=d))
-            cnt["ls"] = cnt.get("ls", 0) + len(e)
+                                        remote_sem=T.sem["n%s%d" % (kind, t)], src=s, dst=d))
+            sent[0] += len(e)
         g.remote_dma_fused(tr, local_sem=T.sem.ls)
 
-    others = [p for p in range(n) if p != r]
+    def ends(t, name, w, to, depc, deps):
+        op("sc%da" % t, lambda: send_ends(t, "c", name, w, to), depc)
+        op("ss%da" % t, lambda: send_ends(t, "s", name, w, to), deps)
+
+    others = inner([p for p in range(n) if p != r])
+    Lbuf = lambda t, a, b, p=0, q=128: (T.LA[p:q, 4 + a:4 + b] if t == 0 else T["L%d" % t][p:q, a:b])
 
     def send_costs(t):
-        s = T["L%d" % t][:, 4 * r:4 * r + 4]
+        s = Lbuf(t, 4 * r, 4 * r + 4)
         e = topo.engines(T.cores[r], T.cores[others[0]])
         g.remote_dma_fused([RemoteDMATransfer(dst_ids=[did(p) for p in others], dma_engine_mask=sum(1 << i for i in e),
                                               remote_sem=T.sem["lm%d" % t], srcs=[s], dsts=[s for p in others])],
                            local_sem=T.sem.ls)
-        cnt["ls"] = cnt.get("ls", 0) + len(e)
+        sent[0] += len(e)
 
-    n_in = sum(len(engs(p, r)) for p in nbs(r))
-    l_in = sum(len(topo.engines(T.cores[p], T.cores[r])) for p in others)
-
-    kx0 = inc("dx0", g.sync.dma_start(T.xt[:, 0:512], T.x[:, 0:512]), 16)
-    kx1 = inc("dx1", act.dma_start(T.xt[:, 512:1024], T.x[:, 512:1024]), 16)
-    ka = inc("da", g.sync.dma_start(T.at[:], T.a[:]), 16)
-    inc("dw", act.dma_start(T.wt[:, 1024:2048], T.w[:, 1024:2048]), 16)
-    kw = inc("dw", g.sync.dma_start(T.wt[:, 0:1024], T.w[:, 0:1024]), 16)
-
-    def zeros(name, *cols):
-        return [V(vec.quantize_mx(T[name][:, a:a + 128], T[name + "s"][:, a:a + 128], T.zt[:])) for a in cols]
-    pads0 = ([48] if right is None else []) + [224 if left is not None else 176]
-    pads = ([48] if left is None else []) + [224 if right is not None else 176]
-    kb = lambda t: V(vec.memset(T.kb[0:32, t:t + 1], 130.0 * HALF[t] - 0.125))
-    vnh = V(vec.memset(T.nh[0:32, :], 80.0))
-    vz = V(vec.memset(T.zt[:], 0.0))
     for t in range(3):
-        V(vec.memset(T["L%d" % t][:, 4 * r:4 * r + 4], 0.0))
-    veps = V(vec.memset(T.eps[:, 0:1], -(2.0 ** -120)))
-    W("v", vz)
-    vpad0 = zeros("N0", *pads0)
-    vpc = zeros("C2", 0, 384)
-    G(g.iota(T.pi[:], [[0, 31]], 0, 1))
-    gj = G(g.iota(T.j0[:], [[16, 31]], 0, 0, allow_small_or_imprecise_dtypes=True))
-    G(g.iota(T.B0[:, 0:1], [[0, 1]], 0, 256, allow_small_or_imprecise_dtypes=True))
-    for k, b0 in enumerate((-160, -240, 16)):
-        G(g.iota(T.gi[:, k:k + 1], [[0, 1]], b0, 2, allow_small_or_imprecise_dtypes=True))
-    W("g", vnh)
-    gk = G(g.affine_select(T.nha[0:32, :], T.nh[0:32, :], [[0, 32]], Op.is_ge, 0.0, -1, 1))
-    W("g", gk)
-    gset = G(g.affine_select(T.nhb[0:32, :], T.nha[0:32, :], [[0, 32]], Op.is_ge, 0.0, n - 1, -1))
+        for kind in "cs":
+            arrive["@%s%d" % (kind, t)] = ("n%s%d" % (kind, t), sum(len(engs(p, r)) for p in nbs(r)))
+        arrive["@l%d" % t] = ("lm%d" % t, sum(len(topo.engines(T.cores[p], T.cores[r])) for p in others))
 
-    W("v", kx0)
-    V(vec.quantize_mx(T.C0[:, 0:128], T.C0s[:, 0:128], T.xt[:, 0:512]))
-    W("v", kx1)
-    vx = V(vec.quantize_mx(T.C0[:, 128:256], T.C0s[:, 128:256], T.xt[:, 512:1024]))
-    W("v", gj)
-    vj = V(vec.tensor_scalar(T.pm[:], T.pi[:], 15, None, Op.bitwise_and))
-    W("v", ka)
-    va = V(vec.quantize_mx(T.qa[:], T.qas[:], T.at[:]))
-    W("g", vx)
-    send_ends(0, "nc", "C0", "N0", 48, (0, 128), (208, 176))
-    send_ends(0, "ns", "C0", "N0", 48, (0, 128), (208, 176))
+    def dma(name, out, in_, sem, deps=""):
+        op(name, lambda: queue[where[name]].dma_start(out, in_), deps, sem)
 
-    def cost_mm(k, name, a):
-        return P(ten.matmul_mx(bank(k, 0, 128), T[name][:, a:a + 128], T[name + "s"][:, a:a + 128], T.qa[:], T.qas[:], True, True))
+    def fill(name, ap, c, deps=""):
+        op(name, lambda: vec.memset(ap, c), deps)
 
-    junk = []
+    def iota(name, ap, pat, base, cm):
+        op(name, lambda: g.iota(ap, pat, base, cm, allow_small_or_imprecise_dtypes=True))
 
-    def count(t, piece, k, tok, a=0, b=128):
-        W("a", tok)
-        j = 128 * len(junk)
-        junk.append(j)
+    def quant(name, buf, a, b, tile, c, deps):
+        op(name, lambda: vec.quantize_mx(T[buf][:, a:b], T[buf + "s"][:, a:b], tile[:, 4 * c:4 * (c + b - a)]), deps)
+
+    def mm(name, k, sb, sa, mb, ma, m, deps):
+        op(name, lambda: ten.matmul_mx(bank(k, 0, m), T[sb][:, sa:sa + 128], T[sb + "s"][:, sa:sa + 128],
+                                       T[mb][:, ma:ma + m], T[mb + "s"][:, ma:ma + m], True, True), deps)
+
+    junk = [0]
+
+    def count(name, t, piece, k, deps):
+        j = junk[0]
+        junk[0] += 128
         c = 4 * r + piece
-        return A(act.activation(T.junk[a:b, j:j + 128], T.ps[a:b, 512 * k:512 * k + 128], Act.Sign, bias=T.eps[a:b, 0:1],
-                                accum_out=T["L%d" % t][a:b, c:c + 1]))
+        op(name, lambda: act.activation(T.junk[:, j:j + 128], bank(k, 0, 128), Act.Sign, bias=T.eps[:, 0:1],
+                                        accum_out=Lbuf(t, c, c + 1)), deps + " zeps zL%d" % t)
 
-    W("p", va, vx)
-    p0, p1 = cost_mm(4, "C0", 0), cost_mm(5, "C0", 128)
-    W("a", veps)
-    count(0, 0, 4, p0)
-    count(0, 1, 5, p1, 0, 64)
-    a1 = count(0, 2, 5, p1, 64, 128)
-    W("g", a1)
-    send_costs(0)
+    def relu(name, k, b, a, h, c, m, deps):
+        out, src = h[:, 4 * c + b:4 * (c + m):4], bank(k, a, a + m)
+        if where[name] == "a":
+            op(name, lambda: act.activation(out, src, Act.Relu, scale=0.0625), deps)
+        else:
+            op(name, lambda: vec.tensor_scalar(out, src, 0.0, 0.0625, Op.max, Op.mult), deps)
 
-    W("v", vj)
-    vj = V(vec.tensor_copy(T.pf[:], T.pm[:]))
-    vmm = V(vec.memset(T.MM[:], 0.0))
-    W("v", vj)
-    vj = V(vec.tensor_tensor(T.J[:], T.j0[:], T.pf[:], Op.add))
-    W("v", kw)
-    vw = V(vec.quantize_mx(T.qw[:], T.qws[:], T.wt[:]))
+    def pick(name, out, window, l, deps):
+        if where[name] == "a":
+            op(name, lambda: act.activation(out, window.indirect(l), Act.Copy), deps)
+        else:
+            op(name, lambda: vec.tensor_copy(out, window.indirect(l)), deps)
 
-    def w_mm(k, b, name, a, m):
-        return P(ten.matmul_mx(bank(k, 0, m), T.qw[:, 128 * b:128 * b + 128], T.qws[:, 128 * b:128 * b + 128],
-                               T[name][:, a:a + m], T[name + "s"][:, a:a + m], True, True))
+    def ts(name, out, in0, s1, s2, o0, o1, deps):
+        op(name, (lambda: vec.tensor_scalar(out, in0, s1, s2, o0, o1)) if o1 is not None else
+           (lambda: vec.tensor_scalar(out, in0, s1, None, o0)), deps)
 
-    def relu(q, out, src):
-        if q == "a":
-            return A(act.activation(out, src, Act.Relu, scale=0.0625))
-        return V(vec.tensor_scalar(out, src, 0.0, 0.0625, Op.max, Op.mult))
+    def aff(name, out, in_, scale, bias, deps):
+        if where[name] == "a":
+            op(name, lambda: act.activation(out, in_, Act.Identity, bias=bias, scale=scale), deps)
+        else:
+            op(name, lambda: vec.tensor_scalar(out, in_, scale, bias, Op.mult, Op.add), deps)
 
-    def relus(q, bs, pm, k0, h, *runs):
-        out = []
-        for b in bs:
-            W(q, pm[b])
-            for a, c, m in runs:
-                out.append(relu(q, h[:, 4 * c + b:4 * (c + m):4], bank(k0 + b, a, a + m)))
-        return out
+    def tt(name, out, a, b, o, deps):
+        op(name, lambda: vec.tensor_tensor(out, a, b, o), deps)
 
-    W("p", vx, vw)
-    pm = [w_mm(b, b, "C0", 0, 256) for b in range(4)]
-    V(vec.memset(T.z16[:], 0.0))
-    for b in range(1, n):
-        V(vec.memset(T.wq[:, b - 1:b], b / 4.0))
-    V(vec.memset(T.XX[0:32, :], 0.0))
-    own = ((0, 176, 208), (176, 0, 80))
-    rl = relus("a", (0, 2), pm, 0, T.h1, *own) + relus("v", (1, 3), pm, 0, T.h1, *own)
-    V(vec.memset(T.c130[0:32, 0:128], 0.0))
-    W("v", *rl)
-    vq1 = V(vec.quantize_mx(T.W1[:, 224:384], T.W1s[:, 224:384], T.h1[:, 896:1536]))
-    W("p", *vpad0, a1, ("nc0", n_in), ("ns0", n_in))
-    ph0 = [w_mm(4 + b, b, "N0", 128, 128) for b in range(4)]
-    W("p", vq1, *rl)
-    pc1 = cost_mm(0, "W1", 224)
+    def turn(name, out, in_, deps):
+        turns.append(name)
+        op(name, lambda: vec.transpose(out, in_), deps)
+
+    words = lambda ap: ap.bitcast(dt.uint32)
+
+    dma("lxa", T.xt[:, 512:672], T.x[:, 864:1024], "dx0")
+    dma("lxb", T.xt[:, 672:1024], T.x[:, 0:352], "dx2")
+    dma("lxr", T.xt[:, 0:512], T.x[:, 352:864], "dx1")
+    dma("la", T.at[:], T.a[:], "da")
+    for b in range(2):
+        dma("lw%d" % b, T.wt[:, 1024 * b:1024 * b + 1024], T.w[:, 1024 * b:1024 * b + 1024], "dw%d" % b)
+
+    fill("znh", T.nh[0:32, :], 80.0)
+    fill("zeps", T.eps[:, 0:1], -(2.0 ** -120))
+    for t in range(2):
+        fill("zL%d" % t, Lbuf(t, 4 * r, 4 * r + 4), 0.0)
+    fill("zLa", T.LA[:, 0:4], 0.0)
+    fill("zLb", T.LA[:, 20:172], 0.0)
+    fill("zMM", T.MM[:], 0.0)
+    fill("zXX", T.XX[0:64, :], 0.0)
+    if not (left and right):
+        fill("zh1", T.h1[:, 480:640] if left else T.h1[:, 640:800], 0.0)
+    fill("zhh", T.hh2[:, 320:512] if left and right else T.hh2[:], 0.0)
+    fill("zRWb", T.RA[0:32, 32:192], 130.0)
+    for t in range(2):
+        fill("zkb%d" % t, T.kb[0:32, t:t + 1], 130.0 * HALF[t] - 0.125)
+    fill("zBh", T.Bh[0:32, :], 0.0)
+    fill("zHM", T.HM[:], 1.0)
+    for k, c in enumerate((0.0, -1.0 / BIG, BIG)):
+        fill("zHM%d" % k, T.HM[:, k:186:6], c, "zHM")
+    fill("zMK", T.MK1[:], 1.0)
+    op("ipi", lambda: g.iota(T.pi[:, 0:1], [[0, 1]], 0, 1))
+    iota("iN", T.K[:, 0:60], [[-32, 60]], 512, 0)
+    for k, (a, b, c) in enumerate(((0, 5, 200), (5, 10, -40), (10, 13, -112 if right else 88), (13, 16, 368 if left else 72))):
+        iota("iM%d" % k, T.K[:, 60 + a:60 + b], [[-32, b - a]], -2 * (c + 16 * a), 0)
+    iota("igi", T.gi[:, 0:7], [[-16, 7]], -80, 2)
+    fill("zgi", T.gi[0:48, 6:7], 10000.0, "igi")
+    fill("zgj", T.gi[0:32, 4:5], 10000.0, "igi")
+    iota("iwq", T.wq[:, 0:3], [[1, 3]], 1, 0)
+    iota("iB0", T.B0[:, 0:1], [[0, 1]], 0, 256)
+    iota("icp0", T.cp[:, 0:2], [[704, 2]], 80, 0)
+    iota("icp1", T.cp[:, 2:4], [[192, 2]], 592, 0)
+    op("sel0", lambda: g.affine_select(T.nha[0:32, :], T.nh[0:32, :], [[0, 32]], Op.is_ge, 0.0, -1, 1), "znh")
+    op("sel1", lambda: g.affine_select(T.nhb[0:32, :], T.nha[0:32, :], [[0, 32]], Op.is_ge, 0.0, n - 1, -1), "sel0")
+    ts("pand", T.pm[:, 0:1], T.pi[:, 0:1], 15, None, Op.bitwise_and, None, "ipi")
+    ts("pcopy", T.pf[:, 0:1], T.pm[:, 0:1], -2.0, None, Op.mult, None, "pand")
+    aff("KK", T.KK[:], T.K[:], 1.0, T.pf[:, 0:1], "pcopy iN" + rng("iM%d"))
+    ts("lo0", T.hi[0:32, 0:1], T.nhb[0:32, 0:1], -1.0, None, Op.mult, None, "sel1")
+
+    quant("qE", "C0", 128, 256, T.xt, 128, "lxa lxb")
+    quant("qR", "C0", 0, 128, T.xt, 0, "lxr")
+    quant("qD", "C0", 256, 384, T.xt, 0, "lxr")
+    quant("qa", "qa", 0, 128, T.at, 0, "la")
+    ends(0, "C0", 40, ((168, 384), (128, 424 if r + 2 < n else 384)), "qE", "qE")
+    mm("mE", 4, "C0", 104, "qa", 0, 128, "qE qR qa")
+    mm("mM", 5, "C0", 232, "qa", 0, 128, "qE qD qa")
+    count("c00", 0, 1, 4, "mE")
+    count("c01", 0, 0, 5, "mM")
+    op("sl0", lambda: send_costs(0), "c00 c01")
+    ha, hc, hm = (336, 120, 80) if left and right else (296, 160 if left else 120, 40)
+    for b in range(4):
+        quant("qw%d" % b, "qw", 128 * b, 128 * b + 128, T.wt, 128 * b, "lw%d" % (b // 2))
+        mm("o%d" % b, b, "qw", 128 * b, "C0", 48, 336, "qE qR qD qw%d" % b)
+        relu("ro%da" % b, b, b, 120, T.h1, 200, 216, "o%d" % b)
+        relu("ro%db" % b, b, b, 0, T.h1, 0, 120, "o%d" % b)
+        mm("h%d" % b, 4 + b, "qw", 128 * b, "C0", ha, 128, "qD qw%d @c0 @s0 c00 c01" % b)
+        relu("rh%d" % b, 4 + b, b, 128 - hm, T.h1, hc, hm, "h%d" % b)
+    quant("q1a", "W1", 328, 544, T.h1, 200, rng("ro%da"))
+    quant("q1b", "W1", 128, 328, T.h1, 0, rng("ro%db") + rng("rh%d") + "zh1")
+    ends(1, "W1", 120, ((288, 8), (168, 544)), "q1a q1b", "q1a q1b")
+    mm("k11", 4, "W1", 376, "qa", 0, 128, "q1a rh0")
+    mm("k10", 5, "W1", 248, "qa", 0, 128, "q1a q1b")
+    mm("k12", 6, "W1", 168, "qa", 0, 128, "q1b")
+    for k, b in ((0, 5), (1, 4), (2, 6)):
+        count("c1%d" % k, 1, k, b, "k1%d" % k)
+    op("sl1", lambda: send_costs(1), "c10 c11 c12")
 
     BO = lambda t, a, b: T.BBB[:, 32 * t + a:32 * t + b]
-
-    def b_mask(t, *toks):
-        W("v", ("lm%d" % t, l_in), *toks)
-        return V(vec.tensor_tensor(T.LM[:, 16 * t:16 * t + 16], T["L%d" % t][:], T["MK%d" % t][:], Op.mult))
-
-    def b_ps(t, *toks):
-        W("v", *toks)
-        src = T.LM[:, 16 * t:16 * t + 16] if t else T.L0[:]
-        return V(vec.tensor_tensor_scan(T.PS[:, 16 * t:16 * t + 16], src, T.z16[:], 0.0, Op.add, Op.add))
-
-    def b_x(t):
-        m, mo = 16 * t, 96 * t
-        v = V(vec.tensor_tensor(T.MM[:, mo + 33:mo + 36], T.LM[:, m + 2:m + 11:4], T.LM[:, m + 4:m + 13:4], Op.add))
-        if t == 1:
-            return V(vec.tensor_copy(T.MM[0:32, mo + 65:mo + 68], T.L1[0:32, 5:14:4]))
-        return V(vec.tensor_tensor(T.MM[:, mo + 65:mo + 68], T.LM[:, m + 3:m + 12:4], T.LM[:, m + 5:m + 14:4], Op.add))
-
-    def b_share(t, v):
-        W("v", v)
-        return V(vec.tensor_scalar(T.TW[:, 4 * t:4 * t + 3], T.wq[:, 0:3], T.PS[:, 16 * t + 15:16 * t + 16], None, Op.mult))
-
-    def b_sub(t, v):
-        W("v", v)
-        return V(vec.tensor_tensor(T.MM[:, 96 * t + 1:96 * t + 4], T.PS[:, 16 * t + 1:16 * t + 10:4], T.TW[:, 4 * t:4 * t + 3],
-                                   Op.subtract))
-
-    def b_tq(t, vq):
-        mo = 96 * t
-        W("v", vq)
+    XX = lambda t, m=32, p=5: T.XX[0:p, 32 * t:32 * t + m]
+    XB = lambda t: T.XX[32:37, 32 * t:32 * t + 32]
+    tb = lambda t: rng("tb%d%%d" % t, 2)
+    for t in range(3):
+        s, lm, Zh = str(t), 4 + 20 * t, T["Zh%d" % t]
+        LM = lambda a, b, c=1, p=0, q=128, lm=lm: T.LA[p:q, lm + a:lm + b:c]
+        have = "@l0 c00 c01 zLa zLb" if t == 0 else "mask" + s
+        if t:
+            tt("mask" + s, LM(0, 16), T["L" + s][:], T["MK" + s][:], Op.mult,
+               "@l%d zLb " % t + ("c10 c11 c12 mk10 mk12" if t == 1 else rng("c2%d") + rng("mk2%d")))
+        op("ps" + s, lambda t=t, LM=LM: vec.tensor_tensor_scan(T.PS[0:64, 16 * t:16 * t + 16],
+                                                               LM(0, 16, 1, 0, 64) if t else LM(-1, 15, 1, 0, 64), LM(0, 16, 1, 64, 128),
+                                                               0.0, Op.add, Op.add), have)
+        ts("sh" + s, T.TW[0:64, 4 * t:4 * t + 3], T.wq[0:64, 0:3], T.PS[0:64, 16 * t + 15:16 * t + 16], 0.25, Op.mult, Op.mult, "iwq ps" + s)
+        k = 16 * t + (2 if t == 2 else 1)
+        tt("sub" + s, T.MM[0:64, 32 * t + 1:32 * t + 4], T.PS[0:64, k:k + 9:4], T.TW[0:64, 4 * t:4 * t + 3], Op.subtract, "zMM sh" + s)
+        if t:
+            tt("x" + s, T.MM[:, 65 + 32 * t:68 + 32 * t], LM(1 + t, 10 + t, 4), LM(4, 13, 4), Op.add, "zMM mask" + s)
+            turn("tz%d4" % t, Zh[0:32, 160:192], LM(1, 126, 4, 0, 32), "mask" + s)
         for k in range(4):
-            v = V(vec.transpose(T["Zh%d" % t][0:32, 32 * k:32 * k + 32], T.MM[32 * k:32 * k + 32, mo:mo + 32]))
-        return v
-
-    def b_tx(t, vxx, half):
-        mo, Zh = 96 * t + 32, T["Zh%d" % t]
-        W("v", vxx)
-        if half == 0:
-            for k in range(4):
-                z = 4 + (k if t else (k + 2) % 4)
-                v = V(vec.transpose(Zh[0:32, 32 * z:32 * z + 32], T.MM[32 * k:32 * k + 32, mo:mo + 32]))
-        else:
-            for k in range((0, 1, 4)[t]):
-                v = V(vec.transpose(Zh[0:32, 256 + 32 * k:288 + 32 * k], T.MM[32 * k:32 * k + 32, mo + 32:mo + 64]))
-        return v
-
-    def b_scan(t, v):
-        h = 128 + HALF[t] + MOVE[t]
-        W("v", v)
-        return V(vec.tensor_tensor_scan(T["Ih%d" % t][0:5, 0:h], T["Zh%d" % t][0:5, 0:h], T.c130[0:5, 0:h], 0.0, Op.add, Op.add))
-
-    def b_sign(t, v):
-        a, w = 127 + HALF[t] - MOVE[t], 2 * MOVE[t]
-        W("a", v)
-        return A(act.activation(T.rjunk[0:5, 512 * t + 128:512 * t + 128 + w], T["Ih%d" % t][0:5, a:a + w], Act.Sign,
-                                bias=T.kb[0:5, t:t + 1], scale=-1.0, accum_out=T.row[0:5, t:t + 1]))
-
-    xx = {}
-
-    def b_clamp(t, av, fill):
-        W("v", av)
-        v = xx[t] = V(vec.tensor_scalar(T.XX[0:5, 32 * t:32 * t + 32], T.lo[0:5, 32 * t:32 * t + 32], T.row[0:5, t:t + 1],
-                                        T.hi[0:5, t:t + 1], Op.max, Op.min))
-        fill()
-        W("v", v)
-        for k in range(4):
-            v = V(vec.transpose(T.BBB[32 * k:32 * k + 32, 32 * t:32 * t + 32], T.XX[0:32, 32 * t:32 * t + 32]))
-        return v
-
-    def b_range(t):
-        V(vec.tensor_tensor(T.lo[0:5, 32 * t + 32:32 * t + 64], T.XX[0:5, 32 * t:32 * t + 32], T.nhb[0:5, :], Op.subtract))
-        return V(vec.tensor_tensor(T.hi[0:5, t + 1:t + 2], T.XX[0:5, 32 * t:32 * t + 1], T.nhb[0:5, 0:1], Op.add))
-
-    def masks(t, cols):
-        MK = T["MK%d" % t]
-        for p, gc, is_left in cols:
-            if is_left:
-                v = V(vec.tensor_scalar(MK[:, p:16:4], BO(t - 1, 0, 4), T.gi[:, gc:gc + 1], None, Op.is_le))
+            p, q = 32 * k, 32 * k + 32
+            if k < 2:
+                turn("tl%d%d" % (t, k), (T.RA if k else Zh)[0:32, 0:32], T.MM[p:q, 32 * t:32 * t + 32],
+                     "sub%d %s" % (t, "scan%d" % (t - 1) if t else ""))
+                turn("tb%d%d" % (t, k), T.BBB[2 * p:2 * q, 32 * t:32 * t + 32], XX(3 if t == 1 else t, 32, 64),
+                     "xd xdb" if t == 1 else "clamp%d clamp%db" % (t, t))
+            if t == 0:
+                a = -3 if k < 2 else 1
+                turn("tz0%d" % k, Zh[0:32, 32 + p:32 + q], LM(a, a + 125, 4, p, q), have)
             else:
-                v = V(vec.tensor_scalar(MK[:, p:16:4], BO(t - 1, 1, 5), T.gi[:, gc:gc + 1], None, Op.is_gt))
-        return v
+                turn("tz%d%d" % (t, k), Zh[0:32, 32 + p:32 + q], T.MM[p:q, 64 + 32 * t:96 + 32 * t], "x" + s)
+        h, a, w = 32 + HALF[t] + MOVE[t], 31 + HALF[t] - MOVE[t], 2 * MOVE[t]
+        op("scan" + s, lambda Zh=Zh, h=h: vec.tensor_tensor_scan(T.Ih[0:5, 0:h], Zh[0:5, 0:h], T.RA[0:5, 0:h], 0.0, Op.add, Op.add),
+           "zRWb" + rng("tl%d%%d" % t, 2) + rng("tz%d%%d" % t, 5 if t else 4) + ("sign%d" % (t - 1) if t else ""))
+        op("sign" + s, lambda t=t, a=a, w=w: act.activation(T.rjunk[0:5, 160 * t:160 * t + w], T.Ih[0:5, a:a + w], Act.Sign,
+                                                            bias=T.kb[0:5, t:t + 1], scale=-1.0, accum_out=T.row[0:5, t:t + 1]),
+           "scan%d %s" % (t, ("zkb0", "zkb1", "kb2")[t]))
+    for b, X in (("", XX), ("b", XB)):
+        ts("clamp0" + b, X(0), T.nhb[0:5, :], T.row[0:5, 0:1], T.hi[0:5, 0:1], Op.min, Op.max, "zXX sign0 lo0")
+        ts("xd" + b, X(3), XX(1), T.hi[0:5, 0:1], -1.0, Op.max, Op.mult, "clamp1")
+        ts("clamp2" + b, X(2), T.lo[0:5, 0:32], T.row[0:5, 2:3], T.hi[0:5, 2:3], Op.max, Op.min, "sign2 lo2 hi2")
+    ts("clamp1", XX(1), XX(0), T.row[0:5, 1:2], T.nhb[0:5, 0:1], Op.subtract, Op.min, "clamp0 sign1")
+    aff("lo2", T.lo[0:5, 0:32], XX(3), 1.0, T.hi[0:5, 0:1], "xd")
+    aff("hi2", T.hi[0:5, 2:3], XX(3, 1), 1.0, T.nhb[0:5, 0:1], "xd")
+    aff("kb2", T.kb[0:5, 2:3], XX(0, 1), -65.0, 130.0 * HALF[2] - 0.125, "clamp0")
+    for name, MK, p, t, gc in (("mk10", T.MK1, 0, 0, 5), ("mk12", T.MK1, 2, 0, 5), ("mk20", T.MK2, 0, 1, 5), ("mk21", T.MK2, 1, 0, 4),
+                               ("mk22", T.MK2, 2, 0, 6), ("mk23", T.MK2, 3, 1, 5)):
+        if p < 2:
+            ts(name, MK[:, p:16:4], BO(t, 0, 4), T.gi[:, gc:gc + 1], None, Op.is_le, None, "igi zgj zMK" + tb(t))
+        else:
+            ts(name, MK[:, p:16:4], BO(t, 1, 5), T.gi[:, gc:gc + 1], None, Op.is_gt, None, "igi zgi zMK" + tb(t))
 
-    lm0 = ("lm0", l_in)
-    halo = ((0, 80, 96),)
-    hr = relus("a", (0, 2), ph0, 4, T.h1, *halo) + relus("v", (1, 3), ph0, 4, T.h1, *halo)
-    kb(0)
-    W("v", *hr, *rl)
-    vp2 = V(vec.quantize_mx(T.W1[:, 0:224], T.W1s[:, 0:224], T.h1[:, 0:896]))
-    W("g", vp2)
-    send_ends(1, "nc", "W1", "W1", 120, (136, 512), (0, 384))
-    send_ends(1, "ns", "W1", "W1", 120, (136, 512), (0, 384))
-    W("p", vp2)
-    pc0 = cost_mm(1, "W1", 96)
-    pc2 = cost_mm(2, "W1", 0)
-    ac1 = count(1, 1, 0, pc1)
-    ac0 = count(1, 0, 1, pc0)
-    ac2 = count(1, 2, 2, pc2)
-    W("g", ac0, ac1, ac2)
-    send_costs(1)
-    vps = b_ps(0, lm0, a1, vmm)
-    V(vec.tensor_copy(T.MM[64:128, 33:36], T.L0[64:128, 2:11:4]))
-    vsh = b_share(0, vps)
-    ax = V(vec.tensor_copy(T.MM[0:64, 33:36], T.L0[0:64, 4:13:4]))
-    vq = b_sub(0, vsh)
-    V(vec.memset(T.c130[0:32, 128:232], 130.0))
-    b_tx(0, ax, 0)
-    vt = b_tq(0, vq)
-    W("v", gset, vj)
-    V(vec.tensor_scalar(T.lo[0:32, 0:32], T.nhb[0:32, :], -1.0, None, Op.mult))
-    vs = b_scan(0, vt)
-    av = b_sign(0, vs)
-    vhi = V(vec.tensor_copy(T.hi[0:32, 0:1], T.nhb[0:32, 0:1]))
-    V(vec.tensor_scalar(T.JL[:], T.J[:, 0:8], 2.0, -160.0, Op.mult, Op.add))
-    V(vec.tensor_scalar(T.JR[:], T.J[:, 0:8], 2.0, -96.0, Op.mult, Op.add))
-    V(vec.tensor_scalar(T.Jm[:, 0:8], T.J[:, 0:8], 96.0, None, Op.add))
-    vj = V(vec.tensor_scalar(T.Jm[:, 8:16], T.J[:, 0:8], 32.0, None, Op.add))
-    W("p", *rl, ac0, ac1, ac2)
-    pm = [w_mm(b, b, "W1", 224, 160) for b in range(4)]
-    rm = relus("a", (0, 1, 2, 3), pm, 0, T.m2, (0, 168, 160))
-    W("v", vhi)
-    vB = b_clamp(0, av, lambda: V(vec.memset(T.MK1[:], 1.0)))
-    kb(1)
-    W("v", vB, vj)
-    V(vec.tensor_scalar(T.t1[:, 0:8], T.JL[:], BO(0, r, r + 1), 288.0, Op.is_lt, Op.mult))
-    vl = V(vec.tensor_scalar(T.t1[:, 8:16], T.JR[:], BO(0, r + 1, r + 2), 472.0, Op.is_ge, Op.mult))
-    masks(1, ((0, 0, True),))
-    W("v", vl)
-    vl = V(vec.tensor_tensor(T.t2[:], T.t1[:], T.Jm[:], Op.add))
-    mk1 = masks(1, ((2, 0, False),))
-    W("v", vl)
-    vl = V(vec.tensor_copy(T.la[:], T.t2[:]))
-    vpad1 = zeros("W1", *(([384] if left is None else []) + ([512] if right is None else [])))
-    b_range(0)
+    for k, (a, b, j) in enumerate(((0, 5, 0), (5, 13, 1), (13, 16, 0))):
+        ts("lM%d" % k, T.la[:, a:b], T.KK[:, 60 + a:60 + b], BO(0, r + j, r + j + 1), -0.5, Op.subtract, Op.mult, "KK" + tb(0))
+    pick("pM0", words(T.M1[:, 0:160]), words(T.W1[:, 128:544]), T.la[:, 0:10], "q1a q1b lM0 lM1")
+    pick("pMs0", T.M1s[:, 0:160], T.W1s[:, 128:544], T.la[:, 0:10], "q1a q1b lM0 lM1")
+    pick("pM1", words(T.M1[:, 160:256]), words(T.W1[:, 0:664]), T.la[:, 10:16], "q1a q1b @c1 lM1 lM2")
+    pick("pMs1", T.M1s[:, 160:256], T.W1s[:, 0:664], T.la[:, 10:16], "q1a q1b @s1 lM1 lM2")
+    for b in range(4):
+        mm("d%d" % b, b, "qw", 128 * b, "W1", 368, 176, "q1a ro%db" % b)
+        relu("rd%d" % b, b, b, 0, T.m2, 256, 176, "d%d" % b)
+        mm("L%d" % b, 4 + b, "qw", 128 * b, "M1", 0, 160, "pM0 pMs0 " + ("c22", "c10", "c12", "rh3")[b])
+        relu("ro%da" % (4 + b), 4 + b, b, 0, T.m2, 176, 80, "L%d" % b)
+        relu("ro%db" % (4 + b), 4 + b, b, 80, T.m2, 0, 80, "L%d" % b)
+        mm("R%d" % b, b, "qw", 128 * b, "M1", 128, 128, "pM0 pMs0 pM1 pMs1 rd%d" % b)
+        relu("rR%d" % b, b, b, 32, T.m2, 80, 96, "R%d" % b)
+    quant("q2m", "C2", 264, 440, T.m2, 256, rng("rd%d"))
+    quant("q2L", "C2", 232, 360, T.m2, 224, "q2m k22 ro4a ro5a ro6a ro7a")
+    quant("q2R", "C2", 8, 232, T.m2, 0, rng("rR%d") + "ro4a ro5a ro6a ro7a ro4b ro5b ro6b ro7b")
+    mm("k21", 7, "C2", 232, "qa", 0, 128, "q2m q2L ro7b")
+    mm("k22", 4, "C2", 312, "qa", 0, 128, "q2m c11")
+    mm("k20", 4, "C2", 104, "qa", 0, 128, "q2R")
+    mm("k23", 0, "C2", 8, "qa", 0, 128, "q2R")
+    count("c21", 2, 1, 7, "k21")
+    count("c22", 2, 2, 4, "k22")
+    count("c20", 2, 0, 4, "k20")
+    count("c23", 2, 3, 0, "k23")
+    op("sl2", lambda: send_costs(2), rng("c2%d"))
+    for k, c in ((0, 27), (1, 19)):
+        ts("lH%d" % k, T.lb[:, 3 * k:3 * k + 3], T.KK[:, c:c + 3], BO(1, r + k, r + k + 1), -0.5, Op.subtract, Op.mult, "KK" + tb(1))
+    pick("pH", words(T.H2[:, 0:96]), words(T.C2[:, 0:264]), T.lb[:, 0:6], "q2L q2R lH0 lH1")
+    pick("pHs", T.H2s[:, 0:96], T.C2s[:, 0:264], T.lb[:, 0:6], "q2L q2R lH0 lH1")
+    ends(2, "H2", 40, ((8, 136 if r > 1 else 96), (48, 96)), "pH", "pHs")
 
-    vpk, apk = [], []
-    W("v", vl, vp2, vq1, *vpad1, ("nc1", n_in))
-    W("a", vl, vp2, vq1, *vpad1, ("ns1", n_in))
-    for k in (0, 1):
-        s = slice(128 * k, 128 * k + 128)
-        l = T.la[:, 8 * k:8 * k + 8]
-        vpk.append(V(vec.tensor_copy(T.M1[:, s].bitcast(dt.uint32), T.W1[:, 0:640].bitcast(dt.uint32).indirect(l))))
-        apk.append(A(act.activation(T.M1s[:, s], T.W1s[:, 0:640].indirect(l), Act.Copy)))
-    W("p", vpk[0], apk[0], *hr)
-    pL = [w_mm(4 + b, b, "M1", 0, 128) for b in range(4)]
-    W("p", vpk[1], apk[1], *rm)
-    pR = [w_mm(b, b, "M1", 128, 128) for b in range(4)]
-    W("v", *rm, *vpc)
-    V(vec.quantize_mx(T.C2[:, 168:328], T.C2s[:, 168:328], T.m2[:, 672:1312]))
-    V(vec.memset(T.c130[0:32, 232:368], 130.0))
-    rL = relus("a", (0, 2), pL, 4, T.m2, (0, 40, 128)) + relus("v", (1, 3), pL, 4, T.m2, (0, 40, 128))
-    rR = relus("a", (0, 1, 2, 3), pR, 0, T.m2, (0, 328, 128))
-    vm = b_mask(1, mk1, ac0, ac1, ac2)
-    W("v", *rL)
-    vc0 = V(vec.quantize_mx(T.C2[:, 40:168], T.C2s[:, 40:168], T.m2[:, 160:672]))
-    vps = b_ps(1, vm)
-    vxx = b_x(1)
-    vsh = b_share(1, vps)
-    b_tx(1, vxx, 0)
-    vq = b_sub(1, vsh)
-    W("v", *rR)
-    vc1 = V(vec.quantize_mx(T.C2[:, 328:456], T.C2s[:, 328:456], T.m2[:, 1312:1824]))
-    b_tx(1, vxx, 1)
-    vt = b_tq(1, vq)
-    W("p", vc0, *rL)
-    pc = [cost_mm(4, "C2", 0), cost_mm(5, "C2", 128)]
-    W("p", vc1)
-    pc += [cost_mm(6, "C2", 256), cost_mm(7, "C2", 384)]
-    ac = [count(2, k, 4 + k, pc[k]) for k in range(4)]
-    W("g", *ac)
-    send_costs(2)
-    kb(2)
-    vs = b_scan(1, vt)
-    av = b_sign(1, vs)
-    W("p", *rR)
-    pm = [w_mm(b, b, "C2", 40, 416) for b in range(4)]
-    ro = relus("a", (0,), pm, 0, T.m3, (0, 0, 416))
-    V(vec.tensor_scalar(T.J8[:, 0:4], T.J[:, 0:4], 2.0, 240.0, Op.mult, Op.add))
-    vj = V(vec.tensor_scalar(T.J8[:, 4:8], T.J[:, 0:4], 2.0, 624.0, Op.mult, Op.add))
-    vpad2 = zeros("N2", *pads)
-    V(vec.tensor_scalar(T.J2m[:], T.J[:], 2.0, -512.0, Op.mult, Op.add))
-    vB = b_clamp(1, av, lambda: V(vec.tensor_scalar(T.J2[:], T.J[:], 2.0, 160.0, Op.mult, Op.add)))
-    vhz = V(vec.memset(T.hh2[:, 320:512], 0.0))
-    W("v", vB, vj)
-    V(vec.tensor_scalar(T.lb[:, 0:4], T.J8[:, 0:4], BO(1, r, r + 1), 0.5, Op.add, Op.mult))
-    vl = V(vec.tensor_scalar(T.lb[:, 4:8], T.J8[:, 4:8], BO(1, r + 1, r + 2), 0.5, Op.add, Op.mult))
-    masks(2, ((0, 1, True),))
-    W("v", vl)
-    vh = V(vec.tensor_copy(T.H2[:].bitcast(dt.uint32), T.C2[:, 0:512].bitcast(dt.uint32).indirect(T.lb[:, 0:8])))
-    mk2 = masks(2, ((1, 2, True), (2, 1, False), (3, 2, False)))
-    V(vec.tensor_scalar(T.kk[:, 0:1], BO(1, r, r + 1), -0.5 / SC, 376.0 / SC, Op.mult, Op.add))
-    W("v", mk2)
-    vm = b_mask(2, *ac)
-    W("a", vl, vc1)
-    ah = A(act.activation(T.H2s[:], T.C2s[:, 0:512].indirect(T.lb[:, 0:8]), Act.Copy))
-    W("g", vh)
-    send_ends(2, "nc", "H2", "N2", 48, (0, 176), (80, 128))
-    W("g", ah)
-    send_ends(2, "ns", "H2", "N2", 48, (0, 176), (80, 128))
-    ro += relus("a", (1, 2, 3), pm, 0, T.m3, (0, 0, 416))
+    na, nc, nm = (48, 0, 80) if left and right else (8, 0 if left else 40, 40)
+    for b in range(4):
+        k = (5, 6, 7, 1)[b]
+        mm("f%d" % b, k, "qw", 128 * b, "C2", 8, 432, "q2m q2L q2R " + ("c21" if k == 7 else ""))
+        relu("rf%d" % b, k, b, 0, T.m3, 0, 432, "f%d" % b)
+        k = (4, 0, 2, 3)[b]
+        mm("n%d" % b, k, "qw", 128 * b, "H2", na, 128, "pH pHs @c2 @s2 c20 c23")
+        relu("rn%d" % b, k, b, 128 - nm, T.hh2, nc, nm, "zhh n%d" % b)
+    quant("q3w", "C3", 0, 432, T.m3, 0, rng("rf%d"))
+    quant("q3h", "C3", 432, 560, T.hh2, 0, "zhh" + rng("rn%d"))
+    tt("c23c", T.cc[:, 0:2], BO(0, r, r + 2), T.cp[:, 0:2], Op.add, "icp0" + tb(0))
+    tt("c14c", T.cc[:, 2:4], T.cp[:, 2:4], BO(1, r, r + 2), Op.subtract, "icp1" + tb(1))
+    ts("th35", T.th[:, 0:36], T.KK[:, 0:36], BO(0, r + 1, r + 2), BO(0, r, r + 1), Op.add, Op.subtract, "KK" + tb(0))
+    aff("th1", T.th[:, 36:67], T.KK[:, 16:47], 1.0, BO(1, r, r + 1), "KK" + tb(1))
+    aff("th4", T.th[:, 68:99], T.th[:, 0:31], 1.0, BO(1, r + 1, r + 2), "th35" + tb(1))
+    e, TM = BO(2, r, r + 1), lambda k: T.TM[:, k:186:6]
+    ts("t3", TM(0), T.th[:, 5:36], e, T.cc[:, 1:2], Op.is_le, Op.mult, "th35 c23c" + tb(2))
+    ts("tend", TM(1), T.th[:, 0:31], BO(2, r + 1, r + 2), e, Op.add, Op.is_le, "th35" + tb(2))
+    aff("tbase", TM(2), T.KK[:, 27:58], -1.0, e, "KK" + tb(2))
+    ts("t1", TM(3), T.th[:, 36:67], e, T.cc[:, 2:3], Op.is_gt, Op.mult, "th1 c14c" + tb(2))
+    ts("t2", TM(4), T.KK[:, 11:42], e, T.cc[:, 0:1], Op.is_le, Op.mult, "KK c23c" + tb(2))
+    ts("t4", TM(5), T.th[:, 68:99], e, T.cc[:, 3:4], Op.is_le, Op.mult, "th4 c14c" + tb(2))
+    op("sum", lambda: vec.tensor_tensor_scan(T.SM[:, 0:186], T.HM[:, 0:186], T.TM[:, 0:186], 0.0, Op.mult, Op.add),
+       "t1 t2 t3 t4 tend tbase" + rng("zHM%d", 3))
+    ts("lF", T.lf[:, 0:31], T.SM[:, 5:186:6], 0.5, 520.0, Op.mult, Op.min, "sum")
+    aff("bh0", T.Bh[0:5, 0:1], XX(0, 1), 0.5, T.B0[0:5, 0:1], "zBh iB0 clamp0")
+    aff("bh1", T.Bh[0:5, 1:2], XX(3, 1), 0.5, T.Bh[0:5, 0:1], "bh0 xd")
+    aff("bh2", T.Bh[0:5, 2:3], XX(2, 1), 0.5, T.Bh[0:5, 0:1], "bh0 clamp2")
+    turn("tbd", T.Ball[0:32, :], T.Bh[0:32, :], "bh1 bh2")
 
-    V(vec.tensor_scalar(T.kk[:, 1:2], BO(1, r + 1, r + 2), -0.5 / SC, 120.0 / SC, Op.mult, Op.add))
-    vps = b_ps(2, vm)
-    vxx = b_x(2)
-    vsh = b_share(2, vps)
-    b_tx(2, vxx, 0)
-    vq = b_sub(2, vsh)
-    b_tx(2, vxx, 1)
-    vt = b_tq(2, vq)
-    b_range(1)
-    vs = b_scan(2, vt)
-    av = b_sign(2, vs)
-    W("v", *ro)
-    vc3 = V(vec.quantize_mx(T.C3[:, 0:416], T.C3s[:, 0:416], T.m3[:]))
-    V(vec.tensor_scalar(T.J2n[:, 0:31], T.J[:], -2.0, BO(1, r, r + 1), Op.mult, Op.add))
-    W("p", *vpad2, *ac, ("nc2", n_in), ("ns2", n_in))
-    ph = [w_mm(4 + b, b, "N2", 128, 128) for b in range(4)]
-    W("p", vc3, *ro)
-    py = P(ten.matmul_mx(bank(0, 0, 416), T.qa[:], T.qas[:], T.C3[:, 0:416], T.C3s[:, 0:416], True, True))
-    vB = b_clamp(2, av, lambda: V(vec.tensor_scalar(T.J2n[:, 31:62], T.J2m[:], -1.0, BO(1, r + 1, r + 2), Op.mult, Op.add)))
-    vbz = V(vec.memset(T.Bh[0:32, :], 0.0))
-    h2 = relus("a", (0, 1, 2, 3), ph, 4, T.hh2, (8, 0, 80))
-    W("a", py)
-    A(act.activation(T.YC[:, 0:416], bank(0, 0, 416), Act.Copy))
-    W("v", vB)
-    d2 = BO(2, r, r + 1)
-    V(vec.tensor_scalar(T.terms[:, 0:31], T.J2[:], d2, 0.5 / SC, Op.add, Op.mult))
-    V(vec.tensor_scalar(T.terms[:, 31:62], T.J2n[:, 0:31], d2, T.kk[:, 0:1], Op.is_gt, Op.mult))
-    V(vec.tensor_scalar(T.terms[:, 62:93], T.J2n[:, 31:62], d2, T.kk[:, 1:2], Op.is_le, Op.mult))
-    vu = V(vec.tensor_scalar(T.terms[:, 93:124], T.J2m[:], d2, BO(2, r + 1, r + 2), Op.add, Op.is_ge))
-    W("v", vbz)
-    vb = V(vec.tensor_scalar(T.Bh[0:5, 0:3], T.XX[0:5, 0:96:32], 0.5, T.B0[0:5, 0:1], Op.mult, Op.add))
-    W("v", vu)
-    vu = V(vec.tensor_tensor(T.sum3[:, 0:62], T.terms[:, 0:62], T.terms[:, 62:124], Op.add))
-    W("v", vhz, *h2)
-    vch = V(vec.quantize_mx(T.C3[:, 416:544], T.C3s[:, 416:544], T.hh2[:]))
-    W("v", vu)
-    vu = V(vec.tensor_tensor(T.sum1[:, 0:31], T.sum3[:, 0:31], T.sum3[:, 31:62], Op.add))
-    vN = V(vec.transpose(T.Ball[0:32, :], T.Bh[0:32, :]))
-    W("v", vu)
-    vl = V(vec.tensor_scalar(T.lf[:, 0:31], T.sum1[:, 0:31], SC, 500.0, Op.mult, Op.min))
-    W("p", vch)
-    pz = P(ten.matmul_mx(bank(1, 0, 128), T.qa[:], T.qas[:], T.C3[:, 416:544], T.C3s[:, 416:544], True, True))
-    W("a", pz)
-    yc = A(act.activation(T.YC[:, 416:544], bank(1, 0, 128), Act.Copy))
-
-    W("v", vl, vch, vc3)
-    W("a", vl, vch, vc3, yc)
-    halves = ((0, 256), (256, 496))
-    vf, af = [], []
-    for a, b in halves:
+    dma("sbd", T.bd[:], T.Ball[0:3, 0:5], "dout", "tbd")
+    for k, (a, b) in enumerate(CUTS):
         l = T.lf[:, a // 16:b // 16]
-        vf.append(V(vec.tensor_copy(T.F[:, a:b].bitcast(dt.uint32), T.C3[:, 0:544].bitcast(dt.uint32).indirect(l))))
-        af.append(A(act.activation(T.yt[:, a:b], T.YC[:, 0:544].indirect(l), Act.Copy)))
-    vs0 = V(vec.tensor_copy(T.Fs[:, 0:352], T.C3s[:, 0:544].indirect(T.lf[:, 0:22])))
-    as1 = A(act.activation(T.Fs[:, 352:496], T.C3s[:, 0:544].indirect(T.lf[:, 22:31]), Act.Copy))
-    W("s", vN)
-    inc("dout", g.sync.dma_start(T.bd[:], T.Ball[0:3, 0:5]), 16)
-    for k, (a, b) in enumerate(halves):
-        W("s", vf[k])
-        inc("dout", g.sync.dma_start(T.oc[:, 4 * a:4 * b], T.F[:, a:b].bitcast(dt.uint8)), 16)
-        W("s", af[k])
-        inc("dout", g.sync.dma_start(T.y[:, a:b], T.yt[:, a:b]), 16)
-    W("s", vs0, as1)
-    W("a", vs0, as1)
+        pick("pF%d" % k, words(T.F[:, a:b]), words(T.C3[:, 0:560]), l, "lF q3w q3h")
+        pick("pFs%d" % k, T.Fs[:, a:b], T.C3s[:, 0:560], l, "lF q3w q3h")
+        mm("y%d" % k, 5 + k, "qa", 0, "F", a, b - a, "pF%d pFs%d" % (k, k))
+        if where["yc%d" % k] == "a":
+            op("yc%d" % k, lambda k=k, a=a, b=b: act.activation(T.yt[:, a:b], bank(5 + k, 0, b - a), Act.Copy), "y%d" % k)
+        else:
+            op("yc%d" % k, lambda k=k, a=a, b=b: vec.tensor_copy(T.yt[:, a:b], bank(5 + k, 0, b - a)), "y%d" % k)
+        dma("soc%d" % k, T.oc[:, 4 * a:4 * b], T.F[:, a:b].bitcast(dt.uint8), "dout", "pF%d" % k)
+        dma("sy%d" % k, T.y[:, a:b], T.yt[:, a:b], "dout", "yc%d" % k)
     for i in range(4):
-        inc("dout", (act if i % 2 else g.sync).dma_start(T.osc[4 * i:4 * i + 4, :], T.Fs[32 * i:32 * i + 4, :]), 16)
-    W("g", *[(s, c) for s, c in cnt.items()])
+        dma("sos%d" % i, T.osc[4 * i:4 * i + 4, :], T.Fs[32 * i:32 * i + 4, :], "dout", rng("pFs%d", len(CUTS)))
+
+    OPS[r] = ops
+    tok, cnt = dict(arrive), {}
+    for q in order:
+        for name in order[q]:
+            if name in ops and (name[:2] not in ("sc", "ss", "sl") or name[:4] == "scan"):
+                sem = ops[name][2] or "s" + q
+                cnt[sem] = cnt.get(sem, 0) + (16 if ops[name][2] else 1)
+                tok[name] = (sem, cnt[sem])
+    for q in order:
+        seen, drain = {}, []
+        for name in order[q]:
+            if name not in ops:
+                continue
+            fn, deps, sem = ops[name]
+            if name not in turns:
+                deps, drain = deps + drain, []
+            need = {}
+            for d in deps:
+                if d in tok:
+                    s, c = tok[d]
+                    need[s] = max(need.get(s, 0), c)
+            for s, c in need.items():
+                if seen.get(s, 0) < c:
+                    queue[q].wait_ge(T.sem[s], c)
+                    seen[s] = c
+            ins = fn()
+            if name[:2] == "ps":
+                drain = [name]
+            if name in tok:
+                ins.then_inc(T.sem[tok[name][0]], 16 if sem else 1)
+    cnt["ls"] = sent[0]
+    for s, c in cnt.items():
+        g.wait_ge(T.sem[s], c)

@@ -3,34 +3,34 @@ from concourse.mybir import dt, AluOpType as Op, ActivationFunctionType as Act
 
 F32, BF, I32, U16, F8, U8 = "float32", "bfloat16", "int32", "uint16", "float8_e4m3fn_x4", "uint8"
 SCRATCH = {"ps": ("psum", [128, 4096], F32)}
-for _names, _d in (("xt:1024 at:512 wt:2048 h1:1664 m2:1728 m3:1728 hh2:512 junk:1408", BF),
-                   ("eps:4 kb:4 RA:192 nh:32 nha:32 nhb:32 MM:160 XX:128 lo:32 hi:4 BBB:96 row:16 rjunk:480 B0:4 Bh:32 Ball:32 "
-                    "pf:4 K:76 KK:76 gi:8 wq:4 cp:4 cc:4 MK1:16 MK2:16 LA:172 L1:16 L2:16 PS:48 TW:12 th:100 TM:188 HM:188 SM:188 "
-                    "yt:496 Zh0:160 Zh1:192 Zh2:192 Ih:192", F32),
-                   ("pi:4 pm:4", I32), ("la:16 lb:8 lf:32", U16)):
+for _names, _d in (("xe:512 xt:1024 at:512 wt:2048 h1:1440 m2:1920 m3:1728 hh2:512 zt:512 junk:1408", BF),
+                   ("eps:4 kb:4 RA:224 nh:32 nha:32 nhb:32 XX:128 lo:32 hi:4 BBB:96 row:16 rjunk:480 B0:4 Bh:12 "
+                    "pf:4 K:80 KK:80 gi:8 wq:4 cp:4 cc:4 MK1:16 MK2:16 G0:392 G1:420 G2:420 L1:16 L2:16 th:100 TM:188 HM:188 SM:188 "
+                    "yt:496 Zh0:192 Zh1:224 Zh2:224 Ih:304 odd:80", F32),
+                   ("pi:4 pm:4", I32), ("la:20 lb:8 lf:32", U16)):
     for _s in _names.split():
         SCRATCH[_s.split(":")[0]] = ("sbuf", [128, int(_s.split(":")[1])], _d)
-for _n, _w in (("qa", 128), ("qw", 512), ("C0", 464), ("W1", 672), ("M1", 256), ("C2", 440), ("C3", 560),
+for _n, _w in (("qa", 128), ("qw", 512), ("XE", 128), ("C0", 464), ("W1", 688), ("M1", 256), ("C2", 488), ("C3", 560),
                ("H2", 176), ("F", 496)):
     SCRATCH[_n] = ("sbuf", [128, _w], F8)
     SCRATCH[_n + "s"] = ("sbuf", [128, _w], U8)
-SEMAPHORES = ["sv", "sa", "sp", "sg", "dx0", "dx1", "dx2", "da", "dw0", "dw1", "dout", "ls"] + \
+SEMAPHORES = ["sv", "sa", "sp", "sg", "dx0", "dx1", "dx2", "da", "dw0", "dw1", "dout", "ls", "nx1"] + \
     ["%s%d" % (n, t) for n in ("nc", "ns", "lm") for t in range(3)]
 HALF = (64, 80, 80)
 MOVE = (40, 80, 80)
 BIG = 2048.0
-CUTS = ((0, 256), (256, 496))
+CUTS = (((0, 192), (192, 384)), ((0, 256), (256, 496)))
 ORDER = {
-    "s0": "lxa lxr lw0 sbd soc0 soc1 sos0 sos2 sy0",
-    "g0": "ipi sel0 sel1 iwq igi sc0a ss0a sl0 iN iM0 iM1 iM2 iM3 iB0 icp0 icp1 sc1a ss1a sl1 sl2 sc2a ss2a",
-    "p0": "mM mE o1 o0 o3 o2 h1 h2 h0 h3 d0 d1 k11 d2 k12 k10 d3 k22 L3 L2 L1 L0 R2 R0 R3 R1 k21 k23 k20 f0 f3 f1 f2 n3 n1 n0 n2 y0 y1",
-    "a0": "lxb la lw1 c01 c00 ro1a ro0a ro3b ro0b ro3a ro1b rh2 rh3 rd0 c11 rd1 c12 rd3 sign0 c10 pMs0 c22 pMs1 ro7b ro7a rR2 rR0 rR1 c21 c23 c20 bh0 sign1 rf3 rf1 pHs th1 rf2 kb2 hi2 sign2 th4 bh2 tbase rn1 rn3 bh1 pFs0 pFs1 sos3 sos1 sy1",
-    "v0": "znh zkb1 zh1 zeps zL0 zhh zHM zHM2 qE pand zLa zXX pcopy zL1 qR qD qa zkb0 zgj qw1 zMM qw0 zHM1 zLb qw3 zMK qw2 ro2a zBh zRWb lo0 zgi q1a ro2b rh1 rh0 KK q1b tz03 ps0 tz02 tz01 sh0 sub0 tz00 tl00 tl01 rd2 scan0 q2m clamp0 clamp0b tb00 tb01 lM1 lM0 lM2 pM0 mk22 pM1 th35 mk12 mk21 ro6a ro6b ro4b ro5b ro5a mk10 ro4a rR3 mask1 q2L x1 q2R ps1 tz11 tz12 sh1 tz13 tz14 sub1 tz10 tl10 tl11 zHM0 scan1 rf0 clamp1 xd xdb c23c tb11 tb10 lH0 lH1 mk23 mk20 pH mask2 x2 ps2 tz24 tz20 sh2 tz21 tz22 sub2 lo2 tz23 tl21 tl20 c14c scan2 q3w clamp2 clamp2b tb20 tb21 t1 t3 t4 t2 tend rn0 rn2 sum q3h lF tbd pF0 pF1 yc0 yc1",
-    "s1": "lxa lxr lw0 soc0 soc1 sos0 sbd sy0 sos2",
-    "g1": "ipi sel0 sel1 iwq igi sc0a ss0a sl0 iN iM0 iM1 iM2 iM3 iB0 icp0 icp1 sc1a ss1a sl1 sl2 sc2a ss2a",
-    "p1": "mM mE o1 o0 o2 o3 h3 h0 h2 h1 d3 k11 d2 d0 d1 k12 k10 k22 L2 L3 L0 L1 R3 R1 R0 R2 k21 k23 k20 f0 f2 f3 f1 n1 n3 n2 n0 y0 y1",
-    "a1": "lxb la lw1 c01 ro0a c00 ro0b ro3a ro3b rh3 rh2 rd3 c11 rd0 rd1 c10 sign0 c12 kb2 pMs0 c22 pMs1 ro7a ro7b rR3 rR1 rR0 c21 c23 c20 sign1 rf0 rf2 pHs rf1 rf3 sign2 th4 bh0 tbase rn3 rn1 bh1 bh2 pFs0 pFs1 sos3 sos1 sy1",
-    "v1": "znh zkb1 zh1 zhh zHM pand zXX zLb zHM1 qE zLa zL1 qD zeps lo0 zgi zL0 qR pcopy zMK qa qw1 qw0 zHM2 zRWb zMM zBh qw2 qw3 ro2a ro1a zgj ro2b q1a ro1b rh0 rh1 q1b ps0 tz01 tz00 sh0 rd2 sub0 tz02 tz03 tl01 tl00 zkb0 scan0 KK q2m clamp0b clamp0 tb01 tb00 lM1 lM0 mk21 pM0 th35 mk12 lM2 mk10 pM1 ro6b ro6a ro4a mk22 ro5b ro5a ro4b mask1 q2L x1 ps1 tz14 rR2 sh1 q2R tz10 sub1 tz13 tz11 tl11 tz12 tl10 c23c scan1 zHM0 clamp1 xd xdb tb11 tb10 lH0 lH1 mk23 mk20 pH hi2 mask2 th1 lo2 x2 ps2 tz24 sh2 tz20 tz22 sub2 tz23 tz21 tl20 tl21 scan2 c14c q3w clamp2b clamp2 tb20 tb21 t4 t2 t3 t1 tend rn2 rn0 sum q3h lF tbd pF0 pF1 yc0 yc1",
+    "s0": "lxa lxr lw0 szc szy sbd0 sbd1 sbd2 soc0 soc1 sos1 sos2 sy1",
+    "g0": "ipi igi iwq sel0 sel1 iN sc0a ss0a sl0 iM0 iM1 iM2 iM3 sx1a sc1a ss1a iodd iB0 sl1 icp0 icp1 sl2 sc2a ss2a",
+    "p0": "mN mE mM o1 o0 o2 o3 h2 h3 h0 d0 h1 d1 k11 d3 d2 k12 k10 k22 L3 L0 L1 L2 R0 R3 R1 R2 k21 k20 k23 f0 f3 f1 f2 n1 n0 n2 n3 y0 y1",
+    "a0": "lxb la lw1 c02 c01 c00 ro0 ro3 rh3 rh0 rh1 rd0 rd3 rd1 sign0 c11 c12 c10 pMs0 c22 kb2 pMs1 ro5a ro5b rR0 rR1 rR3 c21 c20 c23 sign1 rf1 rf2 pHs lo2 rf3 th1 hi2 sign2 th4 bh1 rn1 tbase rn0 rn3 pFs0 pFs1 sos0 sy0 sos3",
+    "v0": "zxa zHM zxb zh1 zRWb znh zLa zLc zhh zkb1 qE zX zzt qX qa zeps zG2 zL0 zXX qZ pand qw0 qw1 zgj zLb zL1 qw2 qw3 zHM1 zkb0 ro1 ro2 zHM2 lo0 zG1 pcopy q1a rh2 q1c zyt ps0 tz03 tz02 sh0 tz01 tl01 tl00 q1b scan0 rd2 zMK clamp0b clamp0 KK tb00 tb01 q2m lM1 lM0 zgi lM2 pM0 mk10 pM1 ro7a ro4a ro4b ex1 mk12 ro6a ro7b ro6b q2L rR2 q2A mk22 mask1 q2R x1 ps1 tz14 tz12 sh1 tz11 tz13 tl11 tl10 zHM0 mk21 scan1 bh0 rf0 xd xdb c23c tb11 tb10 lH0 lH1 mk20 mk23 pH mask2 x2 ps2 tz24 tz22 sh2 tz23 tz21 tl20 tl21 th35 scan2 q3w clamp2b clamp2 c14c tb21 tb20 bh2 t1 t3 t2 tend t4 rn2 sum q3h lF pF0 pF1 yc0 yc1",
+    "s1": "lxa lxr lw0 sbd0 sbd1 sbd2 soc0 soc1 sos1 sy0 sos0 sy1",
+    "g1": "ipi igi iwq sel0 sel1 iN sc0a ss0a sl0 iM0 iM1 iM2 iM3 sx1a sc1a ss1a iodd iB0 sl1 icp0 icp1 sl2 sc2a ss2a",
+    "p1": "mM mN mE o0 o1 o3 o2 h2 h1 h3 h0 d2 d3 d1 k11 d0 k12 k10 k22 L1 L0 L2 L3 R3 R0 R2 R1 k21 k20 k23 f0 f2 f1 f3 n1 n2 n3 n0 y0 y1",
+    "a1": "lxb la lw1 c01 c00 c02 ro0 ro1 ro3 rh2 rh3 rd2 rd3 rd1 rd0 sign0 c11 c10 c12 pMs0 c22 pMs1 ro4a ro4b rR3 rR0 rR1 c21 c20 c23 sign1 rf2 rf1 pHs kb2 lo2 rf3 hi2 sign2 bh0 th1 bh1 th4 tbase rn1 rn3 pFs0 pFs1 sos2 sos3",
+    "v1": "znh zX zxa zkb0 zeps zL0 zHM zL1 zxb zLc qE zHM1 zXX qX qa zHM2 lo0 zLa qw0 zMK qw1 zkb1 zG2 qw3 qw2 qD zhh zRWb ro2 zLb q1a q1c rh1 ps0 tz02 tz03 rh0 sh0 tz01 q1b tl01 tl00 zgj pand scan0 zG1 zgi pcopy q2m clamp0b clamp0 KK tb01 tb00 zHM0 lM1 lM0 lM2 mk10 pM0 mk22 pM1 ro5a ro5b mk12 ro6a ro6b ro7a ro7b q2L q2A mask1 rR2 x1 ps1 tz14 tz12 q2R sh1 tz11 tz13 tl10 tl11 ex1 scan1 rf0 xd xdb mk21 tb10 tb11 lH0 lH1 mk20 mk23 pH mask2 c14c x2 ps2 tz24 tz22 sh2 tz21 tz23 tl20 tl21 th35 scan2 q3w clamp2 clamp2b c23c tb20 tb21 bh2 t4 t2 t3 tend t1 rn2 rn0 sum q3h lF pF0 pF1 yc0 yc1",
 }
 OPS = {}
 
@@ -41,9 +41,10 @@ def rank_program(g, core, T, topo):
         return
     n = len(T.cores)
     left, right = r > 0, r < n - 1
+    both = left and right
     vec, act, ten = g.vector, g.scalar, g.tensor
     queue = {"v": vec, "a": act, "p": ten, "g": g, "s": g.sync}
-    order = {q: ORDER[q + str(int(left and right))].split() for q in queue}
+    order = {q: ORDER[q + str(int(both))].split() for q in queue}
     where = {name: q for q in order for name in order[q]}
     ops, arrive, sent, turns = {}, {}, [0], []
 
@@ -52,7 +53,7 @@ def rank_program(g, core, T, topo):
 
     def rng(s, k=4):
         return " " + " ".join(s % i for i in range(k)) + " "
-    bank = lambda k, a, b: T.ps[:, 512 * k + a:512 * k + b]
+    bank = lambda k, a, b, p=128: T.ps[0:p, 512 * k + a:512 * k + b]
 
     inner = lambda ps: sorted(ps, key=lambda p: abs(2 * p - n + 1))
 
@@ -69,26 +70,26 @@ def rank_program(g, core, T, topo):
         rid, pnc, _ = topo.addr(T.cores[p])
         return DstId(rid=rid, pnc=pnc)
 
-    def send_ends(t, kind, name, w, to):
+    def send_ends(t, kind, name, land, w, to):
         tr = []
         for p in nbs(r):
             a, c = to[int(p > r)]
-            if kind == "c":
-                s, d = T[name][:, a:a + w].bitcast(dt.uint8), T[name][:, c:c + w].bitcast(dt.uint8)
+            if kind != "s":
+                s, d = T[name][:, a:a + w].bitcast(dt.uint8), T[land][:, c:c + w].bitcast(dt.uint8)
             else:
-                s, d = T[name + "s"][:, a:a + w], T[name + "s"][:, c:c + w]
+                s, d = T[name + "s"][:, a:a + w], T[land + "s"][:, c:c + w]
             e = engs(r, p)
             tr.append(RemoteDMATransfer(dst_ids=[did(p)], dma_engine_mask=sum(1 << i for i in e),
                                         remote_sem=T.sem["n%s%d" % (kind, t)], src=s, dst=d))
             sent[0] += len(e)
         g.remote_dma_fused(tr, local_sem=T.sem.ls)
 
-    def ends(t, name, w, to, depc, deps):
-        op("sc%da" % t, lambda: send_ends(t, "c", name, w, to), depc)
-        op("ss%da" % t, lambda: send_ends(t, "s", name, w, to), deps)
+    def ends(t, name, land, w, to, depc, deps):
+        op("sc%da" % t, lambda: send_ends(t, "c", name, land, w, to), depc)
+        op("ss%da" % t, lambda: send_ends(t, "s", name, land, w, to), deps)
 
     others = inner([p for p in range(n) if p != r])
-    Lbuf = lambda t, a, b, p=0, q=128: (T.LA[p:q, 4 + a:4 + b] if t == 0 else T["L%d" % t][p:q, a:b])
+    Lbuf = lambda t, a, b, p=0, q=128: (T.G0[p:q, 260 + a:260 + b] if t == 0 else T["L%d" % t][p:q, a:b])
 
     def send_costs(t):
         s = Lbuf(t, 4 * r, 4 * r + 4)
@@ -99,7 +100,7 @@ def rank_program(g, core, T, topo):
         sent[0] += len(e)
 
     for t in range(3):
-        for kind in "cs":
+        for kind in ("csx" if t == 1 else "cs"):
             arrive["@%s%d" % (kind, t)] = ("n%s%d" % (kind, t), sum(len(engs(p, r)) for p in nbs(r)))
         arrive["@l%d" % t] = ("lm%d" % t, sum(len(topo.engines(T.cores[p], T.cores[r])) for p in others))
 
@@ -121,12 +122,12 @@ def rank_program(g, core, T, topo):
 
     junk = [0]
 
-    def count(name, t, piece, k, deps):
+    def count(name, t, piece, k, deps, p=128):
         j = junk[0]
         junk[0] += 128
         c = 4 * r + piece
-        op(name, lambda: act.activation(T.junk[:, j:j + 128], bank(k, 0, 128), Act.Sign, bias=T.eps[:, 0:1],
-                                        accum_out=Lbuf(t, c, c + 1)), deps + " zeps zL%d" % t)
+        op(name, lambda: act.activation(T.junk[0:p, j:j + 128], bank(k, 0, 128, p), Act.Sign, bias=T.eps[0:p, 0:1],
+                                        accum_out=Lbuf(t, c, c + 1, 0, p)), deps + " zeps zL%d" % t)
 
     def relu(name, k, b, a, h, c, m, deps):
         out, src = h[:, 4 * c + b:4 * (c + m):4], bank(k, a, a + m)
@@ -160,41 +161,51 @@ def rank_program(g, core, T, topo):
 
     words = lambda ap: ap.bitcast(dt.uint32)
 
-    dma("lxa", T.xt[:, 512:672], T.x[:, 864:1024], "dx0")
-    dma("lxb", T.xt[:, 672:1024], T.x[:, 0:352], "dx2")
-    dma("lxr", T.xt[:, 0:512], T.x[:, 352:864], "dx1")
+    dma("lxa", T.xe[:, 96:256], T.x[:, 864:1024], "dx0")
+    dma("lxb", T.xe[:, 256:416], T.x[:, 0:160], "dx2")
+    dma("lxr", T.xt[:], T.x[:], "dx1")
     dma("la", T.at[:], T.a[:], "da")
     for b in range(2):
         dma("lw%d" % b, T.wt[:, 1024 * b:1024 * b + 1024], T.w[:, 1024 * b:1024 * b + 1024], "dw%d" % b)
 
+    fill("zxa", T.xe[:, 0:96], 0.0)
+    fill("zxb", T.xe[:, 416:512], 0.0)
     fill("znh", T.nh[0:32, :], 80.0)
     fill("zeps", T.eps[:, 0:1], -(2.0 ** -120))
     for t in range(2):
         fill("zL%d" % t, Lbuf(t, 4 * r, 4 * r + 4), 0.0)
-    fill("zLa", T.LA[:, 0:4], 0.0)
-    fill("zLb", T.LA[:, 20:172], 0.0)
-    fill("zMM", T.MM[:], 0.0)
+    fill("zLa", T.G0[:, 259:260], 0.0)
+    fill("zLb", T.G0[:, 2:260:4], 0.0)
+    fill("zLc", T.G0[:, 278:392:4], 0.0)
+    fill("zG1", T.G1[:, 1:420:4], 0.0)
+    fill("zG2", T.G2[:, 2:420:4], 0.0)
+    fill("zX", T.m2[:, 0:192], 0.0)
     fill("zXX", T.XX[0:64, :], 0.0)
-    if not (left and right):
-        fill("zh1", T.h1[:, 480:640] if left else T.h1[:, 640:800], 0.0)
-    fill("zhh", T.hh2[:, 320:512] if left and right else T.hh2[:], 0.0)
-    fill("zRWb", T.RA[0:32, 32:192], 130.0)
+    if not both:
+        fill("zh1", T.h1[:, 1024:1184] if left else T.h1[:, 1184:1344], 0.0)
+        fill("zzt", T.zt[:], 0.0)
+        fill("zyt", T.yt[:, 384:496], 0.0)
+        quant("qZ", "F", 368, 496, T.zt, 0, "zzt")
+        dma("szc", T.oc[:, 4 * 384:4 * 496], T.F[:, 384:496].bitcast(dt.uint8), "dout", "qZ")
+        dma("szy", T.y[:, 384:496], T.yt[:, 384:496], "dout", "zyt")
+    fill("zhh", T.hh2[:, 320:512] if both else T.hh2[:], 0.0)
+    fill("zRWb", T.RA[0:32, 64:224], 130.0)
     for t in range(2):
         fill("zkb%d" % t, T.kb[0:32, t:t + 1], 130.0 * HALF[t] - 0.125)
-    fill("zBh", T.Bh[0:32, :], 0.0)
     fill("zHM", T.HM[:], 1.0)
     for k, c in enumerate((0.0, -1.0 / BIG, BIG)):
         fill("zHM%d" % k, T.HM[:, k:186:6], c, "zHM")
     fill("zMK", T.MK1[:], 1.0)
     op("ipi", lambda: g.iota(T.pi[:, 0:1], [[0, 1]], 0, 1))
     iota("iN", T.K[:, 0:60], [[-32, 60]], 512, 0)
-    for k, (a, b, c) in enumerate(((0, 5, 200), (5, 10, -40), (10, 13, -112 if right else 88), (13, 16, 368 if left else 72))):
+    for k, (a, b, c) in enumerate(((0, 5, 208), (5, 10, -32), (10, 13, -112 if right else 96), (13, 20, 384 if left else 80))):
         iota("iM%d" % k, T.K[:, 60 + a:60 + b], [[-32, b - a]], -2 * (c + 16 * a), 0)
     iota("igi", T.gi[:, 0:7], [[-16, 7]], -80, 2)
     fill("zgi", T.gi[0:48, 6:7], 10000.0, "igi")
     fill("zgj", T.gi[0:32, 4:5], 10000.0, "igi")
     iota("iwq", T.wq[:, 0:3], [[1, 3]], 1, 0)
     iota("iB0", T.B0[:, 0:1], [[0, 1]], 0, 256)
+    iota("iodd", T.odd[0:32, :], [[2, 80]], -79, 0)
     iota("icp0", T.cp[:, 0:2], [[704, 2]], 80, 0)
     iota("icp1", T.cp[:, 2:4], [[192, 2]], 592, 0)
     op("sel0", lambda: g.affine_select(T.nha[0:32, :], T.nh[0:32, :], [[0, 32]], Op.is_ge, 0.0, -1, 1), "znh")
@@ -204,30 +215,38 @@ def rank_program(g, core, T, topo):
     aff("KK", T.KK[:], T.K[:], 1.0, T.pf[:, 0:1], "pcopy iN" + rng("iM%d"))
     ts("lo0", T.hi[0:32, 0:1], T.nhb[0:32, 0:1], -1.0, None, Op.mult, None, "sel1")
 
-    quant("qE", "C0", 128, 256, T.xt, 128, "lxa lxb")
-    quant("qR", "C0", 0, 128, T.xt, 0, "lxr")
-    quant("qD", "C0", 256, 384, T.xt, 0, "lxr")
+    quant("qE", "XE", 0, 128, T.xe, 0, "lxa lxb zxa zxb")
+    quant("qX", "C0", 0, 256, T.xt, 0, "lxr")
     quant("qa", "qa", 0, 128, T.at, 0, "la")
-    ends(0, "C0", 40, ((168, 384), (128, 424 if r + 2 < n else 384)), "qE", "qE")
-    mm("mE", 4, "C0", 104, "qa", 0, 128, "qE qR qa")
-    mm("mM", 5, "C0", 232, "qa", 0, 128, "qE qD qa")
-    count("c00", 0, 1, 4, "mE")
+    ends(0, "XE", "C0", 40, ((64, 256), (24, 296 if r + 2 < n else 256)), "qE", "qE")
+    mm("mE", 4, "XE", 0, "qa", 0, 128, "qE qa")
+    mm("mM", 5, "C0", 88, "qa", 0, 128, "qX qa")
+    mm("mN", 6, "C0", 40, "qa", 0, 128, "qX qa")
+    count("c00", 0, 2, 4, "mE")
     count("c01", 0, 0, 5, "mM")
-    op("sl0", lambda: send_costs(0), "c00 c01")
-    ha, hc, hm = (336, 120, 80) if left and right else (296, 160 if left else 120, 40)
+    count("c02", 0, 1, 6, "mN", 48)
+    op("sl0", lambda: send_costs(0), "c00 c01 c02")
+    ha, hc, hm = (232, 256, 104) if both else (168, 296 if left else 256, 40)
+    if both:
+        quant("qD", "C0", 336, 464, T.xt, 0, "lxr")
     for b in range(4):
         quant("qw%d" % b, "qw", 128 * b, 128 * b + 128, T.wt, 128 * b, "lw%d" % (b // 2))
-        mm("o%d" % b, b, "qw", 128 * b, "C0", 48, 336, "qE qR qD qw%d" % b)
-        relu("ro%da" % b, b, b, 120, T.h1, 200, 216, "o%d" % b)
-        relu("ro%db" % b, b, b, 0, T.h1, 0, 120, "o%d" % b)
-        mm("h%d" % b, 4 + b, "qw", 128 * b, "C0", ha, 128, "qD qw%d @c0 @s0 c00 c01" % b)
+        mm("o%d" % b, b, "qw", 128 * b, "C0", 0, 256, "qX qw%d" % b)
+        relu("ro%d" % b, b, b, 0, T.h1, 0, 256, "o%d" % b)
+        mm("h%d" % b, 4 + b, "qw", 128 * b, "C0", ha, 128, "qX qD qw%d @c0 @s0 " % b + ("c00", "c01", "c02", "")[b])
         relu("rh%d" % b, 4 + b, b, 128 - hm, T.h1, hc, hm, "h%d" % b)
-    quant("q1a", "W1", 328, 544, T.h1, 200, rng("ro%da"))
-    quant("q1b", "W1", 128, 328, T.h1, 0, rng("ro%db") + rng("rh%d") + "zh1")
-    ends(1, "W1", 120, ((288, 8), (168, 544)), "q1a q1b", "q1a q1b")
-    mm("k11", 4, "W1", 376, "qa", 0, 128, "q1a rh0")
-    mm("k10", 5, "W1", 248, "qa", 0, 128, "q1a q1b")
-    mm("k12", 6, "W1", 168, "qa", 0, 128, "q1b")
+    quant("q1a", "W1", 336, 560, T.h1, 0, rng("ro%d"))
+    quant("q1c", "W1", 128, 256, T.h1, 128, rng("ro%d"))
+    qb = 232 if both else 208
+    quant("q1b", "W1", qb, qb + 128, T.h1, qb, rng("ro%d") + rng("rh%d") + "zh1 q1a q1c")
+    q1 = " q1b "
+    we = 56 if both else 80 if left else 32
+    op("sx1a", lambda: send_ends(1, "x", "W1", "W1", we, ((416 - we, 128 - we), (176, 560))), "q1a q1c")
+    op("sc1a", lambda: send_ends(1, "c", "W1", "W1", 120 - we, ((296, 8), (176 + we, 560 + we))), q1)
+    op("ss1a", lambda: send_ends(1, "s", "W1", "W1", 120, ((296, 8), (176, 560))), q1)
+    mm("k11", 4, "W1", 384, "qa", 0, 128, "qa q1a rh0")
+    mm("k10", 5, "W1", 256, "qa", 0, 128, "qa q1a q1b")
+    mm("k12", 6, "W1", 176, "qa", 0, 128, "qa q1b")
     for k, b in ((0, 5), (1, 4), (2, 6)):
         count("c1%d" % k, 1, k, b, "k1%d" % k)
     op("sl1", lambda: send_costs(1), "c10 c11 c12")
@@ -237,44 +256,41 @@ def rank_program(g, core, T, topo):
     XB = lambda t: T.XX[32:37, 32 * t:32 * t + 32]
     tb = lambda t: rng("tb%d%%d" % t, 2)
     for t in range(3):
-        s, lm, Zh = str(t), 4 + 20 * t, T["Zh%d" % t]
-        LM = lambda a, b, c=1, p=0, q=128, lm=lm: T.LA[p:q, lm + a:lm + b:c]
-        have = "@l0 c00 c01 zLa zLb" if t == 0 else "mask" + s
+        s, k, G, Zh = str(t), (2, 1, 2)[t], T["G%d" % t], T["Zh%d" % t]
+        lm = k + 287 if t else 260
+        LM = lambda a, b, c=1, p=0, q=128, lm=lm, G=G: G[p:q, lm + a:lm + b:c]
+        have = "@l0 c00 c01 c02 zLa zLb zLc" if t == 0 else "mask" + s
         if t:
             tt("mask" + s, LM(0, 16), T["L" + s][:], T["MK" + s][:], Op.mult,
-               "@l%d zLb " % t + ("c10 c11 c12 mk10 mk12" if t == 1 else rng("c2%d") + rng("mk2%d")))
-        op("ps" + s, lambda t=t, LM=LM: vec.tensor_tensor_scan(T.PS[0:64, 16 * t:16 * t + 16],
-                                                               LM(0, 16, 1, 0, 64) if t else LM(-1, 15, 1, 0, 64), LM(0, 16, 1, 64, 128),
-                                                               0.0, Op.add, Op.add), have)
-        ts("sh" + s, T.TW[0:64, 4 * t:4 * t + 3], T.wq[0:64, 0:3], T.PS[0:64, 16 * t + 15:16 * t + 16], 0.25, Op.mult, Op.mult, "iwq ps" + s)
-        k = 16 * t + (2 if t == 2 else 1)
-        tt("sub" + s, T.MM[0:64, 32 * t + 1:32 * t + 4], T.PS[0:64, k:k + 9:4], T.TW[0:64, 4 * t:4 * t + 3], Op.subtract, "zMM sh" + s)
+               "@l%d zG%d " % (t, t) + ("c10 c11 c12 mk10 mk12" if t == 1 else rng("c2%d") + rng("mk2%d")))
+        op("ps" + s, lambda t=t, LM=LM, G=G: vec.tensor_tensor_scan(G[0:64, 4:20], LM(0, 16, 1, 0, 64) if t else LM(-1, 15, 1, 0, 64),
+                                                                    LM(0, 16, 1, 64, 128), 0.0, Op.add, Op.add), have)
+        ts("sh" + s, G[0:64, k + 132:k + 141:4], T.wq[0:64, 0:3], G[0:64, 19:20], -0.25, Op.mult, Op.mult, "iwq ps" + s)
         if t:
-            tt("x" + s, T.MM[:, 65 + 32 * t:68 + 32 * t], LM(1 + t, 10 + t, 4), LM(4, 13, 4), Op.add, "zMM mask" + s)
-            turn("tz%d4" % t, Zh[0:32, 160:192], LM(1, 126, 4, 0, 32), "mask" + s)
-        for k in range(4):
-            p, q = 32 * k, 32 * k + 32
-            if k < 2:
-                turn("tl%d%d" % (t, k), (T.RA if k else Zh)[0:32, 0:32], T.MM[p:q, 32 * t:32 * t + 32],
-                     "sub%d %s" % (t, "scan%d" % (t - 1) if t else ""))
-                turn("tb%d%d" % (t, k), T.BBB[2 * p:2 * q, 32 * t:32 * t + 32], XX(3 if t == 1 else t, 32, 64),
+            tt("x" + s, G[:, k + 260:k + 269:4], LM(1 + t, 10 + t, 4), LM(4, 13, 4), Op.add, "mask" + s)
+            turn("tz%d4" % t, Zh[0:32, 192:224], LM(1, 126, 4, 0, 32), "mask" + s)
+        turn("tl%d0" % t, Zh[0:32, 0:96], G[0:32, k:k + 381:4], "sh%d %s" % (t, "x" + s if t else ""))
+        turn("tl%d1" % t, T.RA[0:32, 0:64], G[32:64, k:k + 253:4], "sh%d %s" % (t, "~scan%d" % (t - 1) if t else ""))
+        for j in range(4):
+            p, q = 32 * j, 32 * j + 32
+            if j < 2:
+                turn("tb%d%d" % (t, j), T.BBB[2 * p:2 * q, 32 * t:32 * t + 32], XX(3 if t == 1 else t, 32, 64),
                      "xd xdb" if t == 1 else "clamp%d clamp%db" % (t, t))
-            if t == 0:
-                a = -3 if k < 2 else 1
-                turn("tz0%d" % k, Zh[0:32, 32 + p:32 + q], LM(a, a + 125, 4, p, q), have)
-            else:
-                turn("tz%d%d" % (t, k), Zh[0:32, 32 + p:32 + q], T.MM[p:q, 64 + 32 * t:96 + 32 * t], "x" + s)
-        h, a, w = 32 + HALF[t] + MOVE[t], 31 + HALF[t] - MOVE[t], 2 * MOVE[t]
+            if j:
+                a = k + 256 + (4 if j > 1 and not t else 0)
+                turn("tz%d%d" % (t, j), Zh[0:32, 64 + p:64 + q], G[p:q, a:a + 125:4], "x" + s if t else have)
+        h, a, w = 63 + HALF[t] + MOVE[t], 63 + HALF[t] - MOVE[t], 2 * MOVE[t] + (80 if t == 1 else 0)
         op("scan" + s, lambda Zh=Zh, h=h: vec.tensor_tensor_scan(T.Ih[0:5, 0:h], Zh[0:5, 0:h], T.RA[0:5, 0:h], 0.0, Op.add, Op.add),
            "zRWb" + rng("tl%d%%d" % t, 2) + rng("tz%d%%d" % t, 5 if t else 4) + ("sign%d" % (t - 1) if t else ""))
-        op("sign" + s, lambda t=t, a=a, w=w: act.activation(T.rjunk[0:5, 160 * t:160 * t + w], T.Ih[0:5, a:a + w], Act.Sign,
-                                                            bias=T.kb[0:5, t:t + 1], scale=-1.0, accum_out=T.row[0:5, t:t + 1]),
-           "scan%d %s" % (t, ("zkb0", "zkb1", "kb2")[t]))
+        j = (0, 80, 320)[t]
+        op("sign" + s, lambda t=t, a=a, w=w, j=j: act.activation(T.rjunk[0:5, j:j + w], T.Ih[0:5, a:a + w], Act.Sign,
+                                                                 bias=T.kb[0:5, t:t + 1], scale=-1.0, accum_out=T.row[0:5, t:t + 1]),
+           "scan%d %s" % (t, ("zkb0", "zkb1 ex1", "kb2")[t]))
+    ts("ex1", T.Ih[0:5, 223:303], T.odd[0:5, :], XX(0, 1), 65536.0, Op.add, Op.mult, "iodd clamp0")
     for b, X in (("", XX), ("b", XB)):
         ts("clamp0" + b, X(0), T.nhb[0:5, :], T.row[0:5, 0:1], T.hi[0:5, 0:1], Op.min, Op.max, "zXX sign0 lo0")
-        ts("xd" + b, X(3), XX(1), T.hi[0:5, 0:1], -1.0, Op.max, Op.mult, "clamp1")
+        ts("xd" + b, X(3), T.nhb[0:5, :], T.row[0:5, 1:2], T.hi[0:5, 0:1], Op.min, Op.max, "zXX sign1 lo0")
         ts("clamp2" + b, X(2), T.lo[0:5, 0:32], T.row[0:5, 2:3], T.hi[0:5, 2:3], Op.max, Op.min, "sign2 lo2 hi2")
-    ts("clamp1", XX(1), XX(0), T.row[0:5, 1:2], T.nhb[0:5, 0:1], Op.subtract, Op.min, "clamp0 sign1")
     aff("lo2", T.lo[0:5, 0:32], XX(3), 1.0, T.hi[0:5, 0:1], "xd")
     aff("hi2", T.hi[0:5, 2:3], XX(3, 1), 1.0, T.nhb[0:5, 0:1], "xd")
     aff("kb2", T.kb[0:5, 2:3], XX(0, 1), -65.0, 130.0 * HALF[2] - 0.125, "clamp0")
@@ -287,44 +303,43 @@ def rank_program(g, core, T, topo):
 
     for k, (a, b, j) in enumerate(((0, 5, 0), (5, 13, 1), (13, 16, 0))):
         ts("lM%d" % k, T.la[:, a:b], T.KK[:, 60 + a:60 + b], BO(0, r + j, r + j + 1), -0.5, Op.subtract, Op.mult, "KK" + tb(0))
-    pick("pM0", words(T.M1[:, 0:160]), words(T.W1[:, 128:544]), T.la[:, 0:10], "q1a q1b lM0 lM1")
-    pick("pMs0", T.M1s[:, 0:160], T.W1s[:, 128:544], T.la[:, 0:10], "q1a q1b lM0 lM1")
-    pick("pM1", words(T.M1[:, 160:256]), words(T.W1[:, 0:664]), T.la[:, 10:16], "q1a q1b @c1 lM1 lM2")
-    pick("pMs1", T.M1s[:, 160:256], T.W1s[:, 0:664], T.la[:, 10:16], "q1a q1b @s1 lM1 lM2")
+    pick("pM0", words(T.M1[:, 0:160]), words(T.W1[:, 128:560]), T.la[:, 0:10], q1 + "lM0 lM1")
+    pick("pMs0", T.M1s[:, 0:160], T.W1s[:, 128:560], T.la[:, 0:10], q1 + "lM0 lM1")
+    pick("pM1", words(T.M1[:, 160:256]), words(T.W1[:, 0:680]), T.la[:, 10:16], q1 + "@x1 @c1 lM1 lM2")
+    pick("pMs1", T.M1s[:, 160:256], T.W1s[:, 0:680], T.la[:, 10:16], q1 + "@s1 lM1 lM2")
     for b in range(4):
-        mm("d%d" % b, b, "qw", 128 * b, "W1", 368, 176, "q1a ro%db" % b)
-        relu("rd%d" % b, b, b, 0, T.m2, 256, 176, "d%d" % b)
-        mm("L%d" % b, 4 + b, "qw", 128 * b, "M1", 0, 160, "pM0 pMs0 " + ("c22", "c10", "c12", "rh3")[b])
-        relu("ro%da" % (4 + b), 4 + b, b, 0, T.m2, 176, 80, "L%d" % b)
-        relu("ro%db" % (4 + b), 4 + b, b, 80, T.m2, 0, 80, "L%d" % b)
-        mm("R%d" % b, b, "qw", 128 * b, "M1", 128, 128, "pM0 pMs0 pM1 pMs1 rd%d" % b)
-        relu("rR%d" % b, b, b, 32, T.m2, 80, 96, "R%d" % b)
-    quant("q2m", "C2", 264, 440, T.m2, 256, rng("rd%d"))
-    quant("q2L", "C2", 232, 360, T.m2, 224, "q2m k22 ro4a ro5a ro6a ro7a")
-    quant("q2R", "C2", 8, 232, T.m2, 0, rng("rR%d") + "ro4a ro5a ro6a ro7a ro4b ro5b ro6b ro7b")
-    mm("k21", 7, "C2", 232, "qa", 0, 128, "q2m q2L ro7b")
-    mm("k22", 4, "C2", 312, "qa", 0, 128, "q2m c11")
-    mm("k20", 4, "C2", 104, "qa", 0, 128, "q2R")
-    mm("k23", 0, "C2", 8, "qa", 0, 128, "q2R")
-    count("c21", 2, 1, 7, "k21")
-    count("c22", 2, 2, 4, "k22")
-    count("c20", 2, 0, 4, "k20")
-    count("c23", 2, 3, 0, "k23")
+        mm("d%d" % b, b, "qw", 128 * b, "W1", 376, 176, "q1a ro%d" % b)
+        relu("rd%d" % b, b, b, 0, T.m2, 304, 176, "d%d" % b)
+        mm("L%d" % b, 4 + b, "qw", 128 * b, "M1", 0, 160, "pM0 pMs0 " + ("c11", "c10", "c12", "rh3")[b])
+        relu("ro%da" % (4 + b), 4 + b, b, 0, T.m2, 224, 80, "L%d" % b)
+        relu("ro%db" % (4 + b), 4 + b, b, 80, T.m2, 48, 80, "L%d ~ro%da" % (b, 4 + b))
+        mm("R%d" % b, b, "qw", 128 * b, "M1", 128, 128, "pM0 pMs0 pM1 pMs1 rd%d %s" % (b, "" if b else "c22"))
+        relu("rR%d" % b, b, b, 32, T.m2, 128, 96, "R%d" % b)
+    roa, rob = " ro4a ro5a ro6a ro7a ", " ro4b ro5b ro6b ro7b "
+    quant("q2m", "C2", 312, 488, T.m2, 304, rng("rd%d"))
+    quant("q2L", "C2", 232, 360, T.m2, 224, "q2m" + roa)
+    quant("q2A", "C2", 8, 136, T.m2, 0, "zX" + rob)
+    quant("q2R", "C2", 120, 248, T.m2, 112, rng("rR%d") + "q2L q2A")
+    q2 = " q2R "
+    mm("k21", 7, "C2", 280, "qa", 0, 128, "q2m q2L ro7a ro7b")
+    mm("k22", 0, "C2", 360, "qa", 0, 128, "q2m")
+    mm("k20", 4, "C2", 152, "qa", 0, 128, "q2R")
+    mm("k23", 5, "C2", 56, "qa", 0, 128, "q2R")
+    for k in range(4):
+        count("c2%d" % k, 2, k, (4, 7, 0, 5)[k], "k2%d" % k)
     op("sl2", lambda: send_costs(2), rng("c2%d"))
-    for k, c in ((0, 27), (1, 19)):
+    for k, c in ((0, 30), (1, 22)):
         ts("lH%d" % k, T.lb[:, 3 * k:3 * k + 3], T.KK[:, c:c + 3], BO(1, r + k, r + k + 1), -0.5, Op.subtract, Op.mult, "KK" + tb(1))
-    pick("pH", words(T.H2[:, 0:96]), words(T.C2[:, 0:264]), T.lb[:, 0:6], "q2L q2R lH0 lH1")
-    pick("pHs", T.H2s[:, 0:96], T.C2s[:, 0:264], T.lb[:, 0:6], "q2L q2R lH0 lH1")
-    ends(2, "H2", 40, ((8, 136 if r > 1 else 96), (48, 96)), "pH", "pHs")
+    pick("pH", words(T.H2[:, 0:96]), words(T.C2[:, 0:312]), T.lb[:, 0:6], q2 + "lH0 lH1")
+    pick("pHs", T.H2s[:, 0:96], T.C2s[:, 0:312], T.lb[:, 0:6], q2 + "lH0 lH1")
+    ends(2, "H2", "H2", 40, ((8, 136 if r > 1 else 96), (48, 96)), "pH", "pHs")
 
-    na, nc, nm = (48, 0, 80) if left and right else (8, 0 if left else 40, 40)
+    na, nc, nm = (48, 0, 80) if both else (8, 0 if left else 40, 40)
     for b in range(4):
-        k = (5, 6, 7, 1)[b]
-        mm("f%d" % b, k, "qw", 128 * b, "C2", 8, 432, "q2m q2L q2R " + ("c21" if k == 7 else ""))
-        relu("rf%d" % b, k, b, 0, T.m3, 0, 432, "f%d" % b)
-        k = (4, 0, 2, 3)[b]
-        mm("n%d" % b, k, "qw", 128 * b, "H2", na, 128, "pH pHs @c2 @s2 c20 c23")
-        relu("rn%d" % b, k, b, 128 - nm, T.hh2, nc, nm, "zhh n%d" % b)
+        mm("f%d" % b, b, "qw", 128 * b, "C2", 56, 432, q2)
+        relu("rf%d" % b, b, b, 0, T.m3, 0, 432, "f%d" % b)
+        mm("n%d" % b, 4 + b, "qw", 128 * b, "H2", na, 128, "pH pHs @c2 @s2" + rng("c2%d"))
+        relu("rn%d" % b, 4 + b, b, 128 - nm, T.hh2, nc, nm, "zhh n%d" % b)
     quant("q3w", "C3", 0, 432, T.m3, 0, rng("rf%d"))
     quant("q3h", "C3", 432, 560, T.hh2, 0, "zhh" + rng("rn%d"))
     tt("c23c", T.cc[:, 0:2], BO(0, r, r + 2), T.cp[:, 0:2], Op.add, "icp0" + tb(0))
@@ -340,33 +355,34 @@ def rank_program(g, core, T, topo):
     ts("t2", TM(4), T.KK[:, 11:42], e, T.cc[:, 0:1], Op.is_le, Op.mult, "KK c23c" + tb(2))
     ts("t4", TM(5), T.th[:, 68:99], e, T.cc[:, 3:4], Op.is_le, Op.mult, "th4 c14c" + tb(2))
     op("sum", lambda: vec.tensor_tensor_scan(T.SM[:, 0:186], T.HM[:, 0:186], T.TM[:, 0:186], 0.0, Op.mult, Op.add),
-       "t1 t2 t3 t4 tend tbase" + rng("zHM%d", 3))
+       "t1 t2 t3 t4 tend tbase zHM" + rng("zHM%d", 3))
     ts("lF", T.lf[:, 0:31], T.SM[:, 5:186:6], 0.5, 520.0, Op.mult, Op.min, "sum")
-    aff("bh0", T.Bh[0:5, 0:1], XX(0, 1), 0.5, T.B0[0:5, 0:1], "zBh iB0 clamp0")
-    aff("bh1", T.Bh[0:5, 1:2], XX(3, 1), 0.5, T.Bh[0:5, 0:1], "bh0 xd")
-    aff("bh2", T.Bh[0:5, 2:3], XX(2, 1), 0.5, T.Bh[0:5, 0:1], "bh0 clamp2")
-    turn("tbd", T.Ball[0:32, :], T.Bh[0:32, :], "bh1 bh2")
+    aff("bh0", T.Bh[0:5, 0:1], XX(0, 1), 0.5, T.B0[0:5, 0:1], "iB0 clamp0")
+    aff("bh1", T.Bh[0:5, 4:5], XX(3, 1), 0.5, T.Bh[0:5, 0:1], "bh0 xd")
+    aff("bh2", T.Bh[0:5, 8:9], XX(2, 1), 0.5, T.Bh[0:5, 0:1], "bh0 clamp2")
 
-    dma("sbd", T.bd[:], T.Ball[0:3, 0:5], "dout", "tbd")
-    for k, (a, b) in enumerate(CUTS):
+    for t in range(3):
+        dma("sbd%d" % t, T.bd[t, :], T.Bh[0:5, 4 * t:4 * t + 1], "dout", "bh%d" % t)
+    cuts = CUTS[int(both)]
+    for k, (a, b) in enumerate(cuts):
         l = T.lf[:, a // 16:b // 16]
-        pick("pF%d" % k, words(T.F[:, a:b]), words(T.C3[:, 0:560]), l, "lF q3w q3h")
-        pick("pFs%d" % k, T.Fs[:, a:b], T.C3s[:, 0:560], l, "lF q3w q3h")
-        mm("y%d" % k, 5 + k, "qa", 0, "F", a, b - a, "pF%d pFs%d" % (k, k))
+        pick("pF%d" % k, words(T.F[:, a:b]), words(T.C3[:, 0:560]), l, "lF q3w q3h qZ")
+        pick("pFs%d" % k, T.Fs[:, a:b], T.C3s[:, 0:560], l, "lF q3w q3h qZ")
+        mm("y%d" % k, k, "qa", 0, "F", a, b - a, "pF%d pFs%d" % (k, k))
         if where["yc%d" % k] == "a":
-            op("yc%d" % k, lambda k=k, a=a, b=b: act.activation(T.yt[:, a:b], bank(5 + k, 0, b - a), Act.Copy), "y%d" % k)
+            op("yc%d" % k, lambda k=k, a=a, b=b: act.activation(T.yt[:, a:b], bank(k, 0, b - a), Act.Copy), "y%d" % k)
         else:
-            op("yc%d" % k, lambda k=k, a=a, b=b: vec.tensor_copy(T.yt[:, a:b], bank(5 + k, 0, b - a)), "y%d" % k)
+            op("yc%d" % k, lambda k=k, a=a, b=b: vec.tensor_copy(T.yt[:, a:b], bank(k, 0, b - a)), "y%d" % k)
         dma("soc%d" % k, T.oc[:, 4 * a:4 * b], T.F[:, a:b].bitcast(dt.uint8), "dout", "pF%d" % k)
         dma("sy%d" % k, T.y[:, a:b], T.yt[:, a:b], "dout", "yc%d" % k)
     for i in range(4):
-        dma("sos%d" % i, T.osc[4 * i:4 * i + 4, :], T.Fs[32 * i:32 * i + 4, :], "dout", rng("pFs%d", len(CUTS)))
+        dma("sos%d" % i, T.osc[4 * i:4 * i + 4, :], T.Fs[32 * i:32 * i + 4, :], "dout", rng("pFs%d", len(cuts)) + "qZ")
 
     OPS[r] = ops
     tok, cnt = dict(arrive), {}
     for q in order:
         for name in order[q]:
-            if name in ops and (name[:2] not in ("sc", "ss", "sl") or name[:4] == "scan"):
+            if name in ops and (name[:2] not in ("sc", "ss", "sl", "sx") or name[:4] == "scan"):
                 sem = ops[name][2] or "s" + q
                 cnt[sem] = cnt.get(sem, 0) + (16 if ops[name][2] else 1)
                 tok[name] = (sem, cnt[sem])
@@ -380,6 +396,10 @@ def rank_program(g, core, T, topo):
                 deps, drain = deps + drain, []
             need = {}
             for d in deps:
+                if d[0] == "~":
+                    d = d[1:]
+                    if where.get(d) == q:
+                        continue
                 if d in tok:
                     s, c = tok[d]
                     need[s] = max(need.get(s, 0), c)

from concourse.bass import DstId, RemoteDMATransfer
from concourse.mybir import dt, AluOpType as Op, ActivationFunctionType as Act

F32, BF, I32, U16, F8, U8 = "float32", "bfloat16", "int32", "uint16", "float8_e4m3fn_x4", "uint8"
SCRATCH = {"ps": ("psum", [128, 4096], F32)}
for _names, _d in (("xe:512 xt:1024 at:512 wt:2048 h1:1440 m2:1920 m3:1728 hh2:512 zt:512 junk:1408", BF),
                   ("eps:4 kb:4 RA:224 nh:32 nha:32 nhb:32 XX:128 lo:32 hi:4 BBB:96 row:16 rjunk:480 B0:4 Bh:12 "
                    "pf:4 K:80 KK:80 gi:8 wq:4 cp:4 cc:4 MK1:16 MK2:16 G0:392 G1:420 G2:420 L1:16 L2:16 th:100 TM:188 HM:188 SM:188 "
                    "yt:496 Zh0:192 Zh1:224 Zh2:224 Ih:304 odd:80", F32),
                   ("pi:4 pm:4", I32), ("la:20 lb:8 lf:32", U16)):
    for _s in _names.split():
        SCRATCH[_s.split(":")[0]] = ("sbuf", [128, int(_s.split(":")[1])], _d)
for _n, _w in (("qa", 128), ("qw", 512), ("XE", 128), ("C0", 464), ("W1", 688), ("M1", 256), ("C2", 488), ("C3", 560),
               ("H2", 176), ("F", 496)):
    SCRATCH[_n] = ("sbuf", [128, _w], F8)
    SCRATCH[_n + "s"] = ("sbuf", [128, _w], U8)
SEMAPHORES = ["sv", "sa", "sp", "sg", "dx0", "dx1", "dx2", "da", "dw0", "dw1", "dout", "ls", "nx1"] + \
    ["%s%d" % (n, t) for n in ("nc", "ns", "lm") for t in range(3)]
HALF = (64, 80, 80)
MOVE = (40, 80, 80)
BIG = 2048.0
CUTS = (((0, 192), (192, 384)), ((0, 256), (256, 496)))
ORDER = {
    "s0": "lxa lxr lw0 szc szy sbd0 sbd1 sbd2 soc0 soc1 sos1 sos2 sy1",
    "g0": "ipi igi iwq sel0 sel1 iN sc0a ss0a sl0 iM0 iM1 iM2 iM3 sx1a sc1a ss1a iodd iB0 sl1 icp0 icp1 sl2 sc2a ss2a",
    "p0": "mN mE mM o1 o0 o2 o3 h2 h3 h0 d0 h1 d1 k11 d3 d2 k12 k10 k22 L3 L0 L1 L2 R0 R3 R1 R2 k21 k20 k23 f0 f3 f1 f2 n1 n0 n2 n3 y0 y1",
    "a0": "lxb la lw1 c02 c01 c00 ro0 ro3 rh3 rh0 rh1 rd0 rd3 rd1 sign0 c11 c12 c10 pMs0 c22 kb2 pMs1 ro5a ro5b rR0 rR1 rR3 c21 c20 c23 sign1 rf1 rf2 pHs lo2 rf3 th1 hi2 sign2 th4 bh1 rn1 tbase rn0 rn3 pFs0 pFs1 sos0 sy0 sos3",
    "v0": "zxa zHM zxb zh1 zRWb znh zLa zLc zhh zkb1 qE zX zzt qX qa zeps zG2 zL0 zXX qZ pand qw0 qw1 zgj zLb zL1 qw2 qw3 zHM1 zkb0 ro1 ro2 zHM2 lo0 zG1 pcopy q1a rh2 q1c zyt ps0 tz03 tz02 sh0 tz01 tl01 tl00 q1b scan0 rd2 zMK clamp0b clamp0 KK tb00 tb01 q2m lM1 lM0 zgi lM2 pM0 mk10 pM1 ro7a ro4a ro4b ex1 mk12 ro6a ro7b ro6b q2L rR2 q2A mk22 mask1 q2R x1 ps1 tz14 tz12 sh1 tz11 tz13 tl11 tl10 zHM0 mk21 scan1 bh0 rf0 xd xdb c23c tb11 tb10 lH0 lH1 mk20 mk23 pH mask2 x2 ps2 tz24 tz22 sh2 tz23 tz21 tl20 tl21 th35 scan2 q3w clamp2b clamp2 c14c tb21 tb20 bh2 t1 t3 t2 tend t4 rn2 sum q3h lF pF0 pF1 yc0 yc1",
    "s1": "lxa lxr lw0 sbd0 sbd1 sbd2 soc0 soc1 sos1 sy0 sos0 sy1",
    "g1": "ipi igi iwq sel0 sel1 iN sc0a ss0a sl0 iM0 iM1 iM2 iM3 sx1a sc1a ss1a iodd iB0 sl1 icp0 icp1 sl2 sc2a ss2a",
    "p1": "mM mN mE o0 o1 o3 o2 h2 h1 h3 h0 d2 d3 d1 k11 d0 k12 k10 k22 L1 L0 L2 L3 R3 R0 R2 R1 k21 k20 k23 f0 f2 f1 f3 n1 n2 n3 n0 y0 y1",
    "a1": "lxb la lw1 c01 c00 c02 ro0 ro1 ro3 rh2 rh3 rd2 rd3 rd1 rd0 sign0 c11 c10 c12 pMs0 c22 pMs1 ro4a ro4b rR3 rR0 rR1 c21 c20 c23 sign1 rf2 rf1 pHs kb2 lo2 rf3 hi2 sign2 bh0 th1 bh1 th4 tbase rn1 rn3 pFs0 pFs1 sos2 sos3",
    "v1": "znh zX zxa zkb0 zeps zL0 zHM zL1 zxb zLc qE zHM1 zXX qX qa zHM2 lo0 zLa qw0 zMK qw1 zkb1 zG2 qw3 qw2 qD zhh zRWb ro2 zLb q1a q1c rh1 ps0 tz02 tz03 rh0 sh0 tz01 q1b tl01 tl00 zgj pand scan0 zG1 zgi pcopy q2m clamp0b clamp0 KK tb01 tb00 zHM0 lM1 lM0 lM2 mk10 pM0 mk22 pM1 ro5a ro5b mk12 ro6a ro6b ro7a ro7b q2L q2A mask1 rR2 x1 ps1 tz14 tz12 q2R sh1 tz11 tz13 tl10 tl11 ex1 scan1 rf0 xd xdb mk21 tb10 tb11 lH0 lH1 mk20 mk23 pH mask2 c14c x2 ps2 tz24 tz22 sh2 tz21 tz23 tl20 tl21 th35 scan2 q3w clamp2 clamp2b c23c tb20 tb21 bh2 t4 t2 t3 tend t1 rn2 rn0 sum q3h lF pF0 pF1 yc0 yc1",
}
OPS = {}


def rank_program(g, core, T, topo):
    r = T.rank_of(core)
    if r is None:
        return
    n = len(T.cores)
    left, right = r > 0, r < n - 1
    both = left and right
    vec, act, ten = g.vector, g.scalar, g.tensor
    queue = {"v": vec, "a": act, "p": ten, "g": g, "s": g.sync}
    order = {q: ORDER[q + str(int(both))].split() for q in queue}
    where = {name: q for q in order for name in order[q]}
    ops, arrive, sent, turns = {}, {}, [0], []

    def op(name, fn, deps="", sem=None):
        ops[name] = (fn, deps.split(), sem)

    def rng(s, k=4):
        return " " + " ".join(s % i for i in range(k)) + " "
    bank = lambda k, a, b, p=128: T.ps[0:p, 512 * k + a:512 * k + b]

    inner = lambda ps: sorted(ps, key=lambda p: abs(2 * p - n + 1))

    def nbs(q):
        return [p for p in (q - 1, q + 1) if 0 <= p < n]

    def engs(q, p):
        e = topo.engines(T.cores[q], T.cores[p])
        k = len(e) // len(nbs(q))
        i = nbs(q).index(p)
        return e[k * i:k * i + k]

    def did(p):
        rid, pnc, _ = topo.addr(T.cores[p])
        return DstId(rid=rid, pnc=pnc)

    def send_ends(t, kind, name, land, w, to):
        tr = []
        for p in nbs(r):
            a, c = to[int(p > r)]
            if kind != "s":
                s, d = T[name][:, a:a + w].bitcast(dt.uint8), T[land][:, c:c + w].bitcast(dt.uint8)
            else:
                s, d = T[name + "s"][:, a:a + w], T[land + "s"][:, c:c + w]
            e = engs(r, p)
            tr.append(RemoteDMATransfer(dst_ids=[did(p)], dma_engine_mask=sum(1 << i for i in e),
                                        remote_sem=T.sem["n%s%d" % (kind, t)], src=s, dst=d))
            sent[0] += len(e)
        g.remote_dma_fused(tr, local_sem=T.sem.ls)

    def ends(t, name, land, w, to, depc, deps):
        op("sc%da" % t, lambda: send_ends(t, "c", name, land, w, to), depc)
        op("ss%da" % t, lambda: send_ends(t, "s", name, land, w, to), deps)

    others = inner([p for p in range(n) if p != r])
    Lbuf = lambda t, a, b, p=0, q=128: (T.G0[p:q, 260 + a:260 + b] if t == 0 else T["L%d" % t][p:q, a:b])

    def send_costs(t):
        s = Lbuf(t, 4 * r, 4 * r + 4)
        e = topo.engines(T.cores[r], T.cores[others[0]])
        g.remote_dma_fused([RemoteDMATransfer(dst_ids=[did(p) for p in others], dma_engine_mask=sum(1 << i for i in e),
                                              remote_sem=T.sem["lm%d" % t], srcs=[s], dsts=[s for p in others])],
                           local_sem=T.sem.ls)
        sent[0] += len(e)

    for t in range(3):
        for kind in ("csx" if t == 1 else "cs"):
            arrive["@%s%d" % (kind, t)] = ("n%s%d" % (kind, t), sum(len(engs(p, r)) for p in nbs(r)))
        arrive["@l%d" % t] = ("lm%d" % t, sum(len(topo.engines(T.cores[p], T.cores[r])) for p in others))

    def dma(name, out, in_, sem, deps=""):
        op(name, lambda: queue[where[name]].dma_start(out, in_), deps, sem)

    def fill(name, ap, c, deps=""):
        op(name, lambda: vec.memset(ap, c), deps)

    def iota(name, ap, pat, base, cm):
        op(name, lambda: g.iota(ap, pat, base, cm, allow_small_or_imprecise_dtypes=True))

    def quant(name, buf, a, b, tile, c, deps):
        op(name, lambda: vec.quantize_mx(T[buf][:, a:b], T[buf + "s"][:, a:b], tile[:, 4 * c:4 * (c + b - a)]), deps)

    def mm(name, k, sb, sa, mb, ma, m, deps):
        op(name, lambda: ten.matmul_mx(bank(k, 0, m), T[sb][:, sa:sa + 128], T[sb + "s"][:, sa:sa + 128],
                                       T[mb][:, ma:ma + m], T[mb + "s"][:, ma:ma + m], True, True), deps)

    junk = [0]

    def count(name, t, piece, k, deps, p=128):
        j = junk[0]
        junk[0] += 128
        c = 4 * r + piece
        op(name, lambda: act.activation(T.junk[0:p, j:j + 128], bank(k, 0, 128, p), Act.Sign, bias=T.eps[0:p, 0:1],
                                        accum_out=Lbuf(t, c, c + 1, 0, p)), deps + " zeps zL%d" % t)

    def relu(name, k, b, a, h, c, m, deps):
        out, src = h[:, 4 * c + b:4 * (c + m):4], bank(k, a, a + m)
        if where[name] == "a":
            op(name, lambda: act.activation(out, src, Act.Relu, scale=0.0625), deps)
        else:
            op(name, lambda: vec.tensor_scalar(out, src, 0.0, 0.0625, Op.max, Op.mult), deps)

    def pick(name, out, window, l, deps):
        if where[name] == "a":
            op(name, lambda: act.activation(out, window.indirect(l), Act.Copy), deps)
        else:
            op(name, lambda: vec.tensor_copy(out, window.indirect(l)), deps)

    def ts(name, out, in0, s1, s2, o0, o1, deps):
        op(name, (lambda: vec.tensor_scalar(out, in0, s1, s2, o0, o1)) if o1 is not None else
           (lambda: vec.tensor_scalar(out, in0, s1, None, o0)), deps)

    def aff(name, out, in_, scale, bias, deps):
        if where[name] == "a":
            op(name, lambda: act.activation(out, in_, Act.Identity, bias=bias, scale=scale), deps)
        else:
            op(name, lambda: vec.tensor_scalar(out, in_, scale, bias, Op.mult, Op.add), deps)

    def tt(name, out, a, b, o, deps):
        op(name, lambda: vec.tensor_tensor(out, a, b, o), deps)

    def turn(name, out, in_, deps):
        turns.append(name)
        op(name, lambda: vec.transpose(out, in_), deps)

    words = lambda ap: ap.bitcast(dt.uint32)

    dma("lxa", T.xe[:, 96:256], T.x[:, 864:1024], "dx0")
    dma("lxb", T.xe[:, 256:416], T.x[:, 0:160], "dx2")
    dma("lxr", T.xt[:], T.x[:], "dx1")
    dma("la", T.at[:], T.a[:], "da")
    for b in range(2):
        dma("lw%d" % b, T.wt[:, 1024 * b:1024 * b + 1024], T.w[:, 1024 * b:1024 * b + 1024], "dw%d" % b)

    fill("zxa", T.xe[:, 0:96], 0.0)
    fill("zxb", T.xe[:, 416:512], 0.0)
    fill("znh", T.nh[0:32, :], 80.0)
    fill("zeps", T.eps[:, 0:1], -(2.0 ** -120))
    for t in range(2):
        fill("zL%d" % t, Lbuf(t, 4 * r, 4 * r + 4), 0.0)
    fill("zLa", T.G0[:, 259:260], 0.0)
    fill("zLb", T.G0[:, 2:260:4], 0.0)
    fill("zLc", T.G0[:, 278:392:4], 0.0)
    fill("zG1", T.G1[:, 1:420:4], 0.0)
    fill("zG2", T.G2[:, 2:420:4], 0.0)
    fill("zX", T.m2[:, 0:192], 0.0)
    fill("zXX", T.XX[0:64, :], 0.0)
    if not both:
        fill("zh1", T.h1[:, 1024:1184] if left else T.h1[:, 1184:1344], 0.0)
        fill("zzt", T.zt[:], 0.0)
        fill("zyt", T.yt[:, 384:496], 0.0)
        quant("qZ", "F", 368, 496, T.zt, 0, "zzt")
        dma("szc", T.oc[:, 4 * 384:4 * 496], T.F[:, 384:496].bitcast(dt.uint8), "dout", "qZ")
        dma("szy", T.y[:, 384:496], T.yt[:, 384:496], "dout", "zyt")
    fill("zhh", T.hh2[:, 320:512] if both else T.hh2[:], 0.0)
    fill("zRWb", T.RA[0:32, 64:224], 130.0)
    for t in range(2):
        fill("zkb%d" % t, T.kb[0:32, t:t + 1], 130.0 * HALF[t] - 0.125)
    fill("zHM", T.HM[:], 1.0)
    for k, c in enumerate((0.0, -1.0 / BIG, BIG)):
        fill("zHM%d" % k, T.HM[:, k:186:6], c, "zHM")
    fill("zMK", T.MK1[:], 1.0)
    op("ipi", lambda: g.iota(T.pi[:, 0:1], [[0, 1]], 0, 1))
    iota("iN", T.K[:, 0:60], [[-32, 60]], 512, 0)
    for k, (a, b, c) in enumerate(((0, 5, 208), (5, 10, -32), (10, 13, -112 if right else 96), (13, 20, 384 if left else 80))):
        iota("iM%d" % k, T.K[:, 60 + a:60 + b], [[-32, b - a]], -2 * (c + 16 * a), 0)
    iota("igi", T.gi[:, 0:7], [[-16, 7]], -80, 2)
    fill("zgi", T.gi[0:48, 6:7], 10000.0, "igi")
    fill("zgj", T.gi[0:32, 4:5], 10000.0, "igi")
    iota("iwq", T.wq[:, 0:3], [[1, 3]], 1, 0)
    iota("iB0", T.B0[:, 0:1], [[0, 1]], 0, 256)
    iota("iodd", T.odd[0:32, :], [[2, 80]], -79, 0)
    iota("icp0", T.cp[:, 0:2], [[704, 2]], 80, 0)
    iota("icp1", T.cp[:, 2:4], [[192, 2]], 592, 0)
    op("sel0", lambda: g.affine_select(T.nha[0:32, :], T.nh[0:32, :], [[0, 32]], Op.is_ge, 0.0, -1, 1), "znh")
    op("sel1", lambda: g.affine_select(T.nhb[0:32, :], T.nha[0:32, :], [[0, 32]], Op.is_ge, 0.0, n - 1, -1), "sel0")
    ts("pand", T.pm[:, 0:1], T.pi[:, 0:1], 15, None, Op.bitwise_and, None, "ipi")
    ts("pcopy", T.pf[:, 0:1], T.pm[:, 0:1], -2.0, None, Op.mult, None, "pand")
    aff("KK", T.KK[:], T.K[:], 1.0, T.pf[:, 0:1], "pcopy iN" + rng("iM%d"))
    ts("lo0", T.hi[0:32, 0:1], T.nhb[0:32, 0:1], -1.0, None, Op.mult, None, "sel1")

    quant("qE", "XE", 0, 128, T.xe, 0, "lxa lxb zxa zxb")
    quant("qX", "C0", 0, 256, T.xt, 0, "lxr")
    quant("qa", "qa", 0, 128, T.at, 0, "la")
    ends(0, "XE", "C0", 40, ((64, 256), (24, 296 if r + 2 < n else 256)), "qE", "qE")
    mm("mE", 4, "XE", 0, "qa", 0, 128, "qE qa")
    mm("mM", 5, "C0", 88, "qa", 0, 128, "qX qa")
    mm("mN", 6, "C0", 40, "qa", 0, 128, "qX qa")
    count("c00", 0, 2, 4, "mE")
    count("c01", 0, 0, 5, "mM")
    count("c02", 0, 1, 6, "mN", 48)
    op("sl0", lambda: send_costs(0), "c00 c01 c02")
    ha, hc, hm = (232, 256, 104) if both else (168, 296 if left else 256, 40)
    if both:
        quant("qD", "C0", 336, 464, T.xt, 0, "lxr")
    for b in range(4):
        quant("qw%d" % b, "qw", 128 * b, 128 * b + 128, T.wt, 128 * b, "lw%d" % (b // 2))
        mm("o%d" % b, b, "qw", 128 * b, "C0", 0, 256, "qX qw%d" % b)
        relu("ro%d" % b, b, b, 0, T.h1, 0, 256, "o%d" % b)
        mm("h%d" % b, 4 + b, "qw", 128 * b, "C0", ha, 128, "qX qD qw%d @c0 @s0 " % b + ("c00", "c01", "c02", "")[b])
        relu("rh%d" % b, 4 + b, b, 128 - hm, T.h1, hc, hm, "h%d" % b)
    quant("q1a", "W1", 336, 560, T.h1, 0, rng("ro%d"))
    quant("q1c", "W1", 128, 256, T.h1, 128, rng("ro%d"))
    qb = 232 if both else 208
    quant("q1b", "W1", qb, qb + 128, T.h1, qb, rng("ro%d") + rng("rh%d") + "zh1 q1a q1c")
    q1 = " q1b "
    we = 56 if both else 80 if left else 32
    op("sx1a", lambda: send_ends(1, "x", "W1", "W1", we, ((416 - we, 128 - we), (176, 560))), "q1a q1c")
    op("sc1a", lambda: send_ends(1, "c", "W1", "W1", 120 - we, ((296, 8), (176 + we, 560 + we))), q1)
    op("ss1a", lambda: send_ends(1, "s", "W1", "W1", 120, ((296, 8), (176, 560))), q1)
    mm("k11", 4, "W1", 384, "qa", 0, 128, "qa q1a rh0")
    mm("k10", 5, "W1", 256, "qa", 0, 128, "qa q1a q1b")
    mm("k12", 6, "W1", 176, "qa", 0, 128, "qa q1b")
    for k, b in ((0, 5), (1, 4), (2, 6)):
        count("c1%d" % k, 1, k, b, "k1%d" % k)
    op("sl1", lambda: send_costs(1), "c10 c11 c12")

    BO = lambda t, a, b: T.BBB[:, 32 * t + a:32 * t + b]
    XX = lambda t, m=32, p=5: T.XX[0:p, 32 * t:32 * t + m]
    XB = lambda t: T.XX[32:37, 32 * t:32 * t + 32]
    tb = lambda t: rng("tb%d%%d" % t, 2)
    for t in range(3):
        s, k, G, Zh = str(t), (2, 1, 2)[t], T["G%d" % t], T["Zh%d" % t]
        lm = k + 287 if t else 260
        LM = lambda a, b, c=1, p=0, q=128, lm=lm, G=G: G[p:q, lm + a:lm + b:c]
        have = "@l0 c00 c01 c02 zLa zLb zLc" if t == 0 else "mask" + s
        if t:
            tt("mask" + s, LM(0, 16), T["L" + s][:], T["MK" + s][:], Op.mult,
               "@l%d zG%d " % (t, t) + ("c10 c11 c12 mk10 mk12" if t == 1 else rng("c2%d") + rng("mk2%d")))
        op("ps" + s, lambda t=t, LM=LM, G=G: vec.tensor_tensor_scan(G[0:64, 4:20], LM(0, 16, 1, 0, 64) if t else LM(-1, 15, 1, 0, 64),
                                                                    LM(0, 16, 1, 64, 128), 0.0, Op.add, Op.add), have)
        ts("sh" + s, G[0:64, k + 132:k + 141:4], T.wq[0:64, 0:3], G[0:64, 19:20], -0.25, Op.mult, Op.mult, "iwq ps" + s)
        if t:
            tt("x" + s, G[:, k + 260:k + 269:4], LM(1 + t, 10 + t, 4), LM(4, 13, 4), Op.add, "mask" + s)
            turn("tz%d4" % t, Zh[0:32, 192:224], LM(1, 126, 4, 0, 32), "mask" + s)
        turn("tl%d0" % t, Zh[0:32, 0:96], G[0:32, k:k + 381:4], "sh%d %s" % (t, "x" + s if t else ""))
        turn("tl%d1" % t, T.RA[0:32, 0:64], G[32:64, k:k + 253:4], "sh%d %s" % (t, "~scan%d" % (t - 1) if t else ""))
        for j in range(4):
            p, q = 32 * j, 32 * j + 32
            if j < 2:
                turn("tb%d%d" % (t, j), T.BBB[2 * p:2 * q, 32 * t:32 * t + 32], XX(3 if t == 1 else t, 32, 64),
                     "xd xdb" if t == 1 else "clamp%d clamp%db" % (t, t))
            if j:
                a = k + 256 + (4 if j > 1 and not t else 0)
                turn("tz%d%d" % (t, j), Zh[0:32, 64 + p:64 + q], G[p:q, a:a + 125:4], "x" + s if t else have)
        h, a, w = 63 + HALF[t] + MOVE[t], 63 + HALF[t] - MOVE[t], 2 * MOVE[t] + (80 if t == 1 else 0)
        op("scan" + s, lambda Zh=Zh, h=h: vec.tensor_tensor_scan(T.Ih[0:5, 0:h], Zh[0:5, 0:h], T.RA[0:5, 0:h], 0.0, Op.add, Op.add),
           "zRWb" + rng("tl%d%%d" % t, 2) + rng("tz%d%%d" % t, 5 if t else 4) + ("sign%d" % (t - 1) if t else ""))
        j = (0, 80, 320)[t]
        op("sign" + s, lambda t=t, a=a, w=w, j=j: act.activation(T.rjunk[0:5, j:j + w], T.Ih[0:5, a:a + w], Act.Sign,
                                                                 bias=T.kb[0:5, t:t + 1], scale=-1.0, accum_out=T.row[0:5, t:t + 1]),
           "scan%d %s" % (t, ("zkb0", "zkb1 ex1", "kb2")[t]))
    ts("ex1", T.Ih[0:5, 223:303], T.odd[0:5, :], XX(0, 1), 65536.0, Op.add, Op.mult, "iodd clamp0")
    for b, X in (("", XX), ("b", XB)):
        ts("clamp0" + b, X(0), T.nhb[0:5, :], T.row[0:5, 0:1], T.hi[0:5, 0:1], Op.min, Op.max, "zXX sign0 lo0")
        ts("xd" + b, X(3), T.nhb[0:5, :], T.row[0:5, 1:2], T.hi[0:5, 0:1], Op.min, Op.max, "zXX sign1 lo0")
        ts("clamp2" + b, X(2), T.lo[0:5, 0:32], T.row[0:5, 2:3], T.hi[0:5, 2:3], Op.max, Op.min, "sign2 lo2 hi2")
    aff("lo2", T.lo[0:5, 0:32], XX(3), 1.0, T.hi[0:5, 0:1], "xd")
    aff("hi2", T.hi[0:5, 2:3], XX(3, 1), 1.0, T.nhb[0:5, 0:1], "xd")
    aff("kb2", T.kb[0:5, 2:3], XX(0, 1), -65.0, 130.0 * HALF[2] - 0.125, "clamp0")
    for name, MK, p, t, gc in (("mk10", T.MK1, 0, 0, 5), ("mk12", T.MK1, 2, 0, 5), ("mk20", T.MK2, 0, 1, 5), ("mk21", T.MK2, 1, 0, 4),
                               ("mk22", T.MK2, 2, 0, 6), ("mk23", T.MK2, 3, 1, 5)):
        if p < 2:
            ts(name, MK[:, p:16:4], BO(t, 0, 4), T.gi[:, gc:gc + 1], None, Op.is_le, None, "igi zgj zMK" + tb(t))
        else:
            ts(name, MK[:, p:16:4], BO(t, 1, 5), T.gi[:, gc:gc + 1], None, Op.is_gt, None, "igi zgi zMK" + tb(t))

    for k, (a, b, j) in enumerate(((0, 5, 0), (5, 13, 1), (13, 16, 0))):
        ts("lM%d" % k, T.la[:, a:b], T.KK[:, 60 + a:60 + b], BO(0, r + j, r + j + 1), -0.5, Op.subtract, Op.mult, "KK" + tb(0))
    pick("pM0", words(T.M1[:, 0:160]), words(T.W1[:, 128:560]), T.la[:, 0:10], q1 + "lM0 lM1")
    pick("pMs0", T.M1s[:, 0:160], T.W1s[:, 128:560], T.la[:, 0:10], q1 + "lM0 lM1")
    pick("pM1", words(T.M1[:, 160:256]), words(T.W1[:, 0:680]), T.la[:, 10:16], q1 + "@x1 @c1 lM1 lM2")
    pick("pMs1", T.M1s[:, 160:256], T.W1s[:, 0:680], T.la[:, 10:16], q1 + "@s1 lM1 lM2")
    for b in range(4):
        mm("d%d" % b, b, "qw", 128 * b, "W1", 376, 176, "q1a ro%d" % b)
        relu("rd%d" % b, b, b, 0, T.m2, 304, 176, "d%d" % b)
        mm("L%d" % b, 4 + b, "qw", 128 * b, "M1", 0, 160, "pM0 pMs0 " + ("c11", "c10", "c12", "rh3")[b])
        relu("ro%da" % (4 + b), 4 + b, b, 0, T.m2, 224, 80, "L%d" % b)
        relu("ro%db" % (4 + b), 4 + b, b, 80, T.m2, 48, 80, "L%d ~ro%da" % (b, 4 + b))
        mm("R%d" % b, b, "qw", 128 * b, "M1", 128, 128, "pM0 pMs0 pM1 pMs1 rd%d %s" % (b, "" if b else "c22"))
        relu("rR%d" % b, b, b, 32, T.m2, 128, 96, "R%d" % b)
    roa, rob = " ro4a ro5a ro6a ro7a ", " ro4b ro5b ro6b ro7b "
    quant("q2m", "C2", 312, 488, T.m2, 304, rng("rd%d"))
    quant("q2L", "C2", 232, 360, T.m2, 224, "q2m" + roa)
    quant("q2A", "C2", 8, 136, T.m2, 0, "zX" + rob)
    quant("q2R", "C2", 120, 248, T.m2, 112, rng("rR%d") + "q2L q2A")
    q2 = " q2R "
    mm("k21", 7, "C2", 280, "qa", 0, 128, "q2m q2L ro7a ro7b")
    mm("k22", 0, "C2", 360, "qa", 0, 128, "q2m")
    mm("k20", 4, "C2", 152, "qa", 0, 128, "q2R")
    mm("k23", 5, "C2", 56, "qa", 0, 128, "q2R")
    for k in range(4):
        count("c2%d" % k, 2, k, (4, 7, 0, 5)[k], "k2%d" % k)
    op("sl2", lambda: send_costs(2), rng("c2%d"))
    for k, c in ((0, 30), (1, 22)):
        ts("lH%d" % k, T.lb[:, 3 * k:3 * k + 3], T.KK[:, c:c + 3], BO(1, r + k, r + k + 1), -0.5, Op.subtract, Op.mult, "KK" + tb(1))
    pick("pH", words(T.H2[:, 0:96]), words(T.C2[:, 0:312]), T.lb[:, 0:6], q2 + "lH0 lH1")
    pick("pHs", T.H2s[:, 0:96], T.C2s[:, 0:312], T.lb[:, 0:6], q2 + "lH0 lH1")
    ends(2, "H2", "H2", 40, ((8, 136 if r > 1 else 96), (48, 96)), "pH", "pHs")

    na, nc, nm = (48, 0, 80) if both else (8, 0 if left else 40, 40)
    for b in range(4):
        mm("f%d" % b, b, "qw", 128 * b, "C2", 56, 432, q2)
        relu("rf%d" % b, b, b, 0, T.m3, 0, 432, "f%d" % b)
        mm("n%d" % b, 4 + b, "qw", 128 * b, "H2", na, 128, "pH pHs @c2 @s2" + rng("c2%d"))
        relu("rn%d" % b, 4 + b, b, 128 - nm, T.hh2, nc, nm, "zhh n%d" % b)
    quant("q3w", "C3", 0, 432, T.m3, 0, rng("rf%d"))
    quant("q3h", "C3", 432, 560, T.hh2, 0, "zhh" + rng("rn%d"))
    tt("c23c", T.cc[:, 0:2], BO(0, r, r + 2), T.cp[:, 0:2], Op.add, "icp0" + tb(0))
    tt("c14c", T.cc[:, 2:4], T.cp[:, 2:4], BO(1, r, r + 2), Op.subtract, "icp1" + tb(1))
    ts("th35", T.th[:, 0:36], T.KK[:, 0:36], BO(0, r + 1, r + 2), BO(0, r, r + 1), Op.add, Op.subtract, "KK" + tb(0))
    aff("th1", T.th[:, 36:67], T.KK[:, 16:47], 1.0, BO(1, r, r + 1), "KK" + tb(1))
    aff("th4", T.th[:, 68:99], T.th[:, 0:31], 1.0, BO(1, r + 1, r + 2), "th35" + tb(1))
    e, TM = BO(2, r, r + 1), lambda k: T.TM[:, k:186:6]
    ts("t3", TM(0), T.th[:, 5:36], e, T.cc[:, 1:2], Op.is_le, Op.mult, "th35 c23c" + tb(2))
    ts("tend", TM(1), T.th[:, 0:31], BO(2, r + 1, r + 2), e, Op.add, Op.is_le, "th35" + tb(2))
    aff("tbase", TM(2), T.KK[:, 27:58], -1.0, e, "KK" + tb(2))
    ts("t1", TM(3), T.th[:, 36:67], e, T.cc[:, 2:3], Op.is_gt, Op.mult, "th1 c14c" + tb(2))
    ts("t2", TM(4), T.KK[:, 11:42], e, T.cc[:, 0:1], Op.is_le, Op.mult, "KK c23c" + tb(2))
    ts("t4", TM(5), T.th[:, 68:99], e, T.cc[:, 3:4], Op.is_le, Op.mult, "th4 c14c" + tb(2))
    op("sum", lambda: vec.tensor_tensor_scan(T.SM[:, 0:186], T.HM[:, 0:186], T.TM[:, 0:186], 0.0, Op.mult, Op.add),
       "t1 t2 t3 t4 tend tbase zHM" + rng("zHM%d", 3))
    ts("lF", T.lf[:, 0:31], T.SM[:, 5:186:6], 0.5, 520.0, Op.mult, Op.min, "sum")
    aff("bh0", T.Bh[0:5, 0:1], XX(0, 1), 0.5, T.B0[0:5, 0:1], "iB0 clamp0")
    aff("bh1", T.Bh[0:5, 4:5], XX(3, 1), 0.5, T.Bh[0:5, 0:1], "bh0 xd")
    aff("bh2", T.Bh[0:5, 8:9], XX(2, 1), 0.5, T.Bh[0:5, 0:1], "bh0 clamp2")

    for t in range(3):
        dma("sbd%d" % t, T.bd[t, :], T.Bh[0:5, 4 * t:4 * t + 1], "dout", "bh%d" % t)
    cuts = CUTS[int(both)]
    for k, (a, b) in enumerate(cuts):
        l = T.lf[:, a // 16:b // 16]
        pick("pF%d" % k, words(T.F[:, a:b]), words(T.C3[:, 0:560]), l, "lF q3w q3h qZ")
        pick("pFs%d" % k, T.Fs[:, a:b], T.C3s[:, 0:560], l, "lF q3w q3h qZ")
        mm("y%d" % k, k, "qa", 0, "F", a, b - a, "pF%d pFs%d" % (k, k))
        if where["yc%d" % k] == "a":
            op("yc%d" % k, lambda k=k, a=a, b=b: act.activation(T.yt[:, a:b], bank(k, 0, b - a), Act.Copy), "y%d" % k)
        else:
            op("yc%d" % k, lambda k=k, a=a, b=b: vec.tensor_copy(T.yt[:, a:b], bank(k, 0, b - a)), "y%d" % k)
        dma("soc%d" % k, T.oc[:, 4 * a:4 * b], T.F[:, a:b].bitcast(dt.uint8), "dout", "pF%d" % k)
        dma("sy%d" % k, T.y[:, a:b], T.yt[:, a:b], "dout", "yc%d" % k)
    for i in range(4):
        dma("sos%d" % i, T.osc[4 * i:4 * i + 4, :], T.Fs[32 * i:32 * i + 4, :], "dout", rng("pFs%d", len(cuts)) + "qZ")

    OPS[r] = ops
    tok, cnt = dict(arrive), {}
    for q in order:
        for name in order[q]:
            if name in ops and (name[:2] not in ("sc", "ss", "sl", "sx") or name[:4] == "scan"):
                sem = ops[name][2] or "s" + q
                cnt[sem] = cnt.get(sem, 0) + (16 if ops[name][2] else 1)
                tok[name] = (sem, cnt[sem])
    for q in order:
        seen, drain = {}, []
        for name in order[q]:
            if name not in ops:
                continue
            fn, deps, sem = ops[name]
            if name not in turns:
                deps, drain = deps + drain, []
            need = {}
            for d in deps:
                if d[0] == "~":
                    d = d[1:]
                    if where.get(d) == q:
                        continue
                if d in tok:
                    s, c = tok[d]
                    need[s] = max(need.get(s, 0), c)
            for s, c in need.items():
                if seen.get(s, 0) < c:
                    queue[q].wait_ge(T.sem[s], c)
                    seen[s] = c
            ins = fn()
            if name[:2] == "ps":
                drain = [name]
            if name in tok:
                ins.then_inc(T.sem[tok[name][0]], 16 if sem else 1)
    cnt["ls"] = sent[0]
    for s, c in cnt.items():
        g.wait_ge(T.sem[s], c)
